import numpy as np
import ml_dtypes


def mxq(x, axis, fmt="e4m3"):
    dtype, down = {"e4m3": (ml_dtypes.float8_e4m3fn, 7), "e5m2": (ml_dtypes.float8_e5m2, 14)}[fmt]
    v = np.moveaxis(np.asarray(x, np.float32).astype(ml_dtypes.bfloat16).astype(np.float64), axis, -1)
    blocks = v.reshape(v.shape[:-1] + (-1, 32))
    amax = np.abs(blocks).max(-1, keepdims=True)
    byte = np.maximum(np.where(amax > 0, np.frexp(amax)[1] - 1 + 127, 0) - down, 1)
    scale = np.exp2(byte - 127.0)
    codes = (blocks / scale).astype(np.float32).astype(dtype).astype(np.float64)
    return np.moveaxis((codes * scale).reshape(v.shape), -1, axis)


WIDE = False


def mx_kscale(k):
    if not WIDE:
        return np.ones(k)
    levels = np.array([10, -10, 5, -5, 0])
    if k % 512:
        return np.exp2(np.random.permutation(np.resize(levels, k // 32))).repeat(32)
    a = np.empty((k // 512, 16))
    for p in range(k // 512):
        a[p, :8] = np.random.permutation(np.resize(levels, 8))
        for g in range(8):
            far = levels[np.abs(levels - a[p, g]) >= 10]
            a[p, g + 8] = far[np.random.randint(len(far))]
    return np.exp2(a.ravel()).repeat(32)


def f64(x):
    return np.asarray(x).astype(np.float64)


def striped(idx):
    return np.tile(idx.reshape(-1, 16).T, (8, 1)).astype(np.uint16)


def unstriped(offs):
    return offs[:16].T.reshape(-1).astype(np.int64)


E2M1 = np.array([0.0, 0.5, 1.0, 1.5, 2.0, 3.0, 4.0, 6.0, -0.0, -0.5, -1.0, -1.5, -2.0, -3.0, -4.0, -6.0])


def pack_weight(w, fmt):
    k, n = w.shape
    w = f64(np.asarray(w, np.float32).astype(ml_dtypes.bfloat16)).reshape(k // 32, 32, n)
    amax = np.abs(w).max(1)
    if fmt == "e4m3":
        byte = np.frexp(amax)[1] - 1 + 127 - 7
    else:
        mant, ex = np.frexp(amax / 6.0)
        byte = np.where(mant > 0.5, ex, ex - 1) + 127
    byte = np.clip(np.where(amax > 0, byte, 1), 1, 254)
    scaled = (w * np.exp2(127.0 - byte)[:, None, :]).reshape(k, n).astype(np.float32)
    by_word = np.ascontiguousarray(scaled.reshape(k // 512, 128, 4, n).transpose(0, 1, 3, 2))
    if fmt == "e4m3":
        words = by_word.astype(ml_dtypes.float8_e4m3fn).view(np.uint8)
    else:
        c = by_word.astype(ml_dtypes.float4_e2m1fn).view(np.uint8) & 0xF
        words = (c[..., 0::2] | (c[..., 1::2] << 4)).reshape(k // 512, 128, 2 * n)
    return np.ascontiguousarray(words), np.ascontiguousarray(byte.astype(np.uint8).reshape(k // 512, 16, n))


def unpack_weight(words, scales, fmt):
    g, _, n = scales.shape
    words = np.ascontiguousarray(words).reshape(g, 128, n, -1)
    if fmt == "e4m3":
        vals = words.view(ml_dtypes.float8_e4m3fn).astype(np.float64)
    else:
        nib = np.empty((g, 128, n, 4), np.uint8)
        nib[..., 0::2] = words & 0xF
        nib[..., 1::2] = words >> 4
        vals = E2M1[nib]
    vals = vals * np.repeat(np.exp2(scales.astype(np.float64) - 127.0), 8, axis=1)[..., None]
    return vals.transpose(0, 1, 3, 2).reshape(g * 512, n)


def gelu(v):
    return 0.5 * v * (1.0 + np.tanh(np.sqrt(2.0 / np.pi) * (v + 0.044715 * v**3)))


def bf(x):
    return np.asarray(x, np.float32).astype(ml_dtypes.bfloat16)

def planes(Y):
    n, m = Y.shape
    b = f64(bf(Y)).reshape(n // 32, 32, m)
    amax = np.abs(b).max(1)
    byte = np.clip(np.where(amax > 0, np.frexp(amax)[1] - 1 + 127 - 7, 1), 1, 254)
    codes = (b * np.exp2(127.0 - byte)[:, None, :]).reshape(n, m).astype(np.float32).astype(ml_dtypes.float8_e4m3fn).view(np.uint8)
    words = codes.reshape(n // 512, 128, 4, m).transpose(0, 1, 3, 2)
    return np.ascontiguousarray(words), np.ascontiguousarray(byte.astype(np.uint8).reshape(n // 512, 16, m))


K, T, S, T2, S2, N = 1024, 2048, 1024, 4096, 1024, 512

def setup_inputs():
    n = np.random.standard_normal
    s = mx_kscale(K)[:, None]
    u = mx_kscale(S)[:, None]
    tab_words, tab_scales = pack_weight(n((K, T)) * s / np.sqrt(K), "e4m3")
    tab2_words, tab2_scales = pack_weight(n((K, T2)) / s, "e4m3")
    size = np.exp(0.8 * n(N))[None, :]
    w1 = 1.2 * n((S, N)) / np.sqrt(S) * size / u
    w4 = 0.8 * n((S, N)) / np.sqrt(S) * size / u
    w4_words, w4_scales = pack_weight(w4, "e2m1")
    return {
        "tab_words": tab_words, "tab_scales": tab_scales,
        "tab2_words": tab2_words, "tab2_scales": tab2_scales,
        "offs": striped(np.random.permutation(T)[:S]),
        "offs2": striped(np.random.permutation(T2)[:S2]),
        "lo": (-np.exp(0.2 * n(S))).astype(np.float32),
        "hi": (1.1 * np.exp(0.2 * n(S))).astype(np.float32),
        "gain": (np.exp(0.3 * n(S)) * u[:, 0]).astype(np.float32),
        "w1": w1.astype(np.float32),
        "w4_words": w4_words, "w4_scales": w4_scales,
    }

def reference(tab_words, tab_scales, tab2_words, tab2_scales, offs, offs2, lo, hi, gain, w1, w4_words, w4_scales):
    v = unpack_weight(tab_words, tab_scales, "e4m3")[:, unstriped(offs)]
    v2 = unpack_weight(tab2_words, tab2_scales, "e4m3")[:, unstriped(offs2)]
    a = v.T @ v2
    c = np.minimum(np.maximum(a, f64(lo)[:, None]), f64(hi)[:, None])
    h = c * f64(gain)[:, None]
    h2 = h * c
    w4 = unpack_weight(w4_words, w4_scales, "e2m1")
    y = mxq(f64(w1), 0, "e4m3").T @ mxq(h, 0, "e4m3") + w4.T @ mxq(h2, 0, "e4m3")
    words, scales = planes(y)
    return y, words, scales

@@ -1,0 +1,259 @@
+from contextlib import ExitStack
+
+import concourse.mybir as mybir
+
+K, T, S, T2, S2, N = 1024, 2048, 1024, 4096, 1024, 512
+FLOPS = 2 * K * S * S2 + 2 * 2 * S * N * S2
+
+F32 = mybir.dt.float32
+BF16 = mybir.dt.bfloat16
+I32 = mybir.dt.int32
+U32 = mybir.dt.uint32
+U16 = mybir.dt.uint16
+U8 = mybir.dt.uint8
+FP8X4 = mybir.dt.float8_e4m3fn_x4
+FP4X4 = mybir.dt.float4_e2m1fn_x4
+ALU = mybir.AluOpType
+ACT = mybir.ActivationFunctionType
+
+P = 128
+PACK = 4
+PASSES = 2
+HALF = 512
+CHUNKS = (512,256,128,128)
+YB = 128
+VY = 2
+GT = 0
+
+
+def tile_list_satellite_radiance_calibration_kernel(
+    tc, tab_words, tab_scales, tab2_words, tab2_scales, offs, offs2, lo, hi, gain, w1, w4_words, w4_scales,
+    out_0, out_1, out_2,
+):
+    nc = tc.nc
+    with ExitStack() as ctx:
+        held = ctx.enter_context(tc.tile_pool(name="held", bufs=1))
+        work = ctx.enter_context(tc.tile_pool(name="work", bufs=2))
+        psum_a = ctx.enter_context(tc.psum_pool(name="psum_a", bufs=6))
+        psum_y = ctx.enter_context(tc.psum_pool(name="psum_y", bufs=2))
+
+        list1 = held.tile([P, S // 16], U16, name="list1")
+        list2 = held.tile([P, S2 // 16], U16, name="list2")
+        tab_s = held.tile([P, T], U8, name="tab_s", align_bytes=64)
+        tab2_s = held.tile([P, T2], U8, name="tab2_s", align_bytes=64)
+        w4_s = held.tile([P, PASSES, N], U8, name="w4_s", align_bytes=64)
+        tab_w = [held.tile([P, T], U32, name=f"tab_w{a}", align_bytes=64) for a in range(PASSES)]
+        tab2_w = [held.tile([P, T2], U32, name=f"tab2_w{a}", align_bytes=64) for a in range(PASSES)]
+        w1_raw = [held.tile([P, PACK, N], F32, name=f"w1_raw{g}", align_bytes=64) for g in range(PASSES)]
+        w4_w = held.tile([P, PASSES, 2 * N], U8, name="w4_w", align_bytes=64)
+        lo_t = held.tile([P, PASSES, PACK], F32, name="lo_t")
+        hi_t = held.tile([P, PASSES, PACK], F32, name="hi_t")
+        gain_t = held.tile([P, PASSES, PACK], F32, name="gain_t")
+
+        warm = held.tile([P, 2], F32, name="warm")
+        nc.vector.memset(tab_s[:].bitcast(I32), 0)
+        nc.vector.memset(warm[:, 0:1], 0.0)
+        nc.vector.memset(tab2_s[:].bitcast(I32), 0)
+        nc.vector.memset(w4_s[:].rearrange("p a n -> p (a n)").bitcast(I32), 0)
+
+        def load_words(dst, words, a):
+            nc.sync.dma_start(dst[:].bitcast(I32), words[a].rearrange("p t i -> p (t i)").bitcast(I32))
+
+        def load_scales(dst, scales):
+            for q in range(4):
+                nc.scalar.dma_start(
+                    dst[32 * q : 32 * q + 4 * PASSES, :].bitcast(I32), scales[:, 4 * q : 4 * q + 4, :].bitcast(I32)
+                )
+
+        nc.sync.dma_start(list1[:], offs)
+        load_words(tab_w[0], tab_words, 0)
+        load_scales(tab_s, tab_scales)
+        nc.sync.dma_start(list2[:], offs2)
+        load_words(tab_w[1], tab_words, 1)
+        load_scales(tab2_s, tab2_scales)
+        load_words(tab2_w[0], tab2_words, 0)
+        nc.sync.dma_start(w4_w[:].bitcast(I32), w4_words.rearrange("a p b -> p a b").bitcast(I32))
+        load_words(tab2_w[1], tab2_words, 1)
+        for dst, src in ((lo_t, lo), (hi_t, hi), (gain_t, gain)):
+            nc.scalar.dma_start(dst[:], src.rearrange("(g p t) -> p g t", g=PASSES, t=PACK))
+        nc.scalar.activation(warm[:, 1:2], warm[:, 0:1], ACT.Copy)
+        for q in range(4):
+            nc.scalar.dma_start(
+                w4_s[32 * q : 32 * q + 4, :, :].bitcast(I32),
+                w4_scales[:, 4 * q : 4 * q + 4, :].rearrange("a r n -> r a n").bitcast(I32),
+            )
+        for g in range(PASSES):
+            nc.sync.dma_start(w1_raw[g][:], w1[g * HALF : (g + 1) * HALF, :].rearrange("(p j) n -> p j n", j=PACK))
+
+        v_sg = held.tile([P, S], U8, name="v_sg", align_bytes=64)
+        v_s = held.tile([P, S], U8, name="v_s", align_bytes=64)
+        v_wg = [held.tile([P, S], U32, name=f"v_wg{a}", align_bytes=64) for a in range(PASSES)]
+        v_w = [held.tile([P, S], U32, name=f"v_w{a}", align_bytes=64) for a in range(PASSES)]
+        v2_s = [held.tile([P, HALF], U8, name=f"v2_s{h}", align_bytes=64) for h in range(2)]
+        v2_w = [[held.tile([P, HALF], U32, name=f"v2_w{a}{h}", align_bytes=64) for h in range(2)] for a in range(PASSES)]
+
+        def deal(dst, src, run):
+            nc.vector.tensor_copy(
+                dst.rearrange("p (g t b i) -> p g b t i", g=PASSES, t=PACK, i=run),
+                src.rearrange("p (g b i t) -> p g b t i", g=PASSES, t=PACK, i=run),
+            )
+
+        def half_list(h):
+            return list2[:, h * (HALF // 16) : (h + 1) * (HALF // 16)]
+
+        nc.vector.tensor_copy(v_sg[:], tab_s[:].indirect(list1[:]))
+        nc.vector.tensor_copy(v_wg[0][:], tab_w[0][:].indirect(list1[:]))
+        deal(v_s[:], v_sg[:], 16)
+        nc.vector.tensor_copy(v_wg[1][:], tab_w[1][:].indirect(list1[:]))
+        deal(v_w[0][:], v_wg[0][:], 4)
+        nc.vector.tensor_copy(v2_s[0][:], tab2_s[:].indirect(half_list(0)))
+        deal(v_w[1][:], v_wg[1][:], 4)
+        nc.vector.tensor_copy(v2_w[0][0][:], tab2_w[0][:].indirect(half_list(0)))
+        nc.vector.tensor_copy(v2_s[1][:], tab2_s[:].indirect(half_list(1)))
+        nc.vector.tensor_copy(v2_w[0][1][:], tab2_w[0][:].indirect(half_list(1)))
+
+        w4_sd = held.tile([P, PASSES * N], U8, name="w4_sd", align_bytes=64)
+        w4_wd = held.tile([P, PASSES * 2 * N], U8, name="w4_wd", align_bytes=64)
+        w1_b = [held.tile([P, N * PACK], BF16, name=f"w1_b{g}", align_bytes=64) for g in range(PASSES)]
+        w1_q = [held.tile([P, N], U32, name=f"w1_q{g}", align_bytes=64) for g in range(PASSES)]
+        w1_s = [held.tile([P, N], U8, name=f"w1_s{g}", align_bytes=64) for g in range(PASSES)]
+        y_s = held.tile([P, S2], U8, name="y_s", align_bytes=64)
+
+        deal(w4_sd[:], w4_s[:].rearrange("p a n -> p (a n)"), 16)
+        deal(w4_wd[:].bitcast(U16), w4_w[:].rearrange("p a b -> p (a b)").bitcast(U16), 8)
+        nc.vector.tensor_copy(v2_w[1][0][:], tab2_w[1][:].indirect(half_list(0)))
+
+        def late_head():
+            nc.vector.tensor_copy(v2_w[1][1][:], tab2_w[1][:].indirect(half_list(1)))
+
+        def round_w1(g):
+            nc.scalar.copy(
+                w1_b[g][:].rearrange("p (t m j) -> p m t j", t=PACK, j=PACK),
+                w1_raw[g][:].rearrange("p j (m t) -> p m t j", t=PACK),
+            )
+
+        def quant_w1(g):
+            nc.vector.quantize_mx(w1_q[g][:].bitcast(FP8X4), w1_s[g][:], w1_b[g][:])
+
+        starts = [sum(CHUNKS[:c]) for c in range(len(CHUNKS))]
+        units = [(c, g) for c in range(len(CHUNKS)) for g in range(PASSES)]
+        clamped = {}
+        scaled = {}
+        woven = {}
+        quantised = {}
+
+        def first_product(c, g):
+            j0, w = starts[c], CHUNKS[c]
+            h, o = divmod(j0, HALF)
+            c32 = work.tile([P, PACK, w], F32, name="c32", align_bytes=64, bufs=3)
+            h32 = work.tile([P, PACK, w], F32, name="h32", align_bytes=64, bufs=3)
+            for t in range(PACK):
+                acc = psum_a.tile([P, w], F32, name="acc")
+                cols = slice(g * HALF + t * P, g * HALF + (t + 1) * P)
+                for a in range(PASSES):
+                    nc.tensor.matmul_mx(
+                        acc[:],
+                        lhsT=v_w[a][:, cols].bitcast(FP8X4),
+                        lhsT_scale=v_s[4 * a : P, cols],
+                        rhs=v2_w[a][h][:, o : o + w].bitcast(FP8X4),
+                        rhs_scale=v2_s[h][4 * a : P, o : o + w],
+                        start=(a == 0),
+                        stop=(a == PASSES - 1),
+                    )
+                nc.vector.tensor_scalar(
+                    c32[:, t, :], acc[:], lo_t[:, g, t : t + 1], hi_t[:, g, t : t + 1], ALU.max, ALU.min
+                )
+                if t < GT:
+                    nc.gpsimd.tensor_scalar(h32[:, t, :], c32[:, t, :], gain_t[:, g, t : t + 1], 1.0, ALU.mult, ALU.mult)
+                else:
+                    nc.scalar.activation(h32[:, t, :], c32[:, t, :], ACT.Copy, scale=gain_t[:, g, t : t + 1])
+            clamped[c, g] = c32
+            scaled[c, g] = h32
+
+        def weave(c, g):
+            w = CHUNKS[c]
+            hb = work.tile([P, w * PACK], BF16, name="hb", align_bytes=64)
+            h2b = work.tile([P, w * PACK], BF16, name="h2b", align_bytes=64)
+            c_view = clamped[c, g][:].rearrange("p t (b i) -> p b t i", i=4)
+            h_view = scaled[c, g][:].rearrange("p t (b i) -> p b t i", i=4)
+            nc.scalar.copy(hb[:].rearrange("p (b i t) -> p b t i", i=4, t=PACK), h_view)
+            nc.vector.tensor_tensor(h2b[:].rearrange("p (b i t) -> p b t i", i=4, t=PACK), h_view, c_view, ALU.mult)
+            woven[c, g] = (hb, h2b)
+
+        def quantise(c, g):
+            w = CHUNKS[c]
+            made = []
+            for name, src in zip(("h", "h2"), woven[c, g]):
+                codes = work.tile([P, w], U32, name=name + "_q", align_bytes=64, bufs=4)
+                scales = work.tile([P, w], U8, name=name + "_s", align_bytes=64, bufs=4)
+                nc.vector.quantize_mx(codes[:].bitcast(FP8X4), scales[:], src[:])
+                made.append((codes, scales))
+            quantised[c, g] = made
+
+        def second_product(c):
+            j0, w = starts[c], CHUNKS[c]
+            y32 = work.tile([P, PACK, w], F32, name="y32", align_bytes=64)
+            yb = work.tile([P, w * PACK], BF16, name="yb", align_bytes=64)
+            y_q = work.tile([P, w], U32, name="y_q", align_bytes=64)
+            for b in range(w // YB):
+                js = slice(b * YB, (b + 1) * YB)
+                acc = psum_y.tile([P, PACK, YB], F32, name="acc_y")
+                for t in range(PACK):
+                    for g in range(PASSES):
+                        codes, scales = quantised[c, g][0]
+                        nc.tensor.matmul_mx(
+                            acc[:, t, :],
+                            lhsT=w1_q[g][:, t * P : (t + 1) * P].bitcast(FP8X4),
+                            lhsT_scale=w1_s[g][:, t * P : (t + 1) * P],
+                            rhs=codes[:, js].bitcast(FP8X4),
+                            rhs_scale=scales[:, js],
+                            start=(g == 0),
+                            stop=False,
+                        )
+                    for g in range(PASSES):
+                        codes, scales = quantised[c, g][1]
+                        n0 = g * N + t * P
+                        nc.tensor.matmul_mx(
+                            acc[:, t, :],
+                            lhsT=w4_wd[:, 2 * n0 : 2 * (n0 + P)].bitcast(FP4X4),
+                            lhsT_scale=w4_sd[:, n0 : n0 + P],
+                            rhs=codes[:, js].bitcast(FP8X4),
+                            rhs_scale=scales[:, js],
+                            start=False,
+                            stop=(g == PASSES - 1),
+                        )
+                if c >= VY:
+                    nc.scalar.copy(
+                        yb[:, b * YB * PACK : (b + 1) * YB * PACK].rearrange("p (j t) -> p j t", t=PACK),
+                        acc[:].rearrange("p t j -> p j t"),
+                    )
+                nc.scalar.copy(y32[:, :, js], acc[:])
+            if c < VY:
+                nc.vector.tensor_copy(
+                    yb[:].rearrange("p (b i t) -> p b t i", i=4, t=PACK), y32[:].rearrange("p t (b i) -> p b t i", i=4)
+                )
+            nc.sync.dma_start(out_0.rearrange("(p t) j -> p t j", t=PACK)[:, :, j0 : j0 + w], y32[:])
+            nc.vector.quantize_mx(y_q[:].bitcast(FP8X4), y_s[:, j0 : j0 + w], yb[:])
+            nc.sync.dma_start(
+                out_1[0].rearrange("p m t -> p (m t)").bitcast(I32)[:, j0 : j0 + w], y_q[:].bitcast(I32)
+            )
+
+        for step in range(len(units) + 3):
+            if step < len(units):
+                first_product(*units[step])
+            if step == 0:
+                late_head()
+            if step < PASSES:
+                round_w1(step)
+            if 0 <= step - 1 < len(units):
+                weave(*units[step - 1])
+            if 0 <= step - 1 < PASSES:
+                quant_w1(step - 1)
+            if 0 <= step - 2 < len(units):
+                quantise(*units[step - 2])
+            if 0 <= step - 3 < len(units) and units[step - 3][1] == PASSES - 1:
+                second_product(units[step - 3][0])
+
+        for q in range(4):
+            queue = nc.sync if q % 2 == 0 else nc.scalar
+            queue.dma_start(out_2[0, 4 * q : 4 * q + 4, :].bitcast(I32), y_s[32 * q : 32 * q + 4, :].bitcast(I32))

@@ -59,18 +59,19 @@ def tile_list_satellite_radiance_calibration_kernel(
         def load_words(dst, words, a):
             nc.sync.dma_start(dst[:].bitcast(I32), words[a].rearrange("p t i -> p (t i)").bitcast(I32))
 
-        def load_scales(dst, scales):
+        def load_scales(queue, dst, row, scales):
             for q in range(4):
-                nc.scalar.dma_start(
-                    dst[32 * q : 32 * q + 4 * PASSES, :].bitcast(I32), scales[:, 4 * q : 4 * q + 4, :].bitcast(I32)
+                queue.dma_start(
+                    dst[32 * q + row : 32 * q + row + 4 * PASSES, :].bitcast(I32),
+                    scales[:, 4 * q : 4 * q + 4, :].bitcast(I32),
                 )
 
         nc.sync.dma_start(list1[:], offs)
         load_words(tab_w[0], tab_words, 0)
-        load_scales(tab_s, tab_scales)
+        load_scales(nc.scalar, tab_s, 0, tab_scales)
         nc.sync.dma_start(list2[:], offs2)
         load_words(tab_w[1], tab_words, 1)
-        load_scales(tab2_s, tab2_scales)
+        load_scales(nc.gpsimd, tab2_s, 8, tab2_scales)
         load_words(tab2_w[0], tab2_words, 0)
         nc.sync.dma_start(w4_w[:].bitcast(I32), w4_words.rearrange("a p b -> p a b").bitcast(I32))
         load_words(tab2_w[1], tab2_words, 1)
@@ -156,7 +157,7 @@ def tile_list_satellite_radiance_calibration_kernel(
                         lhsT=v_w[a][:, cols].bitcast(FP8X4),
                         lhsT_scale=v_s[4 * a : P, cols],
                         rhs=v2_w[a][h][:, o : o + w].bitcast(FP8X4),
-                        rhs_scale=v2_s[h][4 * a : P, o : o + w],
+                        rhs_scale=v2_s[h][8 + 4 * a : P, o : o + w],
                         start=(a == 0),
                         stop=(a == PASSES - 1),
                     )
@@ -174,10 +175,10 @@ def tile_list_satellite_radiance_calibration_kernel(
             w = CHUNKS[c]
             hb = work.tile([P, w * PACK], BF16, name="hb", align_bytes=64)
             h2b = work.tile([P, w * PACK], BF16, name="h2b", align_bytes=64)
-            c_view = clamped[c, g][:].rearrange("p t (b i) -> p b t i", i=4)
-            h_view = scaled[c, g][:].rearrange("p t (b i) -> p b t i", i=4)
-            nc.scalar.copy(hb[:].rearrange("p (b i t) -> p b t i", i=4, t=PACK), h_view)
-            nc.vector.tensor_tensor(h2b[:].rearrange("p (b i t) -> p b t i", i=4, t=PACK), h_view, c_view, ALU.mult)
+            c_view = clamped[c, g][:].rearrange("p t (b i) -> p b t i", i=2)
+            h_view = scaled[c, g][:].rearrange("p t (b i) -> p b t i", i=2)
+            nc.scalar.copy(hb[:].rearrange("p (b i t) -> p b t i", i=2, t=PACK), h_view)
+            nc.vector.tensor_tensor(h2b[:].rearrange("p (b i t) -> p b t i", i=2, t=PACK), h_view, c_view, ALU.mult)
             woven[c, g] = (hb, h2b)
 
         def quantise(c, g):
@@ -230,7 +231,7 @@ def tile_list_satellite_radiance_calibration_kernel(
                 nc.scalar.copy(y32[:, :, js], acc[:])
             if c < VY:
                 nc.vector.tensor_copy(
-                    yb[:].rearrange("p (b i t) -> p b t i", i=4, t=PACK), y32[:].rearrange("p t (b i) -> p b t i", i=4)
+                    yb[:].rearrange("p (b i t) -> p b t i", i=2, t=PACK), y32[:].rearrange("p t (b i) -> p b t i", i=2)
                 )
             nc.sync.dma_start(out_0.rearrange("(p t) j -> p t j", t=PACK)[:, :, j0 : j0 + w], y32[:])
             nc.vector.quantize_mx(y_q[:].bitcast(FP8X4), y_s[:, j0 : j0 + w], yb[:])

@@ -20,9 +20,22 @@ P = 128
 PACK = 4
 PASSES = 2
 HALF = 512
-CHUNKS = (512,256,128,128)
+CHUNKS = (256,256,256,128,128)
 YB = 128
-VY = 2
+
+
+def pieces(width, largest):
+    out, at = [], 0
+    while at < width:
+        size = largest
+        while size > width - at:
+            size = size // 2
+        out.append((at, size))
+        at = at + size
+    return out
+
+
+VY = 3
 GT = 0
 
 
@@ -33,7 +46,7 @@ def tile_list_satellite_radiance_calibration_kernel(
     nc = tc.nc
     with ExitStack() as ctx:
         held = ctx.enter_context(tc.tile_pool(name="held", bufs=1))
-        work = ctx.enter_context(tc.tile_pool(name="work", bufs=2))
+        work = ctx.enter_context(tc.tile_pool(name="work", bufs=3))
         psum_a = ctx.enter_context(tc.psum_pool(name="psum_a", bufs=6))
         psum_y = ctx.enter_context(tc.psum_pool(name="psum_y", bufs=2))
 
@@ -51,10 +64,10 @@ def tile_list_satellite_radiance_calibration_kernel(
         gain_t = held.tile([P, PASSES, PACK], F32, name="gain_t")
 
         warm = held.tile([P, 2], F32, name="warm")
-        nc.vector.memset(tab_s[:].bitcast(I32), 0)
-        nc.vector.memset(warm[:, 0:1], 0.0)
+        nc.gpsimd.memset(tab_s[:].bitcast(I32), 0)
         nc.vector.memset(tab2_s[:].bitcast(I32), 0)
-        nc.vector.memset(w4_s[:].rearrange("p a n -> p (a n)").bitcast(I32), 0)
+        nc.gpsimd.memset(w4_s[:].rearrange("p a n -> p (a n)").bitcast(I32), 0)
+        nc.vector.memset(warm[:, 0:1], 0.0)
 
         def load_words(dst, words, a):
             nc.sync.dma_start(dst[:].bitcast(I32), words[a].rearrange("p t i -> p (t i)").bitcast(I32))
@@ -66,32 +79,36 @@ def tile_list_satellite_radiance_calibration_kernel(
                     scales[:, 4 * q : 4 * q + 4, :].bitcast(I32),
                 )
 
+        def load_w1(g):
+            nc.sync.dma_start(w1_raw[g][:], w1[g * HALF : (g + 1) * HALF, :].rearrange("(p j) n -> p j n", j=PACK))
+
         nc.sync.dma_start(list1[:], offs)
-        load_words(tab_w[0], tab_words, 0)
         load_scales(nc.scalar, tab_s, 0, tab_scales)
+        load_words(tab_w[0], tab_words, 0)
         nc.sync.dma_start(list2[:], offs2)
         load_words(tab_w[1], tab_words, 1)
-        load_scales(nc.gpsimd, tab2_s, 8, tab2_scales)
+        load_scales(nc.scalar, tab2_s, 8, tab2_scales)
         load_words(tab2_w[0], tab2_words, 0)
-        nc.sync.dma_start(w4_w[:].bitcast(I32), w4_words.rearrange("a p b -> p a b").bitcast(I32))
-        load_words(tab2_w[1], tab2_words, 1)
         for dst, src in ((lo_t, lo), (hi_t, hi), (gain_t, gain)):
-            nc.scalar.dma_start(dst[:], src.rearrange("(g p t) -> p g t", g=PASSES, t=PACK))
-        nc.scalar.activation(warm[:, 1:2], warm[:, 0:1], ACT.Copy)
+            nc.sync.dma_start(dst[:], src.rearrange("(g p t) -> p g t", g=PASSES, t=PACK))
+        nc.sync.dma_start(w4_w[:].bitcast(I32), w4_words.rearrange("a p b -> p a b").bitcast(I32))
+        load_w1(0)
+        load_words(tab2_w[1], tab2_words, 1)
+
+        load_w1(1)
         for q in range(4):
-            nc.scalar.dma_start(
+            nc.sync.dma_start(
                 w4_s[32 * q : 32 * q + 4, :, :].bitcast(I32),
                 w4_scales[:, 4 * q : 4 * q + 4, :].rearrange("a r n -> r a n").bitcast(I32),
             )
-        for g in range(PASSES):
-            nc.sync.dma_start(w1_raw[g][:], w1[g * HALF : (g + 1) * HALF, :].rearrange("(p j) n -> p j n", j=PACK))
+        nc.scalar.activation(warm[:, 1:2], warm[:, 0:1], ACT.Copy)
 
         v_sg = held.tile([P, S], U8, name="v_sg", align_bytes=64)
         v_s = held.tile([P, S], U8, name="v_s", align_bytes=64)
         v_wg = [held.tile([P, S], U32, name=f"v_wg{a}", align_bytes=64) for a in range(PASSES)]
         v_w = [held.tile([P, S], U32, name=f"v_w{a}", align_bytes=64) for a in range(PASSES)]
-        v2_s = [held.tile([P, HALF], U8, name=f"v2_s{h}", align_bytes=64) for h in range(2)]
-        v2_w = [[held.tile([P, HALF], U32, name=f"v2_w{a}{h}", align_bytes=64) for h in range(2)] for a in range(PASSES)]
+        v2_s = held.tile([P, S2], U8, name="v2_s", align_bytes=64)
+        v2_w = [held.tile([P, S2], U32, name=f"v2_w{a}", align_bytes=64) for a in range(PASSES)]
 
         def deal(dst, src, run):
             nc.vector.tensor_copy(
@@ -107,11 +124,11 @@ def tile_list_satellite_radiance_calibration_kernel(
         deal(v_s[:], v_sg[:], 16)
         nc.vector.tensor_copy(v_wg[1][:], tab_w[1][:].indirect(list1[:]))
         deal(v_w[0][:], v_wg[0][:], 4)
-        nc.vector.tensor_copy(v2_s[0][:], tab2_s[:].indirect(half_list(0)))
+        nc.vector.tensor_copy(v2_s[:, 0 * HALF : 1 * HALF], tab2_s[:].indirect(half_list(0)))
         deal(v_w[1][:], v_wg[1][:], 4)
-        nc.vector.tensor_copy(v2_w[0][0][:], tab2_w[0][:].indirect(half_list(0)))
-        nc.vector.tensor_copy(v2_s[1][:], tab2_s[:].indirect(half_list(1)))
-        nc.vector.tensor_copy(v2_w[0][1][:], tab2_w[0][:].indirect(half_list(1)))
+        nc.vector.tensor_copy(v2_w[0][:, 0 * HALF : 1 * HALF], tab2_w[0][:].indirect(half_list(0)))
+        nc.vector.tensor_copy(v2_s[:, 1 * HALF : 2 * HALF], tab2_s[:].indirect(half_list(1)))
+        nc.vector.tensor_copy(v2_w[0][:, 1 * HALF : 2 * HALF], tab2_w[0][:].indirect(half_list(1)))
 
         w4_sd = held.tile([P, PASSES * N], U8, name="w4_sd", align_bytes=64)
         w4_wd = held.tile([P, PASSES * 2 * N], U8, name="w4_wd", align_bytes=64)
@@ -120,18 +137,17 @@ def tile_list_satellite_radiance_calibration_kernel(
         w1_s = [held.tile([P, N], U8, name=f"w1_s{g}", align_bytes=64) for g in range(PASSES)]
         y_s = held.tile([P, S2], U8, name="y_s", align_bytes=64)
 
-        deal(w4_sd[:], w4_s[:].rearrange("p a n -> p (a n)"), 16)
         deal(w4_wd[:].bitcast(U16), w4_w[:].rearrange("p a b -> p (a b)").bitcast(U16), 8)
-        nc.vector.tensor_copy(v2_w[1][0][:], tab2_w[1][:].indirect(half_list(0)))
+        nc.vector.tensor_copy(v2_w[1][:, 0 * HALF : 1 * HALF], tab2_w[1][:].indirect(half_list(0)))
 
         def late_head():
-            nc.vector.tensor_copy(v2_w[1][1][:], tab2_w[1][:].indirect(half_list(1)))
+            nc.vector.tensor_copy(v2_w[1][:, 1 * HALF : 2 * HALF], tab2_w[1][:].indirect(half_list(1)))
 
         def round_w1(g):
-            nc.scalar.copy(
-                w1_b[g][:].rearrange("p (t m j) -> p m t j", t=PACK, j=PACK),
-                w1_raw[g][:].rearrange("p j (m t) -> p m t j", t=PACK),
-            )
+            dst = w1_b[g][:].rearrange("p (u e m j) -> p u m j e", u=2, e=2, j=PACK)
+            src = w1_raw[g][:].rearrange("p j (m u e) -> p u m j e", u=2, e=2)
+            for u in range(2):
+                nc.scalar.copy(dst[:, u], src[:, u])
 
         def quant_w1(g):
             nc.vector.quantize_mx(w1_q[g][:].bitcast(FP8X4), w1_s[g][:], w1_b[g][:])
@@ -142,25 +158,27 @@ def tile_list_satellite_radiance_calibration_kernel(
         scaled = {}
         woven = {}
         quantised = {}
+        results = {}
 
         def first_product(c, g):
             j0, w = starts[c], CHUNKS[c]
-            h, o = divmod(j0, HALF)
             c32 = work.tile([P, PACK, w], F32, name="c32", align_bytes=64, bufs=3)
             h32 = work.tile([P, PACK, w], F32, name="h32", align_bytes=64, bufs=3)
             for t in range(PACK):
                 acc = psum_a.tile([P, w], F32, name="acc")
                 cols = slice(g * HALF + t * P, g * HALF + (t + 1) * P)
-                for a in range(PASSES):
-                    nc.tensor.matmul_mx(
-                        acc[:],
-                        lhsT=v_w[a][:, cols].bitcast(FP8X4),
-                        lhsT_scale=v_s[4 * a : P, cols],
-                        rhs=v2_w[a][h][:, o : o + w].bitcast(FP8X4),
-                        rhs_scale=v2_s[h][8 + 4 * a : P, o : o + w],
-                        start=(a == 0),
-                        stop=(a == PASSES - 1),
-                    )
+                for at, size in pieces(w, 512):
+                    js = slice(j0 + at, j0 + at + size)
+                    for a in range(PASSES):
+                        nc.tensor.matmul_mx(
+                            acc[:, at : at + size],
+                            lhsT=v_w[a][:, cols].bitcast(FP8X4),
+                            lhsT_scale=v_s[4 * a : P, cols],
+                            rhs=v2_w[a][:, js].bitcast(FP8X4),
+                            rhs_scale=v2_s[8 + 4 * a : P, js],
+                            start=(a == 0),
+                            stop=(a == PASSES - 1),
+                        )
                 nc.vector.tensor_scalar(
                     c32[:, t, :], acc[:], lo_t[:, g, t : t + 1], hi_t[:, g, t : t + 1], ALU.max, ALU.min
                 )
@@ -173,29 +191,35 @@ def tile_list_satellite_radiance_calibration_kernel(
 
         def weave(c, g):
             w = CHUNKS[c]
-            hb = work.tile([P, w * PACK], BF16, name="hb", align_bytes=64)
-            h2b = work.tile([P, w * PACK], BF16, name="h2b", align_bytes=64)
+            both = work.tile([P, 2 * w * PACK], BF16, name="both", align_bytes=64)
+            hb = both[:, : w * PACK]
+            h2b = both[:, w * PACK :]
             c_view = clamped[c, g][:].rearrange("p t (b i) -> p b t i", i=2)
             h_view = scaled[c, g][:].rearrange("p t (b i) -> p b t i", i=2)
-            nc.scalar.copy(hb[:].rearrange("p (b i t) -> p b t i", i=2, t=PACK), h_view)
-            nc.vector.tensor_tensor(h2b[:].rearrange("p (b i t) -> p b t i", i=2, t=PACK), h_view, c_view, ALU.mult)
-            woven[c, g] = (hb, h2b)
+            nc.scalar.copy(hb.rearrange("p (b i t) -> p b t i", i=2, t=PACK), h_view)
+            nc.vector.tensor_tensor(h2b.rearrange("p (b i t) -> p b t i", i=2, t=PACK), h_view, c_view, ALU.mult)
+            woven[c, g] = both
+
+        def quantise_all(codes, scales, s0, src, words):
+            for at, size in pieces(words, 1024):
+                nc.vector.quantize_mx(
+                    codes[:, at : at + size].bitcast(FP8X4),
+                    scales[:, s0 + at : s0 + at + size],
+                    src[:, at * PACK : (at + size) * PACK],
+                )
 
         def quantise(c, g):
             w = CHUNKS[c]
-            made = []
-            for name, src in zip(("h", "h2"), woven[c, g]):
-                codes = work.tile([P, w], U32, name=name + "_q", align_bytes=64, bufs=4)
-                scales = work.tile([P, w], U8, name=name + "_s", align_bytes=64, bufs=4)
-                nc.vector.quantize_mx(codes[:].bitcast(FP8X4), scales[:], src[:])
-                made.append((codes, scales))
-            quantised[c, g] = made
+            codes = work.tile([P, 2 * w], U32, name="h_q", align_bytes=64, bufs=4)
+            scales = work.tile([P, 2 * w], U8, name="h_s", align_bytes=64, bufs=4)
+            quantise_all(codes, scales, 0, woven[c, g], 2 * w)
+            quantised[c, g] = [(codes[:, :w], scales[:, :w]), (codes[:, w:], scales[:, w:])]
 
         def second_product(c):
             j0, w = starts[c], CHUNKS[c]
-            y32 = work.tile([P, PACK, w], F32, name="y32", align_bytes=64)
-            yb = work.tile([P, w * PACK], BF16, name="yb", align_bytes=64)
-            y_q = work.tile([P, w], U32, name="y_q", align_bytes=64)
+            y32 = held.tile([P, PACK, w], F32, name=f"y32_{c}", align_bytes=64)
+            yb = held.tile([P, w * PACK], BF16, name=f"yb_{c}", align_bytes=64)
+            results[c] = (y32, yb)
             for b in range(w // YB):
                 js = slice(b * YB, (b + 1) * YB)
                 acc = psum_y.tile([P, PACK, YB], F32, name="acc_y")
@@ -229,31 +253,42 @@ def tile_list_satellite_radiance_calibration_kernel(
                         acc[:].rearrange("p t j -> p j t"),
                     )
                 nc.scalar.copy(y32[:, :, js], acc[:])
+            nc.sync.dma_start(out_0.rearrange("(p t) j -> p t j", t=PACK)[:, :, j0 : j0 + w], y32[:])
+
+        def planes(c):
+            j0, w = starts[c], CHUNKS[c]
+            y32, yb = results[c]
+            y_q = held.tile([P, w], U32, name=f"y_q{c}", align_bytes=64)
             if c < VY:
                 nc.vector.tensor_copy(
                     yb[:].rearrange("p (b i t) -> p b t i", i=2, t=PACK), y32[:].rearrange("p t (b i) -> p b t i", i=2)
                 )
-            nc.sync.dma_start(out_0.rearrange("(p t) j -> p t j", t=PACK)[:, :, j0 : j0 + w], y32[:])
-            nc.vector.quantize_mx(y_q[:].bitcast(FP8X4), y_s[:, j0 : j0 + w], yb[:])
+            quantise_all(y_q, y_s, j0, yb, w)
             nc.sync.dma_start(
                 out_1[0].rearrange("p m t -> p (m t)").bitcast(I32)[:, j0 : j0 + w], y_q[:].bitcast(I32)
             )
 
-        for step in range(len(units) + 3):
+        round_w1(0)
+        quant_w1(0)
+        for step in range(len(units) + 4):
             if step < len(units):
                 first_product(*units[step])
             if step == 0:
                 late_head()
-            if step < PASSES:
-                round_w1(step)
-            if 0 <= step - 1 < len(units):
-                weave(*units[step - 1])
-            if 0 <= step - 1 < PASSES:
-                quant_w1(step - 1)
+            if step == 0:
+                round_w1(1)
             if 0 <= step - 2 < len(units):
-                quantise(*units[step - 2])
-            if 0 <= step - 3 < len(units) and units[step - 3][1] == PASSES - 1:
-                second_product(units[step - 3][0])
+                weave(*units[step - 2])
+            if step == 1:
+                quant_w1(1)
+                deal(w4_sd[:], w4_s[:].rearrange("p a n -> p (a n)"), 16)
+            if 0 <= step - 3 < len(units):
+                quantise(*units[step - 3])
+            if 0 <= step - 4 < len(units) and units[step - 4][1] == PASSES - 1:
+                second_product(units[step - 4][0])
+
+        for c in range(len(CHUNKS)):
+            planes(c)
 
         for q in range(4):
             queue = nc.sync if q % 2 == 0 else nc.scalar

@@ -66,7 +66,7 @@ def tile_list_satellite_radiance_calibration_kernel(
         warm = held.tile([P, 2], F32, name="warm")
         nc.gpsimd.memset(tab_s[:].bitcast(I32), 0)
         nc.vector.memset(tab2_s[:].bitcast(I32), 0)
-        nc.gpsimd.memset(w4_s[:].rearrange("p a n -> p (a n)").bitcast(I32), 0)
+        nc.vector.memset(w4_s[:].rearrange("p a n -> p (a n)").bitcast(I32), 0)
         nc.vector.memset(warm[:, 0:1], 0.0)
 
         def load_words(dst, words, a):
@@ -87,7 +87,7 @@ def tile_list_satellite_radiance_calibration_kernel(
         load_words(tab_w[0], tab_words, 0)
         nc.sync.dma_start(list2[:], offs2)
         load_words(tab_w[1], tab_words, 1)
-        load_scales(nc.scalar, tab2_s, 8, tab2_scales)
+        load_scales(nc.gpsimd, tab2_s, 8, tab2_scales)
         load_words(tab2_w[0], tab2_words, 0)
         for dst, src in ((lo_t, lo), (hi_t, hi), (gain_t, gain)):
             nc.sync.dma_start(dst[:], src.rearrange("(g p t) -> p g t", g=PASSES, t=PACK))
@@ -164,14 +164,15 @@ def tile_list_satellite_radiance_calibration_kernel(
             j0, w = starts[c], CHUNKS[c]
             c32 = work.tile([P, PACK, w], F32, name="c32", align_bytes=64, bufs=3)
             h32 = work.tile([P, PACK, w], F32, name="h32", align_bytes=64, bufs=3)
-            for t in range(PACK):
-                acc = psum_a.tile([P, w], F32, name="acc")
-                cols = slice(g * HALF + t * P, g * HALF + (t + 1) * P)
-                for at, size in pieces(w, 512):
-                    js = slice(j0 + at, j0 + at + size)
+            js = slice(j0, j0 + w)
+            per_bank = 1
+            for t0 in range(0, PACK, per_bank):
+                acc = psum_a.tile([P, per_bank, w], F32, name="acc")
+                for t in range(t0, t0 + per_bank):
+                    cols = slice(g * HALF + t * P, g * HALF + (t + 1) * P)
                     for a in range(PASSES):
                         nc.tensor.matmul_mx(
-                            acc[:, at : at + size],
+                            acc[:, t - t0, :],
                             lhsT=v_w[a][:, cols].bitcast(FP8X4),
                             lhsT_scale=v_s[4 * a : P, cols],
                             rhs=v2_w[a][:, js].bitcast(FP8X4),
@@ -179,12 +180,10 @@ def tile_list_satellite_radiance_calibration_kernel(
                             start=(a == 0),
                             stop=(a == PASSES - 1),
                         )
-                nc.vector.tensor_scalar(
-                    c32[:, t, :], acc[:], lo_t[:, g, t : t + 1], hi_t[:, g, t : t + 1], ALU.max, ALU.min
-                )
-                if t < GT:
-                    nc.gpsimd.tensor_scalar(h32[:, t, :], c32[:, t, :], gain_t[:, g, t : t + 1], 1.0, ALU.mult, ALU.mult)
-                else:
+                for t in range(t0, t0 + per_bank):
+                    nc.vector.tensor_scalar(
+                        c32[:, t, :], acc[:, t - t0, :], lo_t[:, g, t : t + 1], hi_t[:, g, t : t + 1], ALU.max, ALU.min
+                    )
                     nc.scalar.activation(h32[:, t, :], c32[:, t, :], ACT.Copy, scale=gain_t[:, g, t : t + 1])
             clamped[c, g] = c32
             scaled[c, g] = h32

@@ -22,6 +22,7 @@ PASSES = 2
 HALF = 512
 CHUNKS = (256,256,256,128,128)
 YB = 128
+EARLY = 3
 
 
 def pieces(width, largest):
@@ -36,7 +37,7 @@ def pieces(width, largest):
 
 
 VY = 3
-GT = 0
+S_EVAC = ()
 
 
 def tile_list_satellite_radiance_calibration_kernel(
@@ -46,7 +47,7 @@ def tile_list_satellite_radiance_calibration_kernel(
     nc = tc.nc
     with ExitStack() as ctx:
         held = ctx.enter_context(tc.tile_pool(name="held", bufs=1))
-        work = ctx.enter_context(tc.tile_pool(name="work", bufs=3))
+        work = ctx.enter_context(tc.tile_pool(name="work", bufs=4))
         psum_a = ctx.enter_context(tc.psum_pool(name="psum_a", bufs=6))
         psum_y = ctx.enter_context(tc.psum_pool(name="psum_y", bufs=2))
 
@@ -63,11 +64,9 @@ def tile_list_satellite_radiance_calibration_kernel(
         hi_t = held.tile([P, PASSES, PACK], F32, name="hi_t")
         gain_t = held.tile([P, PASSES, PACK], F32, name="gain_t")
 
-        warm = held.tile([P, 2], F32, name="warm")
-        nc.gpsimd.memset(tab_s[:].bitcast(I32), 0)
-        nc.vector.memset(tab2_s[:].bitcast(I32), 0)
+        nc.vector.memset(tab_s[:].bitcast(I32), 0)
+        nc.gpsimd.memset(tab2_s[:].bitcast(I32), 0)
         nc.vector.memset(w4_s[:].rearrange("p a n -> p (a n)").bitcast(I32), 0)
-        nc.vector.memset(warm[:, 0:1], 0.0)
 
         def load_words(dst, words, a):
             nc.sync.dma_start(dst[:].bitcast(I32), words[a].rearrange("p t i -> p (t i)").bitcast(I32))
@@ -83,25 +82,23 @@ def tile_list_satellite_radiance_calibration_kernel(
             nc.sync.dma_start(w1_raw[g][:], w1[g * HALF : (g + 1) * HALF, :].rearrange("(p j) n -> p j n", j=PACK))
 
         nc.sync.dma_start(list1[:], offs)
-        load_scales(nc.scalar, tab_s, 0, tab_scales)
+        nc.sync.dma_start(w4_w[:].bitcast(I32), w4_words.rearrange("a p b -> p a b").bitcast(I32))
+        load_scales(nc.sync, tab_s, 0, tab_scales)
         load_words(tab_w[0], tab_words, 0)
         nc.sync.dma_start(list2[:], offs2)
         load_words(tab_w[1], tab_words, 1)
-        load_scales(nc.gpsimd, tab2_s, 8, tab2_scales)
+        load_scales(nc.sync, tab2_s, 8, tab2_scales)
         load_words(tab2_w[0], tab2_words, 0)
-        for dst, src in ((lo_t, lo), (hi_t, hi), (gain_t, gain)):
-            nc.sync.dma_start(dst[:], src.rearrange("(g p t) -> p g t", g=PASSES, t=PACK))
-        nc.sync.dma_start(w4_w[:].bitcast(I32), w4_words.rearrange("a p b -> p a b").bitcast(I32))
         load_w1(0)
         load_words(tab2_w[1], tab2_words, 1)
-
+        for dst, src in ((lo_t, lo), (hi_t, hi), (gain_t, gain)):
+            nc.sync.dma_start(dst[:], src.rearrange("(g p t) -> p g t", g=PASSES, t=PACK))
         load_w1(1)
         for q in range(4):
             nc.sync.dma_start(
                 w4_s[32 * q : 32 * q + 4, :, :].bitcast(I32),
                 w4_scales[:, 4 * q : 4 * q + 4, :].rearrange("a r n -> r a n").bitcast(I32),
             )
-        nc.scalar.activation(warm[:, 1:2], warm[:, 0:1], ACT.Copy)
 
         v_sg = held.tile([P, S], U8, name="v_sg", align_bytes=64)
         v_s = held.tile([P, S], U8, name="v_s", align_bytes=64)
@@ -119,25 +116,23 @@ def tile_list_satellite_radiance_calibration_kernel(
         def half_list(h):
             return list2[:, h * (HALF // 16) : (h + 1) * (HALF // 16)]
 
+        w4_wd = held.tile([P, PASSES * 2 * N], U8, name="w4_wd", align_bytes=64)
+        deal(w4_wd[:].bitcast(U16), w4_w[:].rearrange("p a b -> p (a b)").bitcast(U16), 8)
         nc.vector.tensor_copy(v_sg[:], tab_s[:].indirect(list1[:]))
         nc.vector.tensor_copy(v_wg[0][:], tab_w[0][:].indirect(list1[:]))
         deal(v_s[:], v_sg[:], 16)
         nc.vector.tensor_copy(v_wg[1][:], tab_w[1][:].indirect(list1[:]))
         deal(v_w[0][:], v_wg[0][:], 4)
-        nc.vector.tensor_copy(v2_s[:, 0 * HALF : 1 * HALF], tab2_s[:].indirect(half_list(0)))
+        nc.vector.tensor_copy(v2_s[:], tab2_s[:].indirect(list2[:]))
         deal(v_w[1][:], v_wg[1][:], 4)
-        nc.vector.tensor_copy(v2_w[0][:, 0 * HALF : 1 * HALF], tab2_w[0][:].indirect(half_list(0)))
-        nc.vector.tensor_copy(v2_s[:, 1 * HALF : 2 * HALF], tab2_s[:].indirect(half_list(1)))
-        nc.vector.tensor_copy(v2_w[0][:, 1 * HALF : 2 * HALF], tab2_w[0][:].indirect(half_list(1)))
+        nc.vector.tensor_copy(v2_w[0][:], tab2_w[0][:].indirect(list2[:]))
 
         w4_sd = held.tile([P, PASSES * N], U8, name="w4_sd", align_bytes=64)
-        w4_wd = held.tile([P, PASSES * 2 * N], U8, name="w4_wd", align_bytes=64)
         w1_b = [held.tile([P, N * PACK], BF16, name=f"w1_b{g}", align_bytes=64) for g in range(PASSES)]
         w1_q = [held.tile([P, N], U32, name=f"w1_q{g}", align_bytes=64) for g in range(PASSES)]
         w1_s = [held.tile([P, N], U8, name=f"w1_s{g}", align_bytes=64) for g in range(PASSES)]
         y_s = held.tile([P, S2], U8, name="y_s", align_bytes=64)
 
-        deal(w4_wd[:].bitcast(U16), w4_w[:].rearrange("p a b -> p (a b)").bitcast(U16), 8)
         nc.vector.tensor_copy(v2_w[1][:, 0 * HALF : 1 * HALF], tab2_w[1][:].indirect(half_list(0)))
 
         def late_head():
@@ -155,6 +150,7 @@ def tile_list_satellite_radiance_calibration_kernel(
         starts = [sum(CHUNKS[:c]) for c in range(len(CHUNKS))]
         units = [(c, g) for c in range(len(CHUNKS)) for g in range(PASSES)]
         clamped = {}
+        staged = {}
         scaled = {}
         woven = {}
         quantised = {}
@@ -162,10 +158,14 @@ def tile_list_satellite_radiance_calibration_kernel(
 
         def first_product(c, g):
             j0, w = starts[c], CHUNKS[c]
-            c32 = work.tile([P, PACK, w], F32, name="c32", align_bytes=64, bufs=3)
-            h32 = work.tile([P, PACK, w], F32, name="h32", align_bytes=64, bufs=3)
+            c32 = work.tile([P, PACK, w], F32, name="c32", align_bytes=64, bufs=4)
+            h32 = work.tile([P, PACK, w], F32, name="h32", align_bytes=64, bufs=4)
             js = slice(j0, j0 + w)
             per_bank = 1
+            if 2 * c + g in S_EVAC:
+                per_bank = HALF // w
+                a32 = work.tile([P, PACK, w], F32, name="a32", align_bytes=64, bufs=4)
+                staged[c, g] = a32
             for t0 in range(0, PACK, per_bank):
                 acc = psum_a.tile([P, per_bank, w], F32, name="acc")
                 for t in range(t0, t0 + per_bank):
@@ -180,13 +180,25 @@ def tile_list_satellite_radiance_calibration_kernel(
                             start=(a == 0),
                             stop=(a == PASSES - 1),
                         )
-                for t in range(t0, t0 + per_bank):
-                    nc.vector.tensor_scalar(
-                        c32[:, t, :], acc[:, t - t0, :], lo_t[:, g, t : t + 1], hi_t[:, g, t : t + 1], ALU.max, ALU.min
-                    )
-                    nc.scalar.activation(h32[:, t, :], c32[:, t, :], ACT.Copy, scale=gain_t[:, g, t : t + 1])
+                if 2 * c + g in S_EVAC:
+                    nc.scalar.copy(a32[:, t0 : t0 + per_bank, :], acc[:])
+                else:
+                    for t in range(t0, t0 + per_bank):
+                        nc.vector.tensor_scalar(
+                            c32[:, t, :], acc[:, t - t0, :], lo_t[:, g, t : t + 1], hi_t[:, g, t : t + 1], ALU.max, ALU.min
+                        )
+                        nc.scalar.activation(h32[:, t, :], c32[:, t, :], ACT.Copy, scale=gain_t[:, g, t : t + 1])
             clamped[c, g] = c32
             scaled[c, g] = h32
+
+        def clamp(c, g):
+            if 2 * c + g in S_EVAC:
+                a32, c32, h32 = staged[c, g], clamped[c, g], scaled[c, g]
+                for t in range(PACK):
+                    nc.vector.tensor_scalar(
+                        c32[:, t, :], a32[:, t, :], lo_t[:, g, t : t + 1], hi_t[:, g, t : t + 1], ALU.max, ALU.min
+                    )
+                    nc.scalar.activation(h32[:, t, :], c32[:, t, :], ACT.Copy, scale=gain_t[:, g, t : t + 1])
 
         def weave(c, g):
             w = CHUNKS[c]
@@ -214,6 +226,36 @@ def tile_list_satellite_radiance_calibration_kernel(
             quantise_all(codes, scales, 0, woven[c, g], 2 * w)
             quantised[c, g] = [(codes[:, :w], scales[:, :w]), (codes[:, w:], scales[:, w:])]
 
+        banks = {}
+
+        def passes(c, b, g):
+            js = slice(b * YB, (b + 1) * YB)
+            if g == 0:
+                banks[c, b] = psum_y.tile([P, PACK, YB], F32, name="acc_y")
+            acc = banks[c, b]
+            for t in range(PACK):
+                codes, scales = quantised[c, g][0]
+                nc.tensor.matmul_mx(
+                    acc[:, t, :],
+                    lhsT=w1_q[g][:, t * P : (t + 1) * P].bitcast(FP8X4),
+                    lhsT_scale=w1_s[g][:, t * P : (t + 1) * P],
+                    rhs=codes[:, js].bitcast(FP8X4),
+                    rhs_scale=scales[:, js],
+                    start=(g == 0 and t == 0),
+                    stop=False,
+                )
+                codes, scales = quantised[c, g][1]
+                n0 = g * N + t * P
+                nc.tensor.matmul_mx(
+                    acc[:, t, :],
+                    lhsT=w4_wd[:, 2 * n0 : 2 * (n0 + P)].bitcast(FP4X4),
+                    lhsT_scale=w4_sd[:, n0 : n0 + P],
+                    rhs=codes[:, js].bitcast(FP8X4),
+                    rhs_scale=scales[:, js],
+                    start=False,
+                    stop=(g == PASSES - 1 and t == PACK - 1),
+                )
+
         def second_product(c):
             j0, w = starts[c], CHUNKS[c]
             y32 = held.tile([P, PACK, w], F32, name=f"y32_{c}", align_bytes=64)
@@ -221,31 +263,10 @@ def tile_list_satellite_radiance_calibration_kernel(
             results[c] = (y32, yb)
             for b in range(w // YB):
                 js = slice(b * YB, (b + 1) * YB)
-                acc = psum_y.tile([P, PACK, YB], F32, name="acc_y")
-                for t in range(PACK):
-                    for g in range(PASSES):
-                        codes, scales = quantised[c, g][0]
-                        nc.tensor.matmul_mx(
-                            acc[:, t, :],
-                            lhsT=w1_q[g][:, t * P : (t + 1) * P].bitcast(FP8X4),
-                            lhsT_scale=w1_s[g][:, t * P : (t + 1) * P],
-                            rhs=codes[:, js].bitcast(FP8X4),
-                            rhs_scale=scales[:, js],
-                            start=(g == 0),
-                            stop=False,
-                        )
-                    for g in range(PASSES):
-                        codes, scales = quantised[c, g][1]
-                        n0 = g * N + t * P
-                        nc.tensor.matmul_mx(
-                            acc[:, t, :],
-                            lhsT=w4_wd[:, 2 * n0 : 2 * (n0 + P)].bitcast(FP4X4),
-                            lhsT_scale=w4_sd[:, n0 : n0 + P],
-                            rhs=codes[:, js].bitcast(FP8X4),
-                            rhs_scale=scales[:, js],
-                            start=False,
-                            stop=(g == PASSES - 1),
-                        )
+                if c < EARLY:
+                    passes(c, b, 0)
+                passes(c, b, 1)
+                acc = banks[c, b]
                 if c >= VY:
                     nc.scalar.copy(
                         yb[:, b * YB * PACK : (b + 1) * YB * PACK].rearrange("p (j t) -> p j t", t=PACK),
@@ -269,13 +290,15 @@ def tile_list_satellite_radiance_calibration_kernel(
 
         round_w1(0)
         quant_w1(0)
-        for step in range(len(units) + 4):
+        for step in range(len(units) + 5):
             if step < len(units):
                 first_product(*units[step])
             if step == 0:
                 late_head()
             if step == 0:
                 round_w1(1)
+            if 0 <= step - 1 < len(units):
+                clamp(*units[step - 1])
             if 0 <= step - 2 < len(units):
                 weave(*units[step - 2])
             if step == 1:
@@ -285,6 +308,9 @@ def tile_list_satellite_radiance_calibration_kernel(
                 quantise(*units[step - 3])
             if 0 <= step - 4 < len(units) and units[step - 4][1] == PASSES - 1:
                 second_product(units[step - 4][0])
+            if 0 <= step - 4 < len(units) and units[step - 4][1] == 0 and units[step - 4][0] >= EARLY:
+                for b in range(CHUNKS[units[step - 4][0]] // YB):
+                    passes(units[step - 4][0], b, 0)
 
         for c in range(len(CHUNKS)):
             planes(c)

@@ -89,10 +89,10 @@ def tile_list_satellite_radiance_calibration_kernel(
         load_words(tab_w[1], tab_words, 1)
         load_scales(nc.sync, tab2_s, 8, tab2_scales)
         load_words(tab2_w[0], tab2_words, 0)
-        load_w1(0)
         load_words(tab2_w[1], tab2_words, 1)
         for dst, src in ((lo_t, lo), (hi_t, hi), (gain_t, gain)):
             nc.sync.dma_start(dst[:], src.rearrange("(g p t) -> p g t", g=PASSES, t=PACK))
+        load_w1(0)
         load_w1(1)
         for q in range(4):
             nc.sync.dma_start(
@@ -288,21 +288,20 @@ def tile_list_satellite_radiance_calibration_kernel(
                 out_1[0].rearrange("p m t -> p (m t)").bitcast(I32)[:, j0 : j0 + w], y_q[:].bitcast(I32)
             )
 
-        round_w1(0)
-        quant_w1(0)
         for step in range(len(units) + 5):
             if step < len(units):
                 first_product(*units[step])
             if step == 0:
                 late_head()
-            if step == 0:
-                round_w1(1)
+            if step in (1, 2):
+                round_w1(step - 1)
             if 0 <= step - 1 < len(units):
                 clamp(*units[step - 1])
             if 0 <= step - 2 < len(units):
                 weave(*units[step - 2])
-            if step == 1:
-                quant_w1(1)
+            if step in (2, 3):
+                quant_w1(step - 2)
+            if step == 3:
                 deal(w4_sd[:], w4_s[:].rearrange("p a n -> p (a n)"), 16)
             if 0 <= step - 3 < len(units):
                 quantise(*units[step - 3])

@@ -65,44 +65,56 @@ def tile_list_satellite_radiance_calibration_kernel(
         gain_t = held.tile([P, PASSES, PACK], F32, name="gain_t")
 
         nc.vector.memset(tab_s[:].bitcast(I32), 0)
-        nc.gpsimd.memset(tab2_s[:].bitcast(I32), 0)
+        nc.vector.memset(tab2_s[:].bitcast(I32), 0)
         nc.vector.memset(w4_s[:].rearrange("p a n -> p (a n)").bitcast(I32), 0)
 
         def load_words(dst, words, a):
             nc.sync.dma_start(dst[:].bitcast(I32), words[a].rearrange("p t i -> p (t i)").bitcast(I32))
 
-        def load_scales(queue, dst, row, scales):
-            for q in range(4):
-                queue.dma_start(
-                    dst[32 * q + row : 32 * q + row + 4 * PASSES, :].bitcast(I32),
-                    scales[:, 4 * q : 4 * q + 4, :].bitcast(I32),
-                )
+        def load_quadrant(dst, row, scales, q):
+            nc.sync.dma_start(
+                dst[32 * q + row : 32 * q + row + 4 * PASSES, :].bitcast(I32),
+                scales[:, 4 * q : 4 * q + 4, :].bitcast(I32),
+            )
+
+        def load_rows(dst, row, scales, q, a):
+            at = 32 * q + row + 4 * a
+            nc.sync.dma_start(dst[at : at + 4, :].bitcast(I32), scales[a, 4 * q : 4 * q + 4, :].bitcast(I32))
 
         def load_w1(g):
             nc.sync.dma_start(w1_raw[g][:], w1[g * HALF : (g + 1) * HALF, :].rearrange("(p j) n -> p j n", j=PACK))
 
+        def load_w4():
+            nc.sync.dma_start(w4_w[:].bitcast(I32), w4_words.rearrange("a p b -> p a b").bitcast(I32))
+
+        def load_w4_scales():
+            for q in range(4):
+                nc.sync.dma_start(
+                    w4_s[32 * q : 32 * q + 4, :, :].bitcast(I32),
+                    w4_scales[:, 4 * q : 4 * q + 4, :].rearrange("a r n -> r a n").bitcast(I32),
+                )
+
         nc.sync.dma_start(list1[:], offs)
-        nc.sync.dma_start(w4_w[:].bitcast(I32), w4_words.rearrange("a p b -> p a b").bitcast(I32))
-        load_scales(nc.sync, tab_s, 0, tab_scales)
-        load_words(tab_w[0], tab_words, 0)
         nc.sync.dma_start(list2[:], offs2)
+        load_words(tab_w[0], tab_words, 0)
+        for q in range(4):
+            load_quadrant(tab_s, 0, tab_scales, q)
+        load_quadrant(tab2_s, 8, tab2_scales, 0)
         load_words(tab_w[1], tab_words, 1)
-        load_scales(nc.sync, tab2_s, 8, tab2_scales)
+        for q in range(1, 4):
+            for a in range(PASSES):
+                load_rows(tab2_s, 8, tab2_scales, q, a)
         load_words(tab2_w[0], tab2_words, 0)
+        load_w4()
+        load_w4_scales()
         load_words(tab2_w[1], tab2_words, 1)
         for dst, src in ((lo_t, lo), (hi_t, hi), (gain_t, gain)):
             nc.sync.dma_start(dst[:], src.rearrange("(g p t) -> p g t", g=PASSES, t=PACK))
         load_w1(0)
         load_w1(1)
-        for q in range(4):
-            nc.sync.dma_start(
-                w4_s[32 * q : 32 * q + 4, :, :].bitcast(I32),
-                w4_scales[:, 4 * q : 4 * q + 4, :].rearrange("a r n -> r a n").bitcast(I32),
-            )
 
         v_sg = held.tile([P, S], U8, name="v_sg", align_bytes=64)
         v_s = held.tile([P, S], U8, name="v_s", align_bytes=64)
-        v_wg = [held.tile([P, S], U32, name=f"v_wg{a}", align_bytes=64) for a in range(PASSES)]
         v_w = [held.tile([P, S], U32, name=f"v_w{a}", align_bytes=64) for a in range(PASSES)]
         v2_s = held.tile([P, S2], U8, name="v2_s", align_bytes=64)
         v2_w = [held.tile([P, S2], U32, name=f"v2_w{a}", align_bytes=64) for a in range(PASSES)]
@@ -113,21 +125,23 @@ def tile_list_satellite_radiance_calibration_kernel(
                 src.rearrange("p (g b i t) -> p g b t i", g=PASSES, t=PACK, i=run),
             )
 
+        def dealt(tile):
+            return tile[:].rearrange("p (g t m) -> p g m t", g=PASSES, t=PACK)
+
         def half_list(h):
             return list2[:, h * (HALF // 16) : (h + 1) * (HALF // 16)]
 
         w4_wd = held.tile([P, PASSES * 2 * N], U8, name="w4_wd", align_bytes=64)
-        deal(w4_wd[:].bitcast(U16), w4_w[:].rearrange("p a b -> p (a b)").bitcast(U16), 8)
-        nc.vector.tensor_copy(v_sg[:], tab_s[:].indirect(list1[:]))
-        nc.vector.tensor_copy(v_wg[0][:], tab_w[0][:].indirect(list1[:]))
-        deal(v_s[:], v_sg[:], 16)
-        nc.vector.tensor_copy(v_wg[1][:], tab_w[1][:].indirect(list1[:]))
-        deal(v_w[0][:], v_wg[0][:], 4)
-        nc.vector.tensor_copy(v2_s[:], tab2_s[:].indirect(list2[:]))
-        deal(v_w[1][:], v_wg[1][:], 4)
-        nc.vector.tensor_copy(v2_w[0][:], tab2_w[0][:].indirect(list2[:]))
-
         w4_sd = held.tile([P, PASSES * N], U8, name="w4_sd", align_bytes=64)
+        nc.vector.tensor_copy(dealt(v_w[0]), tab_w[0][:].indirect(list1[:]))
+        nc.vector.tensor_copy(v_sg[:], tab_s[:].indirect(list1[:]))
+        nc.vector.tensor_copy(dealt(v_w[1]), tab_w[1][:].indirect(list1[:]))
+        deal(v_s[:], v_sg[:], 16)
+        nc.vector.tensor_copy(v2_s[:], tab2_s[:].indirect(list2[:]))
+        deal(w4_wd[:].bitcast(U16), w4_w[:].rearrange("p a b -> p (a b)").bitcast(U16), 8)
+        nc.vector.tensor_copy(v2_w[0][:], tab2_w[0][:].indirect(list2[:]))
+        deal(w4_sd[:], w4_s[:].rearrange("p a n -> p (a n)"), 16)
+
         w1_b = [held.tile([P, N * PACK], BF16, name=f"w1_b{g}", align_bytes=64) for g in range(PASSES)]
         w1_q = [held.tile([P, N], U32, name=f"w1_q{g}", align_bytes=64) for g in range(PASSES)]
         w1_s = [held.tile([P, N], U8, name=f"w1_s{g}", align_bytes=64) for g in range(PASSES)]
@@ -301,8 +315,6 @@ def tile_list_satellite_radiance_calibration_kernel(
                 weave(*units[step - 2])
             if step in (2, 3):
                 quant_w1(step - 2)
-            if step == 3:
-                deal(w4_sd[:], w4_s[:].rearrange("p a n -> p (a n)"), 16)
             if 0 <= step - 3 < len(units):
                 quantise(*units[step - 3])
             if 0 <= step - 4 < len(units) and units[step - 4][1] == PASSES - 1:

@@ -95,17 +95,18 @@ def tile_list_satellite_radiance_calibration_kernel(
                 )
 
         nc.sync.dma_start(list1[:], offs)
+        load_w4()
         nc.sync.dma_start(list2[:], offs2)
-        load_words(tab_w[0], tab_words, 0)
         for q in range(4):
             load_quadrant(tab_s, 0, tab_scales, q)
-        load_quadrant(tab2_s, 8, tab2_scales, 0)
+        load_words(tab_w[0], tab_words, 0)
+        rows = [(q, a) for q in range(4) for a in range(PASSES)]
+        for q, a in rows[:3]:
+            load_rows(tab2_s, 8, tab2_scales, q, a)
         load_words(tab_w[1], tab_words, 1)
-        for q in range(1, 4):
-            for a in range(PASSES):
-                load_rows(tab2_s, 8, tab2_scales, q, a)
+        for q, a in rows[3:]:
+            load_rows(tab2_s, 8, tab2_scales, q, a)
         load_words(tab2_w[0], tab2_words, 0)
-        load_w4()
         load_w4_scales()
         load_words(tab2_w[1], tab2_words, 1)
         for dst, src in ((lo_t, lo), (hi_t, hi), (gain_t, gain)):
@@ -133,12 +134,12 @@ def tile_list_satellite_radiance_calibration_kernel(
 
         w4_wd = held.tile([P, PASSES * 2 * N], U8, name="w4_wd", align_bytes=64)
         w4_sd = held.tile([P, PASSES * N], U8, name="w4_sd", align_bytes=64)
-        nc.vector.tensor_copy(dealt(v_w[0]), tab_w[0][:].indirect(list1[:]))
-        nc.vector.tensor_copy(v_sg[:], tab_s[:].indirect(list1[:]))
-        nc.vector.tensor_copy(dealt(v_w[1]), tab_w[1][:].indirect(list1[:]))
-        deal(v_s[:], v_sg[:], 16)
-        nc.vector.tensor_copy(v2_s[:], tab2_s[:].indirect(list2[:]))
         deal(w4_wd[:].bitcast(U16), w4_w[:].rearrange("p a b -> p (a b)").bitcast(U16), 8)
+        nc.vector.tensor_copy(v_sg[:], tab_s[:].indirect(list1[:]))
+        nc.vector.tensor_copy(dealt(v_w[0]), tab_w[0][:].indirect(list1[:]))
+        deal(v_s[:], v_sg[:], 16)
+        nc.vector.tensor_copy(dealt(v_w[1]), tab_w[1][:].indirect(list1[:]))
+        nc.vector.tensor_copy(v2_s[:], tab2_s[:].indirect(list2[:]))
         nc.vector.tensor_copy(v2_w[0][:], tab2_w[0][:].indirect(list2[:]))
         deal(w4_sd[:], w4_s[:].rearrange("p a n -> p (a n)"), 16)
 

@@ -36,8 +36,9 @@ def pieces(width, largest):
     return out
 
 
-VY = 3
+S_WEAVES = (3,)
 S_EVAC = ()
+V_WEAVES = ((1, 1),)
 
 
 def tile_list_satellite_radiance_calibration_kernel(
@@ -222,7 +223,10 @@ def tile_list_satellite_radiance_calibration_kernel(
             h2b = both[:, w * PACK :]
             c_view = clamped[c, g][:].rearrange("p t (b i) -> p b t i", i=2)
             h_view = scaled[c, g][:].rearrange("p t (b i) -> p b t i", i=2)
-            nc.scalar.copy(hb.rearrange("p (b i t) -> p b t i", i=2, t=PACK), h_view)
+            if (c, g) in V_WEAVES:
+                nc.vector.tensor_copy(hb.rearrange("p (b i t) -> p b t i", i=2, t=PACK), h_view)
+            else:
+                nc.scalar.copy(hb.rearrange("p (b i t) -> p b t i", i=2, t=PACK), h_view)
             nc.vector.tensor_tensor(h2b.rearrange("p (b i t) -> p b t i", i=2, t=PACK), h_view, c_view, ALU.mult)
             woven[c, g] = both
 
@@ -282,7 +286,7 @@ def tile_list_satellite_radiance_calibration_kernel(
                     passes(c, b, 0)
                 passes(c, b, 1)
                 acc = banks[c, b]
-                if c >= VY:
+                if c in S_WEAVES:
                     nc.scalar.copy(
                         yb[:, b * YB * PACK : (b + 1) * YB * PACK].rearrange("p (j t) -> p j t", t=PACK),
                         acc[:].rearrange("p t j -> p j t"),
@@ -294,7 +298,7 @@ def tile_list_satellite_radiance_calibration_kernel(
             j0, w = starts[c], CHUNKS[c]
             y32, yb = results[c]
             y_q = held.tile([P, w], U32, name=f"y_q{c}", align_bytes=64)
-            if c < VY:
+            if c not in S_WEAVES:
                 nc.vector.tensor_copy(
                     yb[:].rearrange("p (b i t) -> p b t i", i=2, t=PACK), y32[:].rearrange("p t (b i) -> p b t i", i=2)
                 )

@@ -19,26 +19,14 @@ ACT = mybir.ActivationFunctionType
 P = 128
 PACK = 4
 PASSES = 2
-HALF = 512
-CHUNKS = (256,256,256,128,128)
-YB = 128
-EARLY = 3
-
-
-def pieces(width, largest):
-    out, at = [], 0
-    while at < width:
-        size = largest
-        while size > width - at:
-            size = size // 2
-        out.append((at, size))
-        at = at + size
-    return out
-
-
-S_WEAVES = (3,)
-S_EVAC = ()
-V_WEAVES = ((1, 1),)
+PASS = P * PACK
+QUADRANTS = 4
+CHUNKS = (256, 256, 256, 128, 128)
+BLOCK = 128
+H_WEAVES_ON_VECTOR = ((1, 1),)
+Y_WEAVES_ON_SCALAR = (2, 3)
+CODE_STORES = ((0, 1), (2, 3), (4,))
+WEAVE_LAG, QUANTISE_LAG, SECOND_LAG = 2, 3, 4
 
 
 def tile_list_satellite_radiance_calibration_kernel(
@@ -72,54 +60,43 @@ def tile_list_satellite_radiance_calibration_kernel(
         def load_words(dst, words, a):
             nc.sync.dma_start(dst[:].bitcast(I32), words[a].rearrange("p t i -> p (t i)").bitcast(I32))
 
-        def load_quadrant(dst, row, scales, q):
-            nc.sync.dma_start(
-                dst[32 * q + row : 32 * q + row + 4 * PASSES, :].bitcast(I32),
-                scales[:, 4 * q : 4 * q + 4, :].bitcast(I32),
-            )
-
-        def load_rows(dst, row, scales, q, a):
-            at = 32 * q + row + 4 * a
-            nc.sync.dma_start(dst[at : at + 4, :].bitcast(I32), scales[a, 4 * q : 4 * q + 4, :].bitcast(I32))
-
-        def load_w1(g):
-            nc.sync.dma_start(w1_raw[g][:], w1[g * HALF : (g + 1) * HALF, :].rearrange("(p j) n -> p j n", j=PACK))
-
-        def load_w4():
-            nc.sync.dma_start(w4_w[:].bitcast(I32), w4_words.rearrange("a p b -> p a b").bitcast(I32))
-
-        def load_w4_scales():
-            for q in range(4):
-                nc.sync.dma_start(
-                    w4_s[32 * q : 32 * q + 4, :, :].bitcast(I32),
-                    w4_scales[:, 4 * q : 4 * q + 4, :].rearrange("a r n -> r a n").bitcast(I32),
-                )
+        def load_tab2_scale_rows(q, a):
+            row = 32 * q + 8 + 4 * a
+            nc.sync.dma_start(tab2_s[row : row + 4, :].bitcast(I32), tab2_scales[a, 4 * q : 4 * q + 4, :].bitcast(I32))
 
         nc.sync.dma_start(list1[:], offs)
-        load_w4()
+        nc.sync.dma_start(w4_w[:].bitcast(I32), w4_words.rearrange("a p b -> p a b").bitcast(I32))
         nc.sync.dma_start(list2[:], offs2)
-        for q in range(4):
-            load_quadrant(tab_s, 0, tab_scales, q)
+        for q in range(QUADRANTS):
+            nc.sync.dma_start(
+                tab_s[32 * q : 32 * q + 4 * PASSES, :].bitcast(I32), tab_scales[:, 4 * q : 4 * q + 4, :].bitcast(I32)
+            )
         load_words(tab_w[0], tab_words, 0)
-        rows = [(q, a) for q in range(4) for a in range(PASSES)]
-        for q, a in rows[:3]:
-            load_rows(tab2_s, 8, tab2_scales, q, a)
+        row_groups = [(q, a) for q in range(QUADRANTS) for a in range(PASSES)]
+        for q, a in row_groups[:3]:
+            load_tab2_scale_rows(q, a)
         load_words(tab_w[1], tab_words, 1)
-        for q, a in rows[3:]:
-            load_rows(tab2_s, 8, tab2_scales, q, a)
+        for q, a in row_groups[3:]:
+            load_tab2_scale_rows(q, a)
         load_words(tab2_w[0], tab2_words, 0)
-        load_w4_scales()
+        for q in range(QUADRANTS):
+            nc.sync.dma_start(
+                w4_s[32 * q : 32 * q + 4, :, :].bitcast(I32),
+                w4_scales[:, 4 * q : 4 * q + 4, :].rearrange("a r n -> r a n").bitcast(I32),
+            )
         load_words(tab2_w[1], tab2_words, 1)
         for dst, src in ((lo_t, lo), (hi_t, hi), (gain_t, gain)):
             nc.sync.dma_start(dst[:], src.rearrange("(g p t) -> p g t", g=PASSES, t=PACK))
-        load_w1(0)
-        load_w1(1)
+        for g in range(PASSES):
+            nc.sync.dma_start(w1_raw[g][:], w1[g * PASS : (g + 1) * PASS, :].rearrange("(p j) n -> p j n", j=PACK))
 
         v_sg = held.tile([P, S], U8, name="v_sg", align_bytes=64)
         v_s = held.tile([P, S], U8, name="v_s", align_bytes=64)
         v_w = [held.tile([P, S], U32, name=f"v_w{a}", align_bytes=64) for a in range(PASSES)]
         v2_s = held.tile([P, S2], U8, name="v2_s", align_bytes=64)
         v2_w = [held.tile([P, S2], U32, name=f"v2_w{a}", align_bytes=64) for a in range(PASSES)]
+        w4_wd = held.tile([P, PASSES * 2 * N], U8, name="w4_wd", align_bytes=64)
+        w4_sd = held.tile([P, PASSES * N], U8, name="w4_sd", align_bytes=64)
 
         def deal(dst, src, run):
             nc.vector.tensor_copy(
@@ -127,32 +104,32 @@ def tile_list_satellite_radiance_calibration_kernel(
                 src.rearrange("p (g b i t) -> p g b t i", g=PASSES, t=PACK, i=run),
             )
 
-        def dealt(tile):
-            return tile[:].rearrange("p (g t m) -> p g m t", g=PASSES, t=PACK)
+        def gather_v_words(a):
+            dealt = v_w[a][:].rearrange("p (g t m) -> p g m t", g=PASSES, t=PACK)
+            nc.vector.tensor_copy(dealt, tab_w[a][:].indirect(list1[:]))
 
-        def half_list(h):
-            return list2[:, h * (HALF // 16) : (h + 1) * (HALF // 16)]
+        def gather_last_pass(half):
+            width = S2 // 2
+            nc.vector.tensor_copy(
+                v2_w[1][:, half * width : (half + 1) * width],
+                tab2_w[1][:].indirect(list2[:, half * width // 16 : (half + 1) * width // 16]),
+            )
 
-        w4_wd = held.tile([P, PASSES * 2 * N], U8, name="w4_wd", align_bytes=64)
-        w4_sd = held.tile([P, PASSES * N], U8, name="w4_sd", align_bytes=64)
         deal(w4_wd[:].bitcast(U16), w4_w[:].rearrange("p a b -> p (a b)").bitcast(U16), 8)
         nc.vector.tensor_copy(v_sg[:], tab_s[:].indirect(list1[:]))
-        nc.vector.tensor_copy(dealt(v_w[0]), tab_w[0][:].indirect(list1[:]))
+        gather_v_words(0)
         deal(v_s[:], v_sg[:], 16)
-        nc.vector.tensor_copy(dealt(v_w[1]), tab_w[1][:].indirect(list1[:]))
+        gather_v_words(1)
         nc.vector.tensor_copy(v2_s[:], tab2_s[:].indirect(list2[:]))
         nc.vector.tensor_copy(v2_w[0][:], tab2_w[0][:].indirect(list2[:]))
         deal(w4_sd[:], w4_s[:].rearrange("p a n -> p (a n)"), 16)
+        gather_last_pass(0)
 
         w1_b = [held.tile([P, N * PACK], BF16, name=f"w1_b{g}", align_bytes=64) for g in range(PASSES)]
         w1_q = [held.tile([P, N], U32, name=f"w1_q{g}", align_bytes=64) for g in range(PASSES)]
         w1_s = [held.tile([P, N], U8, name=f"w1_s{g}", align_bytes=64) for g in range(PASSES)]
+        y_q = held.tile([P, S2], U32, name="y_q", align_bytes=64)
         y_s = held.tile([P, S2], U8, name="y_s", align_bytes=64)
-
-        nc.vector.tensor_copy(v2_w[1][:, 0 * HALF : 1 * HALF], tab2_w[1][:].indirect(half_list(0)))
-
-        def late_head():
-            nc.vector.tensor_copy(v2_w[1][:, 1 * HALF : 2 * HALF], tab2_w[1][:].indirect(half_list(1)))
 
         def round_w1(g):
             dst = w1_b[g][:].rearrange("p (u e m j) -> p u m j e", u=2, e=2, j=PACK)
@@ -160,177 +137,161 @@ def tile_list_satellite_radiance_calibration_kernel(
             for u in range(2):
                 nc.scalar.copy(dst[:, u], src[:, u])
 
-        def quant_w1(g):
+        def quantise_w1(g):
             nc.vector.quantize_mx(w1_q[g][:].bitcast(FP8X4), w1_s[g][:], w1_b[g][:])
 
+        def woven(ap):
+            return ap.rearrange("p (b i t) -> p b t i", i=2, t=PACK)
+
+        def in_pairs(ap):
+            return ap.rearrange("p t (b i) -> p b t i", i=2)
+
+        last = len(CHUNKS) - 1
         starts = [sum(CHUNKS[:c]) for c in range(len(CHUNKS))]
         units = [(c, g) for c in range(len(CHUNKS)) for g in range(PASSES)]
-        clamped = {}
-        staged = {}
-        scaled = {}
-        woven = {}
+        signals = {}
+        rounded = {}
         quantised = {}
+        banks = {}
         results = {}
 
         def first_product(c, g):
-            j0, w = starts[c], CHUNKS[c]
-            c32 = work.tile([P, PACK, w], F32, name="c32", align_bytes=64, bufs=4)
-            h32 = work.tile([P, PACK, w], F32, name="h32", align_bytes=64, bufs=4)
-            js = slice(j0, j0 + w)
-            per_bank = 1
-            if 2 * c + g in S_EVAC:
-                per_bank = HALF // w
-                a32 = work.tile([P, PACK, w], F32, name="a32", align_bytes=64, bufs=4)
-                staged[c, g] = a32
-            for t0 in range(0, PACK, per_bank):
-                acc = psum_a.tile([P, per_bank, w], F32, name="acc")
-                for t in range(t0, t0 + per_bank):
-                    cols = slice(g * HALF + t * P, g * HALF + (t + 1) * P)
-                    for a in range(PASSES):
-                        nc.tensor.matmul_mx(
-                            acc[:, t - t0, :],
-                            lhsT=v_w[a][:, cols].bitcast(FP8X4),
-                            lhsT_scale=v_s[4 * a : P, cols],
-                            rhs=v2_w[a][:, js].bitcast(FP8X4),
-                            rhs_scale=v2_s[8 + 4 * a : P, js],
-                            start=(a == 0),
-                            stop=(a == PASSES - 1),
-                        )
-                if 2 * c + g in S_EVAC:
-                    nc.scalar.copy(a32[:, t0 : t0 + per_bank, :], acc[:])
-                else:
-                    for t in range(t0, t0 + per_bank):
-                        nc.vector.tensor_scalar(
-                            c32[:, t, :], acc[:, t - t0, :], lo_t[:, g, t : t + 1], hi_t[:, g, t : t + 1], ALU.max, ALU.min
-                        )
-                        nc.scalar.activation(h32[:, t, :], c32[:, t, :], ACT.Copy, scale=gain_t[:, g, t : t + 1])
-            clamped[c, g] = c32
-            scaled[c, g] = h32
-
-        def clamp(c, g):
-            if 2 * c + g in S_EVAC:
-                a32, c32, h32 = staged[c, g], clamped[c, g], scaled[c, g]
-                for t in range(PACK):
-                    nc.vector.tensor_scalar(
-                        c32[:, t, :], a32[:, t, :], lo_t[:, g, t : t + 1], hi_t[:, g, t : t + 1], ALU.max, ALU.min
+            w = CHUNKS[c]
+            js = slice(starts[c], starts[c] + w)
+            c32 = work.tile([P, PACK, w], F32, name="c32", align_bytes=64)
+            h32 = work.tile([P, PACK, w], F32, name="h32", align_bytes=64)
+            for t in range(PACK):
+                acc = psum_a.tile([P, w], F32, name="acc")
+                cols = slice(g * PASS + t * P, g * PASS + (t + 1) * P)
+                for a in range(PASSES):
+                    nc.tensor.matmul_mx(
+                        acc[:],
+                        lhsT=v_w[a][:, cols].bitcast(FP8X4),
+                        lhsT_scale=v_s[4 * a : P, cols],
+                        rhs=v2_w[a][:, js].bitcast(FP8X4),
+                        rhs_scale=v2_s[8 + 4 * a : P, js],
+                        start=(a == 0),
+                        stop=(a == PASSES - 1),
                     )
-                    nc.scalar.activation(h32[:, t, :], c32[:, t, :], ACT.Copy, scale=gain_t[:, g, t : t + 1])
+                nc.vector.tensor_scalar(
+                    c32[:, t, :], acc[:], lo_t[:, g, t : t + 1], hi_t[:, g, t : t + 1], ALU.max, ALU.min
+                )
+                nc.scalar.activation(h32[:, t, :], c32[:, t, :], ACT.Copy, scale=gain_t[:, g, t : t + 1])
+            signals[c, g] = (c32, h32)
 
         def weave(c, g):
             w = CHUNKS[c]
+            c32, h32 = signals[c, g]
             both = work.tile([P, 2 * w * PACK], BF16, name="both", align_bytes=64)
-            hb = both[:, : w * PACK]
-            h2b = both[:, w * PACK :]
-            c_view = clamped[c, g][:].rearrange("p t (b i) -> p b t i", i=2)
-            h_view = scaled[c, g][:].rearrange("p t (b i) -> p b t i", i=2)
-            if (c, g) in V_WEAVES:
-                nc.vector.tensor_copy(hb.rearrange("p (b i t) -> p b t i", i=2, t=PACK), h_view)
+            if (c, g) in H_WEAVES_ON_VECTOR:
+                nc.vector.tensor_copy(woven(both[:, : w * PACK]), in_pairs(h32[:]))
             else:
-                nc.scalar.copy(hb.rearrange("p (b i t) -> p b t i", i=2, t=PACK), h_view)
-            nc.vector.tensor_tensor(h2b.rearrange("p (b i t) -> p b t i", i=2, t=PACK), h_view, c_view, ALU.mult)
-            woven[c, g] = both
-
-        def quantise_all(codes, scales, s0, src, words):
-            for at, size in pieces(words, 1024):
-                nc.vector.quantize_mx(
-                    codes[:, at : at + size].bitcast(FP8X4),
-                    scales[:, s0 + at : s0 + at + size],
-                    src[:, at * PACK : (at + size) * PACK],
-                )
+                nc.scalar.copy(woven(both[:, : w * PACK]), in_pairs(h32[:]))
+            nc.vector.tensor_tensor(woven(both[:, w * PACK :]), in_pairs(h32[:]), in_pairs(c32[:]), ALU.mult)
+            rounded[c, g] = both
 
         def quantise(c, g):
             w = CHUNKS[c]
-            codes = work.tile([P, 2 * w], U32, name="h_q", align_bytes=64, bufs=4)
-            scales = work.tile([P, 2 * w], U8, name="h_s", align_bytes=64, bufs=4)
-            quantise_all(codes, scales, 0, woven[c, g], 2 * w)
-            quantised[c, g] = [(codes[:, :w], scales[:, :w]), (codes[:, w:], scales[:, w:])]
+            codes = work.tile([P, 2 * w], U32, name="h_q", align_bytes=64)
+            scales = work.tile([P, 2 * w], U8, name="h_s", align_bytes=64)
+            nc.vector.quantize_mx(codes[:].bitcast(FP8X4), scales[:], rounded[c, g][:])
+            quantised[c, g] = (codes, scales)
 
-        banks = {}
+        def bank_slices(c):
+            if c == last:
+                return [(0, (0, 1)), (0, (2, 3))]
+            return [(b, (0, 1, 2, 3)) for b in range(CHUNKS[c] // BLOCK)]
 
-        def passes(c, b, g):
-            js = slice(b * YB, (b + 1) * YB)
+        def second_passes(c, bank, g):
+            w = CHUNKS[c]
+            b, slices = bank_slices(c)[bank]
             if g == 0:
-                banks[c, b] = psum_y.tile([P, PACK, YB], F32, name="acc_y")
-            acc = banks[c, b]
-            for t in range(PACK):
-                codes, scales = quantised[c, g][0]
+                if c == last:
+                    banks[c, bank] = psum_a.tile([P, len(slices), BLOCK], F32, name="acc")
+                else:
+                    banks[c, bank] = psum_y.tile([P, len(slices), BLOCK], F32, name="acc_y")
+            acc = banks[c, bank]
+            codes, scales = quantised[c, g]
+            h_cols = slice(b * BLOCK, (b + 1) * BLOCK)
+            h2_cols = slice(w + b * BLOCK, w + (b + 1) * BLOCK)
+            for s, t in enumerate(slices):
                 nc.tensor.matmul_mx(
-                    acc[:, t, :],
+                    acc[:, s, :],
                     lhsT=w1_q[g][:, t * P : (t + 1) * P].bitcast(FP8X4),
                     lhsT_scale=w1_s[g][:, t * P : (t + 1) * P],
-                    rhs=codes[:, js].bitcast(FP8X4),
-                    rhs_scale=scales[:, js],
-                    start=(g == 0 and t == 0),
+                    rhs=codes[:, h_cols].bitcast(FP8X4),
+                    rhs_scale=scales[:, h_cols],
+                    start=(g == 0 and s == 0),
                     stop=False,
                 )
-                codes, scales = quantised[c, g][1]
                 n0 = g * N + t * P
                 nc.tensor.matmul_mx(
-                    acc[:, t, :],
+                    acc[:, s, :],
                     lhsT=w4_wd[:, 2 * n0 : 2 * (n0 + P)].bitcast(FP4X4),
                     lhsT_scale=w4_sd[:, n0 : n0 + P],
-                    rhs=codes[:, js].bitcast(FP8X4),
-                    rhs_scale=scales[:, js],
+                    rhs=codes[:, h2_cols].bitcast(FP8X4),
+                    rhs_scale=scales[:, h2_cols],
                     start=False,
-                    stop=(g == PASSES - 1 and t == PACK - 1),
+                    stop=(g == PASSES - 1 and s == len(slices) - 1),
                 )
 
-        def second_product(c):
-            j0, w = starts[c], CHUNKS[c]
+        out_rows = out_0.rearrange("(p t) j -> p t j", t=PACK)
+
+        def second_product(c, g):
+            w = CHUNKS[c]
+            narrow = w == BLOCK
+            if g == 0:
+                if narrow:
+                    for bank in range(len(bank_slices(c))):
+                        second_passes(c, bank, 0)
+                return
             y32 = held.tile([P, PACK, w], F32, name=f"y32_{c}", align_bytes=64)
-            yb = held.tile([P, w * PACK], BF16, name=f"yb_{c}", align_bytes=64)
-            results[c] = (y32, yb)
-            for b in range(w // YB):
-                js = slice(b * YB, (b + 1) * YB)
-                if c < EARLY:
-                    passes(c, b, 0)
-                passes(c, b, 1)
-                acc = banks[c, b]
-                if c in S_WEAVES:
-                    nc.scalar.copy(
-                        yb[:, b * YB * PACK : (b + 1) * YB * PACK].rearrange("p (j t) -> p j t", t=PACK),
-                        acc[:].rearrange("p t j -> p j t"),
-                    )
-                nc.scalar.copy(y32[:, :, js], acc[:])
-            nc.sync.dma_start(out_0.rearrange("(p t) j -> p t j", t=PACK)[:, :, j0 : j0 + w], y32[:])
+            results[c] = y32
+            for bank, (b, slices) in enumerate(bank_slices(c)):
+                if not narrow:
+                    second_passes(c, bank, 0)
+                second_passes(c, bank, 1)
+                dst = y32[:, slices[0] : slices[-1] + 1, b * BLOCK : (b + 1) * BLOCK]
+                if c == last and bank == 1:
+                    nc.vector.tensor_copy(dst, banks[c, bank][:])
+                else:
+                    nc.scalar.copy(dst, banks[c, bank][:])
+            nc.sync.dma_start(out_rows[:, :, starts[c] : starts[c] + w], y32[:])
 
         def planes(c):
-            j0, w = starts[c], CHUNKS[c]
-            y32, yb = results[c]
-            y_q = held.tile([P, w], U32, name=f"y_q{c}", align_bytes=64)
-            if c not in S_WEAVES:
-                nc.vector.tensor_copy(
-                    yb[:].rearrange("p (b i t) -> p b t i", i=2, t=PACK), y32[:].rearrange("p t (b i) -> p b t i", i=2)
-                )
-            quantise_all(y_q, y_s, j0, yb, w)
-            nc.sync.dma_start(
-                out_1[0].rearrange("p m t -> p (m t)").bitcast(I32)[:, j0 : j0 + w], y_q[:].bitcast(I32)
-            )
+            w = CHUNKS[c]
+            js = slice(starts[c], starts[c] + w)
+            yb = held.tile([P, w * PACK], BF16, name=f"yb_{c}", align_bytes=64)
+            if c in Y_WEAVES_ON_SCALAR:
+                nc.scalar.copy(woven(yb[:]), in_pairs(results[c][:]))
+            else:
+                nc.vector.tensor_copy(woven(yb[:]), in_pairs(results[c][:]))
+            nc.vector.quantize_mx(y_q[:, js].bitcast(FP8X4), y_s[:, js], yb[:])
 
-        for step in range(len(units) + 5):
+        for step in range(len(units) + SECOND_LAG):
             if step < len(units):
                 first_product(*units[step])
             if step == 0:
-                late_head()
+                gather_last_pass(1)
             if step in (1, 2):
                 round_w1(step - 1)
-            if 0 <= step - 1 < len(units):
-                clamp(*units[step - 1])
-            if 0 <= step - 2 < len(units):
-                weave(*units[step - 2])
+            if 0 <= step - WEAVE_LAG < len(units):
+                weave(*units[step - WEAVE_LAG])
             if step in (2, 3):
-                quant_w1(step - 2)
-            if 0 <= step - 3 < len(units):
-                quantise(*units[step - 3])
-            if 0 <= step - 4 < len(units) and units[step - 4][1] == PASSES - 1:
-                second_product(units[step - 4][0])
-            if 0 <= step - 4 < len(units) and units[step - 4][1] == 0 and units[step - 4][0] >= EARLY:
-                for b in range(CHUNKS[units[step - 4][0]] // YB):
-                    passes(units[step - 4][0], b, 0)
+                quantise_w1(step - 2)
+            if 0 <= step - QUANTISE_LAG < len(units):
+                quantise(*units[step - QUANTISE_LAG])
+            if step >= SECOND_LAG:
+                second_product(*units[step - SECOND_LAG])
 
-        for c in range(len(CHUNKS)):
-            planes(c)
+        out_words = out_1[0].rearrange("p m t -> p (m t)").bitcast(I32)
+        for group in CODE_STORES:
+            for c in group:
+                planes(c)
+            js = slice(starts[group[0]], starts[group[-1]] + CHUNKS[group[-1]])
+            queue = nc.scalar if last in group else nc.sync
+            queue.dma_start(out_words[:, js], y_q[:, js].bitcast(I32))
 
-        for q in range(4):
+        for q in range(QUADRANTS):
             queue = nc.sync if q % 2 == 0 else nc.scalar
             queue.dma_start(out_2[0, 4 * q : 4 * q + 4, :].bitcast(I32), y_s[32 * q : 32 * q + 4, :].bitcast(I32))

@@ -26,7 +26,7 @@ BLOCK = 128
 H_WEAVES_ON_VECTOR = ((1, 1),)
 Y_WEAVES_ON_SCALAR = (2, 3)
 CODE_STORES = ((0, 1), (2, 3), (4,))
-WEAVE_LAG, QUANTISE_LAG, SECOND_LAG = 2, 3, 4
+WEAVE_LAG, QUANTISE_LAG, SECOND_LAG = 3, 4, 5
 
 
 def tile_list_satellite_radiance_calibration_kernel(
@@ -36,7 +36,7 @@ def tile_list_satellite_radiance_calibration_kernel(
     nc = tc.nc
     with ExitStack() as ctx:
         held = ctx.enter_context(tc.tile_pool(name="held", bufs=1))
-        work = ctx.enter_context(tc.tile_pool(name="work", bufs=4))
+        work = ctx.enter_context(tc.tile_pool(name="work", bufs=5))
         psum_a = ctx.enter_context(tc.psum_pool(name="psum_a", bufs=6))
         psum_y = ctx.enter_context(tc.psum_pool(name="psum_y", bufs=2))
 
@@ -198,22 +198,22 @@ def tile_list_satellite_radiance_calibration_kernel(
             quantised[c, g] = (codes, scales)
 
         def bank_slices(c):
-            if c == last:
-                return [(0, (0, 1)), (0, (2, 3))]
-            return [(b, (0, 1, 2, 3)) for b in range(CHUNKS[c] // BLOCK)]
+            if c == last or CHUNKS[c] > BLOCK:
+                return [(0, 1), (2, 3)]
+            return [(0, 1, 2, 3)]
 
         def second_passes(c, bank, g):
             w = CHUNKS[c]
-            b, slices = bank_slices(c)[bank]
+            slices = bank_slices(c)[bank]
             if g == 0:
                 if c == last:
-                    banks[c, bank] = psum_a.tile([P, len(slices), BLOCK], F32, name="acc")
+                    banks[c, bank] = psum_a.tile([P, len(slices), w], F32, name="acc")
                 else:
-                    banks[c, bank] = psum_y.tile([P, len(slices), BLOCK], F32, name="acc_y")
+                    banks[c, bank] = psum_y.tile([P, len(slices), w], F32, name="acc_y")
             acc = banks[c, bank]
             codes, scales = quantised[c, g]
-            h_cols = slice(b * BLOCK, (b + 1) * BLOCK)
-            h2_cols = slice(w + b * BLOCK, w + (b + 1) * BLOCK)
+            h_cols = slice(0, w)
+            h2_cols = slice(w, 2 * w)
             for s, t in enumerate(slices):
                 nc.tensor.matmul_mx(
                     acc[:, s, :],
@@ -247,11 +247,11 @@ def tile_list_satellite_radiance_calibration_kernel(
                 return
             y32 = held.tile([P, PACK, w], F32, name=f"y32_{c}", align_bytes=64)
             results[c] = y32
-            for bank, (b, slices) in enumerate(bank_slices(c)):
+            for bank, slices in enumerate(bank_slices(c)):
                 if not narrow:
                     second_passes(c, bank, 0)
                 second_passes(c, bank, 1)
-                dst = y32[:, slices[0] : slices[-1] + 1, b * BLOCK : (b + 1) * BLOCK]
+                dst = y32[:, slices[0] : slices[-1] + 1, :]
                 if c == last and bank == 1:
                     nc.vector.tensor_copy(dst, banks[c, bank][:])
                 else:

@@ -23,8 +23,9 @@ PASS = P * PACK
 QUADRANTS = 4
 CHUNKS = (256, 256, 256, 128, 128)
 BLOCK = 128
+SPANS = ((0,), (1,), (2,), (3, 4))
 H_WEAVES_ON_VECTOR = ((1, 1),)
-Y_WEAVES_ON_SCALAR = (2, 3)
+Y_WEAVES_ON_SCALAR = (3,)
 CODE_STORES = ((0, 1), (2, 3), (4,))
 WEAVE_LAG, QUANTISE_LAG, SECOND_LAG = 3, 4, 5
 
@@ -37,8 +38,8 @@ def tile_list_satellite_radiance_calibration_kernel(
     with ExitStack() as ctx:
         held = ctx.enter_context(tc.tile_pool(name="held", bufs=1))
         work = ctx.enter_context(tc.tile_pool(name="work", bufs=5))
-        psum_a = ctx.enter_context(tc.psum_pool(name="psum_a", bufs=6))
-        psum_y = ctx.enter_context(tc.psum_pool(name="psum_y", bufs=2))
+        psum_a = ctx.enter_context(tc.psum_pool(name="psum_a", bufs=5))
+        psum_y = ctx.enter_context(tc.psum_pool(name="psum_y", bufs=3))
 
         list1 = held.tile([P, S // 16], U16, name="list1")
         list2 = held.tile([P, S2 // 16], U16, name="list2")
@@ -85,7 +86,7 @@ def tile_list_satellite_radiance_calibration_kernel(
                 w4_scales[:, 4 * q : 4 * q + 4, :].rearrange("a r n -> r a n").bitcast(I32),
             )
         load_words(tab2_w[1], tab2_words, 1)
-        for dst, src in ((lo_t, lo), (hi_t, hi), (gain_t, gain)):
+        for dst, src in ((gain_t, gain), (lo_t, lo), (hi_t, hi)):
             nc.sync.dma_start(dst[:], src.rearrange("(g p t) -> p g t", g=PASSES, t=PACK))
         for g in range(PASSES):
             nc.sync.dma_start(w1_raw[g][:], w1[g * PASS : (g + 1) * PASS, :].rearrange("(p j) n -> p j n", j=PACK))
@@ -148,18 +149,20 @@ def tile_list_satellite_radiance_calibration_kernel(
 
         last = len(CHUNKS) - 1
         starts = [sum(CHUNKS[:c]) for c in range(len(CHUNKS))]
-        units = [(c, g) for c in range(len(CHUNKS)) for g in range(PASSES)]
+        units = [(c, g) for span in SPANS for g in range(PASSES) for c in span]
+        leads = {span[0]: span for span in SPANS}
         signals = {}
         rounded = {}
         quantised = {}
         banks = {}
         results = {}
 
-        def first_product(c, g):
-            w = CHUNKS[c]
-            js = slice(starts[c], starts[c] + w)
-            c32 = work.tile([P, PACK, w], F32, name="c32", align_bytes=64)
-            h32 = work.tile([P, PACK, w], F32, name="h32", align_bytes=64)
+        def first_product(span, g):
+            w = sum(CHUNKS[c] for c in span)
+            j0 = starts[span[0]]
+            js = slice(j0, j0 + w)
+            c32 = work.tile([P, PACK, w], F32, name="c32", align_bytes=64, bufs=5)
+            h32 = work.tile([P, PACK, w], F32, name="h32", align_bytes=64, bufs=5)
             for t in range(PACK):
                 acc = psum_a.tile([P, w], F32, name="acc")
                 cols = slice(g * PASS + t * P, g * PASS + (t + 1) * P)
@@ -177,17 +180,19 @@ def tile_list_satellite_radiance_calibration_kernel(
                     c32[:, t, :], acc[:], lo_t[:, g, t : t + 1], hi_t[:, g, t : t + 1], ALU.max, ALU.min
                 )
                 nc.scalar.activation(h32[:, t, :], c32[:, t, :], ACT.Copy, scale=gain_t[:, g, t : t + 1])
-            signals[c, g] = (c32, h32)
+            for c in span:
+                part = slice(starts[c] - j0, starts[c] - j0 + CHUNKS[c])
+                signals[c, g] = (c32[:, :, part], h32[:, :, part])
 
         def weave(c, g):
             w = CHUNKS[c]
             c32, h32 = signals[c, g]
             both = work.tile([P, 2 * w * PACK], BF16, name="both", align_bytes=64)
             if (c, g) in H_WEAVES_ON_VECTOR:
-                nc.vector.tensor_copy(woven(both[:, : w * PACK]), in_pairs(h32[:]))
+                nc.vector.tensor_copy(woven(both[:, : w * PACK]), in_pairs(h32))
             else:
-                nc.scalar.copy(woven(both[:, : w * PACK]), in_pairs(h32[:]))
-            nc.vector.tensor_tensor(woven(both[:, w * PACK :]), in_pairs(h32[:]), in_pairs(c32[:]), ALU.mult)
+                nc.scalar.copy(woven(both[:, : w * PACK]), in_pairs(h32))
+            nc.vector.tensor_tensor(woven(both[:, w * PACK :]), in_pairs(h32), in_pairs(c32), ALU.mult)
             rounded[c, g] = both
 
         def quantise(c, g):
@@ -269,8 +274,8 @@ def tile_list_satellite_radiance_calibration_kernel(
             nc.vector.quantize_mx(y_q[:, js].bitcast(FP8X4), y_s[:, js], yb[:])
 
         for step in range(len(units) + SECOND_LAG):
-            if step < len(units):
-                first_product(*units[step])
+            if step < len(units) and units[step][0] in leads:
+                first_product(leads[units[step][0]], units[step][1])
             if step == 0:
                 gather_last_pass(1)
             if step in (1, 2):

@@ -94,6 +94,7 @@ def tile_list_satellite_radiance_calibration_kernel(
         v_sg = held.tile([P, S], U8, name="v_sg", align_bytes=64)
         v_s = held.tile([P, S], U8, name="v_s", align_bytes=64)
         v_w = [held.tile([P, S], U32, name=f"v_w{a}", align_bytes=64) for a in range(PASSES)]
+        v_wg = [held.tile([P, S], U32, name=f"v_wg{a}", align_bytes=64) for a in range(PASSES)]
         v2_s = held.tile([P, S2], U8, name="v2_s", align_bytes=64)
         v2_w = [held.tile([P, S2], U32, name=f"v2_w{a}", align_bytes=64) for a in range(PASSES)]
         w4_wd = held.tile([P, PASSES * 2 * N], U8, name="w4_wd", align_bytes=64)
@@ -106,8 +107,7 @@ def tile_list_satellite_radiance_calibration_kernel(
             )
 
         def gather_v_words(a):
-            dealt = v_w[a][:].rearrange("p (g t m) -> p g m t", g=PASSES, t=PACK)
-            nc.vector.tensor_copy(dealt, tab_w[a][:].indirect(list1[:]))
+            nc.vector.tensor_copy(v_wg[a][:], tab_w[a][:].indirect(list1[:]))
 
         def gather_last_pass(half):
             width = S2 // 2
@@ -121,7 +121,9 @@ def tile_list_satellite_radiance_calibration_kernel(
         gather_v_words(0)
         deal(v_s[:], v_sg[:], 16)
         gather_v_words(1)
+        deal(v_w[0][:], v_wg[0][:], 4)
         nc.vector.tensor_copy(v2_s[:], tab2_s[:].indirect(list2[:]))
+        deal(v_w[1][:], v_wg[1][:], 4)
         nc.vector.tensor_copy(v2_w[0][:], tab2_w[0][:].indirect(list2[:]))
         deal(w4_sd[:], w4_s[:].rearrange("p a n -> p (a n)"), 16)
         gather_last_pass(0)

@@ -21,13 +21,13 @@ PACK = 4
 PASSES = 2
 PASS = P * PACK
 QUADRANTS = 4
+BANK = 512
+HALVES = S2 // BANK
 CHUNKS = (256, 256, 256, 128, 128)
-BLOCK = 128
-SPANS = ((0,), (1,), (2,), (3, 4))
-H_WEAVES_ON_VECTOR = ((1, 1),)
-Y_WEAVES_ON_SCALAR = (3,)
+GPSIMD_SLICES = (4, 4, 2, 1)
+Y_WEAVES_ON_SCALAR = (0, 1, 2)
+EARLY_SUMS = 2
 CODE_STORES = ((0, 1), (2, 3), (4,))
-WEAVE_LAG, QUANTISE_LAG, SECOND_LAG = 3, 4, 5
 
 
 def tile_list_satellite_radiance_calibration_kernel(
@@ -37,18 +37,17 @@ def tile_list_satellite_radiance_calibration_kernel(
     nc = tc.nc
     with ExitStack() as ctx:
         held = ctx.enter_context(tc.tile_pool(name="held", bufs=1))
-        work = ctx.enter_context(tc.tile_pool(name="work", bufs=5))
-        psum_a = ctx.enter_context(tc.psum_pool(name="psum_a", bufs=5))
-        psum_y = ctx.enter_context(tc.psum_pool(name="psum_y", bufs=3))
+        work = ctx.enter_context(tc.tile_pool(name="work", bufs=6))
+        psum = ctx.enter_context(tc.psum_pool(name="psum", bufs=8))
 
         list1 = held.tile([P, S // 16], U16, name="list1")
         list2 = held.tile([P, S2 // 16], U16, name="list2")
         tab_s = held.tile([P, T], U8, name="tab_s", align_bytes=64)
         tab2_s = held.tile([P, T2], U8, name="tab2_s", align_bytes=64)
         w4_s = held.tile([P, PASSES, N], U8, name="w4_s", align_bytes=64)
-        tab_w = [held.tile([P, T], U32, name=f"tab_w{a}", align_bytes=64) for a in range(PASSES)]
+        tab_w = [held.tile([P, T], U32, name=f"tab_w{a}", tag=f"page{a}", align_bytes=64) for a in range(PASSES)]
         tab2_w = [held.tile([P, T2], U32, name=f"tab2_w{a}", align_bytes=64) for a in range(PASSES)]
-        w1_raw = [held.tile([P, PACK, N], F32, name=f"w1_raw{g}", align_bytes=64) for g in range(PASSES)]
+        w1_raw = [held.tile([P, PACK, N], F32, name=f"w1_raw{g}", tag=f"raw{g}", align_bytes=64) for g in range(PASSES)]
         w4_w = held.tile([P, PASSES, 2 * N], U8, name="w4_w", align_bytes=64)
         lo_t = held.tile([P, PASSES, PACK], F32, name="lo_t")
         hi_t = held.tile([P, PASSES, PACK], F32, name="hi_t")
@@ -65,8 +64,11 @@ def tile_list_satellite_radiance_calibration_kernel(
             row = 32 * q + 8 + 4 * a
             nc.sync.dma_start(tab2_s[row : row + 4, :].bitcast(I32), tab2_scales[a, 4 * q : 4 * q + 4, :].bitcast(I32))
 
+        def load_by_mode(dst, src):
+            nc.sync.dma_start(dst[:], src.rearrange("(g p t) -> p g t", g=PASSES, t=PACK))
+
         nc.sync.dma_start(list1[:], offs)
-        nc.sync.dma_start(w4_w[:].bitcast(I32), w4_words.rearrange("a p b -> p a b").bitcast(I32))
+        load_by_mode(gain_t, gain)
         nc.sync.dma_start(list2[:], offs2)
         for q in range(QUADRANTS):
             nc.sync.dma_start(
@@ -86,10 +88,11 @@ def tile_list_satellite_radiance_calibration_kernel(
                 w4_scales[:, 4 * q : 4 * q + 4, :].rearrange("a r n -> r a n").bitcast(I32),
             )
         load_words(tab2_w[1], tab2_words, 1)
-        for dst, src in ((gain_t, gain), (lo_t, lo), (hi_t, hi)):
-            nc.sync.dma_start(dst[:], src.rearrange("(g p t) -> p g t", g=PASSES, t=PACK))
+        load_by_mode(lo_t, lo)
+        load_by_mode(hi_t, hi)
         for g in range(PASSES):
             nc.sync.dma_start(w1_raw[g][:], w1[g * PASS : (g + 1) * PASS, :].rearrange("(p j) n -> p j n", j=PACK))
+        nc.sync.dma_start(w4_w[:].bitcast(I32), w4_words.rearrange("a p b -> p a b").bitcast(I32))
 
         v_sg = held.tile([P, S], U8, name="v_sg", align_bytes=64)
         v_s = held.tile([P, S], U8, name="v_s", align_bytes=64)
@@ -100,8 +103,8 @@ def tile_list_satellite_radiance_calibration_kernel(
         w4_wd = held.tile([P, PASSES * 2 * N], U8, name="w4_wd", align_bytes=64)
         w4_sd = held.tile([P, PASSES * N], U8, name="w4_sd", align_bytes=64)
 
-        def deal(dst, src, run):
-            nc.vector.tensor_copy(
+        def deal(copy, dst, src, run):
+            copy(
                 dst.rearrange("p (g t b i) -> p g b t i", g=PASSES, t=PACK, i=run),
                 src.rearrange("p (g b i t) -> p g b t i", g=PASSES, t=PACK, i=run),
             )
@@ -109,29 +112,24 @@ def tile_list_satellite_radiance_calibration_kernel(
         def gather_v_words(a):
             nc.vector.tensor_copy(v_wg[a][:], tab_w[a][:].indirect(list1[:]))
 
-        def gather_last_pass(half):
-            width = S2 // 2
-            nc.vector.tensor_copy(
-                v2_w[1][:, half * width : (half + 1) * width],
-                tab2_w[1][:].indirect(list2[:, half * width // 16 : (half + 1) * width // 16]),
-            )
-
-        deal(w4_wd[:].bitcast(U16), w4_w[:].rearrange("p a b -> p (a b)").bitcast(U16), 8)
         nc.vector.tensor_copy(v_sg[:], tab_s[:].indirect(list1[:]))
         gather_v_words(0)
-        deal(v_s[:], v_sg[:], 16)
+        deal(nc.vector.tensor_copy, v_s[:], v_sg[:], 16)
         gather_v_words(1)
-        deal(v_w[0][:], v_wg[0][:], 4)
+        deal(nc.vector.tensor_copy, v_w[0][:], v_wg[0][:], 4)
         nc.vector.tensor_copy(v2_s[:], tab2_s[:].indirect(list2[:]))
-        deal(v_w[1][:], v_wg[1][:], 4)
+        deal(nc.vector.tensor_copy, v_w[1][:], v_wg[1][:], 4)
         nc.vector.tensor_copy(v2_w[0][:], tab2_w[0][:].indirect(list2[:]))
-        deal(w4_sd[:], w4_s[:].rearrange("p a n -> p (a n)"), 16)
-        gather_last_pass(0)
+        deal(nc.vector.tensor_copy, w4_sd[:], w4_s[:].rearrange("p a n -> p (a n)"), 16)
+        for half in range(HALVES):
+            nc.vector.tensor_copy(
+                v2_w[1][:, half * BANK : (half + 1) * BANK],
+                tab2_w[1][:].indirect(list2[:, half * BANK // 16 : (half + 1) * BANK // 16]),
+            )
 
         w1_b = [held.tile([P, N * PACK], BF16, name=f"w1_b{g}", align_bytes=64) for g in range(PASSES)]
         w1_q = [held.tile([P, N], U32, name=f"w1_q{g}", align_bytes=64) for g in range(PASSES)]
         w1_s = [held.tile([P, N], U8, name=f"w1_s{g}", align_bytes=64) for g in range(PASSES)]
-        y_q = held.tile([P, S2], U32, name="y_q", align_bytes=64)
         y_s = held.tile([P, S2], U8, name="y_s", align_bytes=64)
 
         def round_w1(g):
@@ -151,113 +149,116 @@ def tile_list_satellite_radiance_calibration_kernel(
 
         last = len(CHUNKS) - 1
         starts = [sum(CHUNKS[:c]) for c in range(len(CHUNKS))]
-        units = [(c, g) for span in SPANS for g in range(PASSES) for c in span]
-        leads = {span[0]: span for span in SPANS}
-        signals = {}
+        pieces = [(c, g) for c in range(len(CHUNKS)) for g in range(PASSES)]
+        fields = [(half, g) for half in range(HALVES) for g in range(PASSES)]
+        c32 = {}
+        h32 = {}
+        for f, field in enumerate(fields):
+            reuse = f == len(fields) - 1
+            c32[field] = held.tile([P, PACK, BANK], F32, name=f"c32_{f}", tag="page0" if reuse else f"c{f}", align_bytes=64)
+            h32[field] = held.tile([P, PACK, BANK], F32, name=f"h32_{f}", tag="page1" if reuse else f"h{f}", align_bytes=64)
+        y_q = held.tile([P, S2], U32, name="y_q", tag="page1", align_bytes=64)
+        sums = {}
+        woven_field = {}
         rounded = {}
         quantised = {}
         banks = {}
         results = {}
+        rounded_y = {}
 
-        def first_product(span, g):
-            w = sum(CHUNKS[c] for c in span)
-            j0 = starts[span[0]]
-            js = slice(j0, j0 + w)
-            c32 = work.tile([P, PACK, w], F32, name="c32", align_bytes=64, bufs=5)
-            h32 = work.tile([P, PACK, w], F32, name="h32", align_bytes=64, bufs=5)
-            for t in range(PACK):
-                acc = psum_a.tile([P, w], F32, name="acc")
-                cols = slice(g * PASS + t * P, g * PASS + (t + 1) * P)
-                for a in range(PASSES):
-                    nc.tensor.matmul_mx(
-                        acc[:],
-                        lhsT=v_w[a][:, cols].bitcast(FP8X4),
-                        lhsT_scale=v_s[4 * a : P, cols],
-                        rhs=v2_w[a][:, js].bitcast(FP8X4),
-                        rhs_scale=v2_s[8 + 4 * a : P, js],
-                        start=(a == 0),
-                        stop=(a == PASSES - 1),
-                    )
-                nc.vector.tensor_scalar(
-                    c32[:, t, :], acc[:], lo_t[:, g, t : t + 1], hi_t[:, g, t : t + 1], ALU.max, ALU.min
-                )
-                nc.scalar.activation(h32[:, t, :], c32[:, t, :], ACT.Copy, scale=gain_t[:, g, t : t + 1])
-            for c in span:
-                part = slice(starts[c] - j0, starts[c] - j0 + CHUNKS[c])
-                signals[c, g] = (c32[:, :, part], h32[:, :, part])
+        def first_pass(half, g, t, a, opens):
+            if opens:
+                sums[half, g, t] = psum.tile([P, BANK], F32, name="acc")
+            cols = slice(g * PASS + t * P, g * PASS + (t + 1) * P)
+            js = slice(half * BANK, (half + 1) * BANK)
+            nc.tensor.matmul_mx(
+                sums[half, g, t][:],
+                lhsT=v_w[a][:, cols].bitcast(FP8X4),
+                lhsT_scale=v_s[4 * a : P, cols],
+                rhs=v2_w[a][:, js].bitcast(FP8X4),
+                rhs_scale=v2_s[8 + 4 * a : P, js],
+                start=opens,
+                stop=not opens,
+            )
 
-        def weave(c, g):
-            w = CHUNKS[c]
-            c32, h32 = signals[c, g]
-            both = work.tile([P, 2 * w * PACK], BF16, name="both", align_bytes=64)
-            if (c, g) in H_WEAVES_ON_VECTOR:
-                nc.vector.tensor_copy(woven(both[:, : w * PACK]), in_pairs(h32))
+        def clamp_and_gain(f, t):
+            half, g = fields[f]
+            c_row = c32[half, g][:, t, :]
+            h_row = h32[half, g][:, t, :]
+            nc.vector.tensor_scalar(
+                c_row, sums[half, g, t][:], lo_t[:, g, t : t + 1], hi_t[:, g, t : t + 1], ALU.max, ALU.min
+            )
+            if t < GPSIMD_SLICES[f]:
+                nc.gpsimd.tensor_scalar(h_row, c_row, gain_t[:, g, t : t + 1], 0.0, ALU.mult, ALU.add)
             else:
-                nc.scalar.copy(woven(both[:, : w * PACK]), in_pairs(h32))
-            nc.vector.tensor_tensor(woven(both[:, w * PACK :]), in_pairs(h32), in_pairs(c32), ALU.mult)
-            rounded[c, g] = both
+                nc.scalar.activation(h_row, c_row, ACT.Copy, scale=gain_t[:, g, t : t + 1])
+
+        def signal(tiles, c, g):
+            j0 = starts[c] % BANK
+            return in_pairs(tiles[starts[c] // BANK, g][:, :, j0 : j0 + CHUNKS[c]])
+
+        def weave_h(c, g):
+            w = CHUNKS[c]
+            half, j0 = divmod(starts[c], BANK)
+            if j0 == 0:
+                tag = f"raw{1 - g}" if half == 0 else f"late{g}"
+                woven_field[half, g] = held.tile([P, 2 * BANK * PACK], BF16, name=f"both{half}{g}", tag=tag, align_bytes=64)
+            rounded[c, g] = woven_field[half, g][:, 2 * PACK * j0 : 2 * PACK * (j0 + w)]
+            nc.scalar.copy(woven(rounded[c, g][:, : w * PACK]), signal(h32, c, g))
+
+        def weave_h2(c, g):
+            w = CHUNKS[c]
+            nc.vector.tensor_tensor(
+                woven(rounded[c, g][:, w * PACK :]), signal(h32, c, g), signal(c32, c, g), ALU.mult
+            )
 
         def quantise(c, g):
             w = CHUNKS[c]
-            codes = work.tile([P, 2 * w], U32, name="h_q", align_bytes=64)
-            scales = work.tile([P, 2 * w], U8, name="h_s", align_bytes=64)
-            nc.vector.quantize_mx(codes[:].bitcast(FP8X4), scales[:], rounded[c, g][:])
+            codes = work.tile([P, 2 * w], U32, name="h_q", align_bytes=64, bufs=4)
+            scales = work.tile([P, 2 * w], U8, name="h_s", align_bytes=64, bufs=4)
+            nc.vector.quantize_mx(codes[:].bitcast(FP8X4), scales[:], rounded[c, g])
             quantised[c, g] = (codes, scales)
 
         def bank_slices(c):
-            if c == last or CHUNKS[c] > BLOCK:
+            if c == last or CHUNKS[c] * PACK > BANK:
                 return [(0, 1), (2, 3)]
             return [(0, 1, 2, 3)]
 
-        def second_passes(c, bank, g):
+        def second_passes(c, g):
             w = CHUNKS[c]
-            slices = bank_slices(c)[bank]
-            if g == 0:
-                if c == last:
-                    banks[c, bank] = psum_a.tile([P, len(slices), w], F32, name="acc")
-                else:
-                    banks[c, bank] = psum_y.tile([P, len(slices), w], F32, name="acc_y")
-            acc = banks[c, bank]
             codes, scales = quantised[c, g]
-            h_cols = slice(0, w)
-            h2_cols = slice(w, 2 * w)
-            for s, t in enumerate(slices):
-                nc.tensor.matmul_mx(
-                    acc[:, s, :],
-                    lhsT=w1_q[g][:, t * P : (t + 1) * P].bitcast(FP8X4),
-                    lhsT_scale=w1_s[g][:, t * P : (t + 1) * P],
-                    rhs=codes[:, h_cols].bitcast(FP8X4),
-                    rhs_scale=scales[:, h_cols],
-                    start=(g == 0 and s == 0),
-                    stop=False,
-                )
-                n0 = g * N + t * P
-                nc.tensor.matmul_mx(
-                    acc[:, s, :],
-                    lhsT=w4_wd[:, 2 * n0 : 2 * (n0 + P)].bitcast(FP4X4),
-                    lhsT_scale=w4_sd[:, n0 : n0 + P],
-                    rhs=codes[:, h2_cols].bitcast(FP8X4),
-                    rhs_scale=scales[:, h2_cols],
-                    start=False,
-                    stop=(g == PASSES - 1 and s == len(slices) - 1),
-                )
+            for bank, slices in enumerate(bank_slices(c)):
+                if g == 0:
+                    banks[c, bank] = psum.tile([P, len(slices), w], F32, name="acc")
+                acc = banks[c, bank]
+                for s, t in enumerate(slices):
+                    nc.tensor.matmul_mx(
+                        acc[:, s, :],
+                        lhsT=w1_q[g][:, t * P : (t + 1) * P].bitcast(FP8X4),
+                        lhsT_scale=w1_s[g][:, t * P : (t + 1) * P],
+                        rhs=codes[:, :w].bitcast(FP8X4),
+                        rhs_scale=scales[:, :w],
+                        start=(g == 0 and s == 0),
+                        stop=False,
+                    )
+                    n0 = g * N + t * P
+                    nc.tensor.matmul_mx(
+                        acc[:, s, :],
+                        lhsT=w4_wd[:, 2 * n0 : 2 * (n0 + P)].bitcast(FP4X4),
+                        lhsT_scale=w4_sd[:, n0 : n0 + P],
+                        rhs=codes[:, w:].bitcast(FP8X4),
+                        rhs_scale=scales[:, w:],
+                        start=False,
+                        stop=(g == PASSES - 1 and s == len(slices) - 1),
+                    )
 
         out_rows = out_0.rearrange("(p t) j -> p t j", t=PACK)
 
-        def second_product(c, g):
+        def hand_out(c):
             w = CHUNKS[c]
-            narrow = w == BLOCK
-            if g == 0:
-                if narrow:
-                    for bank in range(len(bank_slices(c))):
-                        second_passes(c, bank, 0)
-                return
             y32 = held.tile([P, PACK, w], F32, name=f"y32_{c}", align_bytes=64)
             results[c] = y32
             for bank, slices in enumerate(bank_slices(c)):
-                if not narrow:
-                    second_passes(c, bank, 0)
-                second_passes(c, bank, 1)
                 dst = y32[:, slices[0] : slices[-1] + 1, :]
                 if c == last and bank == 1:
                     nc.vector.tensor_copy(dst, banks[c, bank][:])
@@ -265,36 +266,56 @@ def tile_list_satellite_radiance_calibration_kernel(
                     nc.scalar.copy(dst, banks[c, bank][:])
             nc.sync.dma_start(out_rows[:, :, starts[c] : starts[c] + w], y32[:])
 
-        def planes(c):
-            w = CHUNKS[c]
-            js = slice(starts[c], starts[c] + w)
-            yb = held.tile([P, w * PACK], BF16, name=f"yb_{c}", align_bytes=64)
+        def weave_y(c):
+            rounded_y[c] = held.tile([P, CHUNKS[c] * PACK], BF16, name=f"yb_{c}", align_bytes=64)
             if c in Y_WEAVES_ON_SCALAR:
-                nc.scalar.copy(woven(yb[:]), in_pairs(results[c][:]))
+                nc.scalar.copy(woven(rounded_y[c][:]), in_pairs(results[c][:]))
             else:
-                nc.vector.tensor_copy(woven(yb[:]), in_pairs(results[c][:]))
-            nc.vector.quantize_mx(y_q[:, js].bitcast(FP8X4), y_s[:, js], yb[:])
+                nc.vector.tensor_copy(woven(rounded_y[c][:]), in_pairs(results[c][:]))
 
-        for step in range(len(units) + SECOND_LAG):
-            if step < len(units) and units[step][0] in leads:
-                first_product(leads[units[step][0]], units[step][1])
-            if step == 0:
-                gather_last_pass(1)
-            if step in (1, 2):
-                round_w1(step - 1)
-            if 0 <= step - WEAVE_LAG < len(units):
-                weave(*units[step - WEAVE_LAG])
-            if step in (2, 3):
-                quantise_w1(step - 2)
-            if 0 <= step - QUANTISE_LAG < len(units):
-                quantise(*units[step - QUANTISE_LAG])
-            if step >= SECOND_LAG:
-                second_product(*units[step - SECOND_LAG])
+        def quantise_y(c):
+            js = slice(starts[c], starts[c] + CHUNKS[c])
+            nc.vector.quantize_mx(y_q[:, js].bitcast(FP8X4), y_s[:, js], rounded_y[c][:])
+
+        for t in range(EARLY_SUMS):
+            first_pass(0, 0, t, 0, True)
+        for f, (half, g) in enumerate(fields):
+            if f < PASSES:
+                round_w1(f)
+            if f == PASSES:
+                deal(nc.scalar.copy, w4_wd[:].bitcast(U16), w4_w[:].rearrange("p a b -> p (a b)").bitcast(U16), 8)
+                weave_h(0, 0)
+                weave_h(0, 1)
+            for t in range(PACK):
+                if f == 0 and t < EARLY_SUMS:
+                    first_pass(half, g, t, 1, False)
+                else:
+                    first_pass(half, g, t, 1, True)
+                    first_pass(half, g, t, 0, False)
+                clamp_and_gain(f, t)
+
+        for piece in pieces[PASSES:]:
+            weave_h(*piece)
+        for step in range(len(pieces) + 1):
+            if step < len(pieces):
+                weave_h2(*pieces[step])
+            if step < PASSES:
+                quantise_w1(step)
+            if step >= 1:
+                c, g = pieces[step - 1]
+                quantise(c, g)
+                second_passes(c, g)
+                if g == PASSES - 1:
+                    hand_out(c)
+                    if c >= 1 and c - 1 in Y_WEAVES_ON_SCALAR:
+                        weave_y(c - 1)
 
         out_words = out_1[0].rearrange("p m t -> p (m t)").bitcast(I32)
         for group in CODE_STORES:
             for c in group:
-                planes(c)
+                if c not in Y_WEAVES_ON_SCALAR:
+                    weave_y(c)
+                quantise_y(c)
             js = slice(starts[group[0]], starts[group[-1]] + CHUNKS[group[-1]])
             queue = nc.scalar if last in group else nc.sync
             queue.dma_start(out_words[:, js], y_q[:, js].bitcast(I32))

@@ -24,7 +24,7 @@ QUADRANTS = 4
 BANK = 512
 HALVES = S2 // BANK
 CHUNKS = (256, 256, 256, 128, 128)
-GPSIMD_SLICES = (4, 4, 2, 1)
+GPSIMD_SLICES = (4, 0, 3, 3)
 Y_WEAVES_ON_SCALAR = (0, 1, 2)
 EARLY_SUMS = 2
 CODE_STORES = ((0, 1), (2, 3), (4,))
@@ -46,7 +46,7 @@ def tile_list_satellite_radiance_calibration_kernel(
         tab2_s = held.tile([P, T2], U8, name="tab2_s", align_bytes=64)
         w4_s = held.tile([P, PASSES, N], U8, name="w4_s", align_bytes=64)
         tab_w = [held.tile([P, T], U32, name=f"tab_w{a}", tag=f"page{a}", align_bytes=64) for a in range(PASSES)]
-        tab2_w = [held.tile([P, T2], U32, name=f"tab2_w{a}", align_bytes=64) for a in range(PASSES)]
+        tab2_w = [held.tile([P, T2], U32, name=f"tab2_w{a}", tag=f"wide{a}", align_bytes=64) for a in range(PASSES)]
         w1_raw = [held.tile([P, PACK, N], F32, name=f"w1_raw{g}", tag=f"raw{g}", align_bytes=64) for g in range(PASSES)]
         w4_w = held.tile([P, PASSES, 2 * N], U8, name="w4_w", align_bytes=64)
         lo_t = held.tile([P, PASSES, PACK], F32, name="lo_t")
@@ -68,7 +68,7 @@ def tile_list_satellite_radiance_calibration_kernel(
             nc.sync.dma_start(dst[:], src.rearrange("(g p t) -> p g t", g=PASSES, t=PACK))
 
         nc.sync.dma_start(list1[:], offs)
-        load_by_mode(gain_t, gain)
+        nc.sync.dma_start(w4_w[:].bitcast(I32), w4_words.rearrange("a p b -> p a b").bitcast(I32))
         nc.sync.dma_start(list2[:], offs2)
         for q in range(QUADRANTS):
             nc.sync.dma_start(
@@ -88,11 +88,11 @@ def tile_list_satellite_radiance_calibration_kernel(
                 w4_scales[:, 4 * q : 4 * q + 4, :].rearrange("a r n -> r a n").bitcast(I32),
             )
         load_words(tab2_w[1], tab2_words, 1)
+        load_by_mode(gain_t, gain)
         load_by_mode(lo_t, lo)
         load_by_mode(hi_t, hi)
         for g in range(PASSES):
             nc.sync.dma_start(w1_raw[g][:], w1[g * PASS : (g + 1) * PASS, :].rearrange("(p j) n -> p j n", j=PACK))
-        nc.sync.dma_start(w4_w[:].bitcast(I32), w4_words.rearrange("a p b -> p a b").bitcast(I32))
 
         v_sg = held.tile([P, S], U8, name="v_sg", align_bytes=64)
         v_s = held.tile([P, S], U8, name="v_s", align_bytes=64)
@@ -112,6 +112,7 @@ def tile_list_satellite_radiance_calibration_kernel(
         def gather_v_words(a):
             nc.vector.tensor_copy(v_wg[a][:], tab_w[a][:].indirect(list1[:]))
 
+        deal(nc.vector.tensor_copy, w4_wd[:].bitcast(U16), w4_w[:].rearrange("p a b -> p (a b)").bitcast(U16), 8)
         nc.vector.tensor_copy(v_sg[:], tab_s[:].indirect(list1[:]))
         gather_v_words(0)
         deal(nc.vector.tensor_copy, v_s[:], v_sg[:], 16)
@@ -135,8 +136,7 @@ def tile_list_satellite_radiance_calibration_kernel(
         def round_w1(g):
             dst = w1_b[g][:].rearrange("p (u e m j) -> p u m j e", u=2, e=2, j=PACK)
             src = w1_raw[g][:].rearrange("p j (m u e) -> p u m j e", u=2, e=2)
-            for u in range(2):
-                nc.scalar.copy(dst[:, u], src[:, u])
+            nc.scalar.copy(dst, src)
 
         def quantise_w1(g):
             nc.vector.quantize_mx(w1_q[g][:].bitcast(FP8X4), w1_s[g][:], w1_b[g][:])
@@ -155,9 +155,12 @@ def tile_list_satellite_radiance_calibration_kernel(
         h32 = {}
         for f, field in enumerate(fields):
             reuse = f == len(fields) - 1
-            c32[field] = held.tile([P, PACK, BANK], F32, name=f"c32_{f}", tag="page0" if reuse else f"c{f}", align_bytes=64)
-            h32[field] = held.tile([P, PACK, BANK], F32, name=f"h32_{f}", tag="page1" if reuse else f"h{f}", align_bytes=64)
-        y_q = held.tile([P, S2], U32, name="y_q", tag="page1", align_bytes=64)
+            c32[field] = held.tile([P, PACK, BANK], F32, name=f"c32_{f}", tag="page0" if reuse else "wide1" if f == 0 else f"c{f}", align_bytes=64)
+            h32[field] = held.tile([P, PACK, BANK], F32, name=f"h32_{f}", tag="page1" if reuse else "raw1" if f == 1 else f"h{f}", align_bytes=64)
+        y_q = [
+            held.tile([P, BANK], U32, name=f"y_q{half}", tag="page1" if half else "y_q", align_bytes=64)
+            for half in range(HALVES)
+        ]
         sums = {}
         woven_field = {}
         rounded = {}
@@ -197,19 +200,32 @@ def tile_list_satellite_radiance_calibration_kernel(
             j0 = starts[c] % BANK
             return in_pairs(tiles[starts[c] // BANK, g][:, :, j0 : j0 + CHUNKS[c]])
 
-        def weave_h(c, g):
+        def place(c, g):
             w = CHUNKS[c]
             half, j0 = divmod(starts[c], BANK)
             if j0 == 0:
-                tag = f"raw{1 - g}" if half == 0 else f"late{g}"
+                tag = "raw0" if (half, g) == (0, 0) else f"woven{half}{g}"
                 woven_field[half, g] = held.tile([P, 2 * BANK * PACK], BF16, name=f"both{half}{g}", tag=tag, align_bytes=64)
             rounded[c, g] = woven_field[half, g][:, 2 * PACK * j0 : 2 * PACK * (j0 + w)]
+
+        def weave_h(c, g):
+            w = CHUNKS[c]
             nc.scalar.copy(woven(rounded[c, g][:, : w * PACK]), signal(h32, c, g))
 
         def weave_h2(c, g):
             w = CHUNKS[c]
             nc.vector.tensor_tensor(
                 woven(rounded[c, g][:, w * PACK :]), signal(h32, c, g), signal(c32, c, g), ALU.mult
+            )
+
+        def weave_h2_on_gpsimd(c, g):
+            w = CHUNKS[c]
+            half, j0 = divmod(starts[c], BANK)
+            nc.gpsimd.tensor_tensor(
+                rounded[c, g][:, w * PACK :].rearrange("p (j t) -> p j t", t=PACK),
+                h32[half, g][:, :, j0 : j0 + w].rearrange("p t j -> p j t"),
+                c32[half, g][:, :, j0 : j0 + w].rearrange("p t j -> p j t"),
+                ALU.mult,
             )
 
         def quantise(c, g):
@@ -275,15 +291,32 @@ def tile_list_satellite_radiance_calibration_kernel(
 
         def quantise_y(c):
             js = slice(starts[c], starts[c] + CHUNKS[c])
-            nc.vector.quantize_mx(y_q[:, js].bitcast(FP8X4), y_s[:, js], rounded_y[c][:])
+            half, j0 = divmod(starts[c], BANK)
+            nc.vector.quantize_mx(y_q[half][:, j0 : j0 + CHUNKS[c]].bitcast(FP8X4), y_s[:, js], rounded_y[c][:])
+
+        out_words = out_1[0].rearrange("p m t -> p (m t)").bitcast(I32)
+
+        def planes(group):
+            for c in group:
+                if c not in Y_WEAVES_ON_SCALAR:
+                    weave_y(c)
+                quantise_y(c)
+            js = slice(starts[group[0]], starts[group[-1]] + CHUNKS[group[-1]])
+            half = js.start // BANK
+            queue = nc.scalar if last in group else nc.sync
+            queue.dma_start(out_words[:, js], y_q[half][:, js.start - half * BANK : js.stop - half * BANK].bitcast(I32))
+
+        for piece in pieces:
+            place(*piece)
 
         for t in range(EARLY_SUMS):
             first_pass(0, 0, t, 0, True)
         for f, (half, g) in enumerate(fields):
             if f < PASSES:
                 round_w1(f)
+            if f == 1:
+                weave_h2_on_gpsimd(0, 0)
             if f == PASSES:
-                deal(nc.scalar.copy, w4_wd[:].bitcast(U16), w4_w[:].rearrange("p a b -> p (a b)").bitcast(U16), 8)
                 weave_h(0, 0)
                 weave_h(0, 1)
             for t in range(PACK):
@@ -294,10 +327,11 @@ def tile_list_satellite_radiance_calibration_kernel(
                     first_pass(half, g, t, 0, False)
                 clamp_and_gain(f, t)
 
-        for piece in pieces[PASSES:]:
+        wide = [piece for piece in pieces if CHUNKS[piece[0]] * PACK > BANK]
+        for piece in wide[PASSES:]:
             weave_h(*piece)
         for step in range(len(pieces) + 1):
-            if step < len(pieces):
+            if 0 < step < len(pieces):
                 weave_h2(*pieces[step])
             if step < PASSES:
                 quantise_w1(step)
@@ -307,18 +341,16 @@ def tile_list_satellite_radiance_calibration_kernel(
                 second_passes(c, g)
                 if g == PASSES - 1:
                     hand_out(c)
-                    if c >= 1 and c - 1 in Y_WEAVES_ON_SCALAR:
-                        weave_y(c - 1)
+                    if c == 0:
+                        for piece in pieces[len(wide) :]:
+                            weave_h(*piece)
+                    if c in Y_WEAVES_ON_SCALAR:
+                        weave_y(c)
+                    if c == CODE_STORES[0][-1] + 1:
+                        planes(CODE_STORES[0])
 
-        out_words = out_1[0].rearrange("p m t -> p (m t)").bitcast(I32)
-        for group in CODE_STORES:
-            for c in group:
-                if c not in Y_WEAVES_ON_SCALAR:
-                    weave_y(c)
-                quantise_y(c)
-            js = slice(starts[group[0]], starts[group[-1]] + CHUNKS[group[-1]])
-            queue = nc.scalar if last in group else nc.sync
-            queue.dma_start(out_words[:, js], y_q[:, js].bitcast(I32))
+        for group in CODE_STORES[1:]:
+            planes(group)
 
         for q in range(QUADRANTS):
             queue = nc.sync if q % 2 == 0 else nc.scalar

@@ -24,7 +24,7 @@ QUADRANTS = 4
 BANK = 512
 HALVES = S2 // BANK
 CHUNKS = (256, 256, 256, 128, 128)
-GPSIMD_SLICES = (4, 0, 3, 3)
+GPSIMD_SLICES = (4, 4, 2, 1)
 Y_WEAVES_ON_SCALAR = (0, 1, 2)
 EARLY_SUMS = 2
 CODE_STORES = ((0, 1), (2, 3), (4,))
@@ -156,7 +156,7 @@ def tile_list_satellite_radiance_calibration_kernel(
         for f, field in enumerate(fields):
             reuse = f == len(fields) - 1
             c32[field] = held.tile([P, PACK, BANK], F32, name=f"c32_{f}", tag="page0" if reuse else "wide1" if f == 0 else f"c{f}", align_bytes=64)
-            h32[field] = held.tile([P, PACK, BANK], F32, name=f"h32_{f}", tag="page1" if reuse else "raw1" if f == 1 else f"h{f}", align_bytes=64)
+            h32[field] = held.tile([P, PACK, BANK], F32, name=f"h32_{f}", tag="page1" if reuse else f"h{f}", align_bytes=64)
         y_q = [
             held.tile([P, BANK], U32, name=f"y_q{half}", tag="page1" if half else "y_q", align_bytes=64)
             for half in range(HALVES)
@@ -204,7 +204,7 @@ def tile_list_satellite_radiance_calibration_kernel(
             w = CHUNKS[c]
             half, j0 = divmod(starts[c], BANK)
             if j0 == 0:
-                tag = "raw0" if (half, g) == (0, 0) else f"woven{half}{g}"
+                tag = f"raw{1 - g}" if half == 0 else f"late{g}"
                 woven_field[half, g] = held.tile([P, 2 * BANK * PACK], BF16, name=f"both{half}{g}", tag=tag, align_bytes=64)
             rounded[c, g] = woven_field[half, g][:, 2 * PACK * j0 : 2 * PACK * (j0 + w)]
 
@@ -218,25 +218,21 @@ def tile_list_satellite_radiance_calibration_kernel(
                 woven(rounded[c, g][:, w * PACK :]), signal(h32, c, g), signal(c32, c, g), ALU.mult
             )
 
-        def weave_h2_on_gpsimd(c, g):
-            w = CHUNKS[c]
-            half, j0 = divmod(starts[c], BANK)
-            nc.gpsimd.tensor_tensor(
-                rounded[c, g][:, w * PACK :].rearrange("p (j t) -> p j t", t=PACK),
-                h32[half, g][:, :, j0 : j0 + w].rearrange("p t j -> p j t"),
-                c32[half, g][:, :, j0 : j0 + w].rearrange("p t j -> p j t"),
-                ALU.mult,
-            )
-
         def quantise(c, g):
             w = CHUNKS[c]
             codes = work.tile([P, 2 * w], U32, name="h_q", align_bytes=64, bufs=4)
             scales = work.tile([P, 2 * w], U8, name="h_s", align_bytes=64, bufs=4)
-            nc.vector.quantize_mx(codes[:].bitcast(FP8X4), scales[:], rounded[c, g])
+            if (c, g) == pieces[-1]:
+                for part in range(2):
+                    cols = slice(part * w, (part + 1) * w)
+                    source = rounded[c, g][:, part * w * PACK : (part + 1) * w * PACK]
+                    nc.vector.quantize_mx(codes[:, cols].bitcast(FP8X4), scales[:, cols], source)
+            else:
+                nc.vector.quantize_mx(codes[:].bitcast(FP8X4), scales[:], rounded[c, g])
             quantised[c, g] = (codes, scales)
 
         def bank_slices(c):
-            if c == last or CHUNKS[c] * PACK > BANK:
+            if CHUNKS[c] * PACK > BANK:
                 return [(0, 1), (2, 3)]
             return [(0, 1, 2, 3)]
 
@@ -246,10 +242,10 @@ def tile_list_satellite_radiance_calibration_kernel(
             for bank, slices in enumerate(bank_slices(c)):
                 if g == 0:
                     banks[c, bank] = psum.tile([P, len(slices), w], F32, name="acc")
-                acc = banks[c, bank]
+            for bank, slices in enumerate(bank_slices(c)):
                 for s, t in enumerate(slices):
                     nc.tensor.matmul_mx(
-                        acc[:, s, :],
+                        banks[c, bank][:, s, :],
                         lhsT=w1_q[g][:, t * P : (t + 1) * P].bitcast(FP8X4),
                         lhsT_scale=w1_s[g][:, t * P : (t + 1) * P],
                         rhs=codes[:, :w].bitcast(FP8X4),
@@ -257,9 +253,11 @@ def tile_list_satellite_radiance_calibration_kernel(
                         start=(g == 0 and s == 0),
                         stop=False,
                     )
+            for bank, slices in enumerate(bank_slices(c)):
+                for s, t in enumerate(slices):
                     n0 = g * N + t * P
                     nc.tensor.matmul_mx(
-                        acc[:, s, :],
+                        banks[c, bank][:, s, :],
                         lhsT=w4_wd[:, 2 * n0 : 2 * (n0 + P)].bitcast(FP4X4),
                         lhsT_scale=w4_sd[:, n0 : n0 + P],
                         rhs=codes[:, w:].bitcast(FP8X4),
@@ -276,7 +274,7 @@ def tile_list_satellite_radiance_calibration_kernel(
             results[c] = y32
             for bank, slices in enumerate(bank_slices(c)):
                 dst = y32[:, slices[0] : slices[-1] + 1, :]
-                if c == last and bank == 1:
+                if c == last:
                     nc.vector.tensor_copy(dst, banks[c, bank][:])
                 else:
                     nc.scalar.copy(dst, banks[c, bank][:])
@@ -314,8 +312,6 @@ def tile_list_satellite_radiance_calibration_kernel(
         for f, (half, g) in enumerate(fields):
             if f < PASSES:
                 round_w1(f)
-            if f == 1:
-                weave_h2_on_gpsimd(0, 0)
             if f == PASSES:
                 weave_h(0, 0)
                 weave_h(0, 1)
@@ -331,7 +327,7 @@ def tile_list_satellite_radiance_calibration_kernel(
         for piece in wide[PASSES:]:
             weave_h(*piece)
         for step in range(len(pieces) + 1):
-            if 0 < step < len(pieces):
+            if step < len(pieces):
                 weave_h2(*pieces[step])
             if step < PASSES:
                 quantise_w1(step)

@@ -25,9 +25,9 @@ BANK = 512
 HALVES = S2 // BANK
 CHUNKS = (256, 256, 256, 128, 128)
 GPSIMD_SLICES = (4, 4, 2, 1)
-Y_WEAVES_ON_SCALAR = (0, 1, 2)
+Y_WEAVES_ON_SCALAR = (0, 1, 3)
 EARLY_SUMS = 2
-CODE_STORES = ((0, 1), (2, 3), (4,))
+CODE_STORES = ((0,), (1,), (2, 3), (4,))
 
 
 def tile_list_satellite_radiance_calibration_kernel(
@@ -43,7 +43,7 @@ def tile_list_satellite_radiance_calibration_kernel(
         list1 = held.tile([P, S // 16], U16, name="list1")
         list2 = held.tile([P, S2 // 16], U16, name="list2")
         tab_s = held.tile([P, T], U8, name="tab_s", align_bytes=64)
-        tab2_s = held.tile([P, T2], U8, name="tab2_s", align_bytes=64)
+        tab2_s = held.tile([P, T2], U8, name="tab2_s", tag="relay", align_bytes=64)
         w4_s = held.tile([P, PASSES, N], U8, name="w4_s", align_bytes=64)
         tab_w = [held.tile([P, T], U32, name=f"tab_w{a}", tag=f"page{a}", align_bytes=64) for a in range(PASSES)]
         tab2_w = [held.tile([P, T2], U32, name=f"tab2_w{a}", tag=f"wide{a}", align_bytes=64) for a in range(PASSES)]
@@ -68,40 +68,39 @@ def tile_list_satellite_radiance_calibration_kernel(
             nc.sync.dma_start(dst[:], src.rearrange("(g p t) -> p g t", g=PASSES, t=PACK))
 
         nc.sync.dma_start(list1[:], offs)
-        nc.sync.dma_start(w4_w[:].bitcast(I32), w4_words.rearrange("a p b -> p a b").bitcast(I32))
+        load_words(tab_w[0], tab_words, 0)
         nc.sync.dma_start(list2[:], offs2)
         for q in range(QUADRANTS):
             nc.sync.dma_start(
                 tab_s[32 * q : 32 * q + 4 * PASSES, :].bitcast(I32), tab_scales[:, 4 * q : 4 * q + 4, :].bitcast(I32)
             )
-        load_words(tab_w[0], tab_words, 0)
-        row_groups = [(q, a) for q in range(QUADRANTS) for a in range(PASSES)]
-        for q, a in row_groups[:3]:
-            load_tab2_scale_rows(q, a)
         load_words(tab_w[1], tab_words, 1)
-        for q, a in row_groups[3:]:
+        row_groups = [(q, a) for q in range(QUADRANTS) for a in range(PASSES)]
+        for q, a in row_groups[:2]:
             load_tab2_scale_rows(q, a)
         load_words(tab2_w[0], tab2_words, 0)
-        for q in range(QUADRANTS):
-            nc.sync.dma_start(
-                w4_s[32 * q : 32 * q + 4, :, :].bitcast(I32),
-                w4_scales[:, 4 * q : 4 * q + 4, :].rearrange("a r n -> r a n").bitcast(I32),
-            )
+        for q, a in row_groups[2:]:
+            load_tab2_scale_rows(q, a)
         load_words(tab2_w[1], tab2_words, 1)
         load_by_mode(gain_t, gain)
         load_by_mode(lo_t, lo)
         load_by_mode(hi_t, hi)
         for g in range(PASSES):
             nc.sync.dma_start(w1_raw[g][:], w1[g * PASS : (g + 1) * PASS, :].rearrange("(p j) n -> p j n", j=PACK))
+        nc.sync.dma_start(w4_w[:].bitcast(I32), w4_words.rearrange("a p b -> p a b").bitcast(I32))
+        for q in range(QUADRANTS):
+            nc.sync.dma_start(
+                w4_s[32 * q : 32 * q + 4, :, :].bitcast(I32),
+                w4_scales[:, 4 * q : 4 * q + 4, :].rearrange("a r n -> r a n").bitcast(I32),
+            )
 
         v_sg = held.tile([P, S], U8, name="v_sg", align_bytes=64)
         v_s = held.tile([P, S], U8, name="v_s", align_bytes=64)
         v_w = [held.tile([P, S], U32, name=f"v_w{a}", align_bytes=64) for a in range(PASSES)]
-        v_wg = [held.tile([P, S], U32, name=f"v_wg{a}", align_bytes=64) for a in range(PASSES)]
         v2_s = held.tile([P, S2], U8, name="v2_s", align_bytes=64)
-        v2_w = [held.tile([P, S2], U32, name=f"v2_w{a}", align_bytes=64) for a in range(PASSES)]
+        v2_w = [held.tile([P, S2], U32, name=f"v2_w{a}", tag="relay" if a else "v2_w", align_bytes=64) for a in range(PASSES)]
         w4_wd = held.tile([P, PASSES * 2 * N], U8, name="w4_wd", align_bytes=64)
-        w4_sd = held.tile([P, PASSES * N], U8, name="w4_sd", align_bytes=64)
+        w4_sd = held.tile([P, PASSES * N], U8, name="w4_sd", tag="relay", align_bytes=64)
 
         def deal(copy, dst, src, run):
             copy(
@@ -110,18 +109,16 @@ def tile_list_satellite_radiance_calibration_kernel(
             )
 
         def gather_v_words(a):
-            nc.vector.tensor_copy(v_wg[a][:], tab_w[a][:].indirect(list1[:]))
+            nc.vector.tensor_copy(
+                v_w[a][:].rearrange("p (g t m) -> p g m t", g=PASSES, t=PACK), tab_w[a][:].indirect(list1[:])
+            )
 
-        deal(nc.vector.tensor_copy, w4_wd[:].bitcast(U16), w4_w[:].rearrange("p a b -> p (a b)").bitcast(U16), 8)
-        nc.vector.tensor_copy(v_sg[:], tab_s[:].indirect(list1[:]))
         gather_v_words(0)
-        deal(nc.vector.tensor_copy, v_s[:], v_sg[:], 16)
+        nc.vector.tensor_copy(v_sg[:], tab_s[:].indirect(list1[:]))
         gather_v_words(1)
-        deal(nc.vector.tensor_copy, v_w[0][:], v_wg[0][:], 4)
-        nc.vector.tensor_copy(v2_s[:], tab2_s[:].indirect(list2[:]))
-        deal(nc.vector.tensor_copy, v_w[1][:], v_wg[1][:], 4)
+        deal(nc.vector.tensor_copy, v_s[:], v_sg[:], 16)
         nc.vector.tensor_copy(v2_w[0][:], tab2_w[0][:].indirect(list2[:]))
-        deal(nc.vector.tensor_copy, w4_sd[:], w4_s[:].rearrange("p a n -> p (a n)"), 16)
+        nc.vector.tensor_copy(v2_s[:], tab2_s[:].indirect(list2[:]))
         for half in range(HALVES):
             nc.vector.tensor_copy(
                 v2_w[1][:, half * BANK : (half + 1) * BANK],
@@ -274,10 +271,7 @@ def tile_list_satellite_radiance_calibration_kernel(
             results[c] = y32
             for bank, slices in enumerate(bank_slices(c)):
                 dst = y32[:, slices[0] : slices[-1] + 1, :]
-                if c == last:
-                    nc.vector.tensor_copy(dst, banks[c, bank][:])
-                else:
-                    nc.scalar.copy(dst, banks[c, bank][:])
+                nc.scalar.copy(dst, banks[c, bank][:])
             nc.sync.dma_start(out_rows[:, :, starts[c] : starts[c] + w], y32[:])
 
         def weave_y(c):
@@ -313,6 +307,7 @@ def tile_list_satellite_radiance_calibration_kernel(
             if f < PASSES:
                 round_w1(f)
             if f == PASSES:
+                deal(nc.scalar.copy, w4_wd[:].bitcast(U16), w4_w[:].rearrange("p a b -> p (a b)").bitcast(U16), 8)
                 weave_h(0, 0)
                 weave_h(0, 1)
             for t in range(PACK):
@@ -323,6 +318,7 @@ def tile_list_satellite_radiance_calibration_kernel(
                     first_pass(half, g, t, 0, False)
                 clamp_and_gain(f, t)
 
+        deal(nc.vector.tensor_copy, w4_sd[:], w4_s[:].rearrange("p a n -> p (a n)"), 16)
         wide = [piece for piece in pieces if CHUNKS[piece[0]] * PACK > BANK]
         for piece in wide[PASSES:]:
             weave_h(*piece)
@@ -340,12 +336,14 @@ def tile_list_satellite_radiance_calibration_kernel(
                     if c == 0:
                         for piece in pieces[len(wide) :]:
                             weave_h(*piece)
-                    if c in Y_WEAVES_ON_SCALAR:
-                        weave_y(c)
-                    if c == CODE_STORES[0][-1] + 1:
+                    if c - 1 in Y_WEAVES_ON_SCALAR:
+                        weave_y(c - 1)
+                    if c == CODE_STORES[0][-1] + 2:
                         planes(CODE_STORES[0])
+                    if c == CODE_STORES[1][-1] + 2:
+                        planes(CODE_STORES[1])
 
-        for group in CODE_STORES[1:]:
+        for group in CODE_STORES[2:]:
             planes(group)
 
         for q in range(QUADRANTS):

@@ -139,10 +139,10 @@ def tile_list_satellite_radiance_calibration_kernel(
             nc.vector.quantize_mx(w1_q[g][:].bitcast(FP8X4), w1_s[g][:], w1_b[g][:])
 
         def woven(ap):
-            return ap.rearrange("p (b i t) -> p b t i", i=2, t=PACK)
+            return ap.rearrange("p (b i t) -> p b t i", i=4, t=PACK)
 
         def in_pairs(ap):
-            return ap.rearrange("p t (b i) -> p b t i", i=2)
+            return ap.rearrange("p t (b i) -> p b t i", i=4)
 
         last = len(CHUNKS) - 1
         starts = [sum(CHUNKS[:c]) for c in range(len(CHUNKS))]

@@ -23,11 +23,12 @@ PASS = P * PACK
 QUADRANTS = 4
 BANK = 512
 HALVES = S2 // BANK
-CHUNKS = (256, 256, 256, 128, 128)
-GPSIMD_SLICES = (4, 4, 2, 1)
-Y_WEAVES_ON_SCALAR = (0, 1, 3)
+CHUNKS = (256, 256, 128, 128, 128, 128)
+GPSIMD_SLICES = (3, 4, 3, 1)
+Y_WEAVES_ON_SCALAR = (0, 1, 2, 3, 4)
 EARLY_SUMS = 2
-CODE_STORES = ((0,), (1,), (2, 3), (4,))
+W1_PART = 256
+CODE_STORES = ((0, 1), (2, 3, 4), (5,))
 
 
 def tile_list_satellite_radiance_calibration_kernel(
@@ -47,7 +48,11 @@ def tile_list_satellite_radiance_calibration_kernel(
         w4_s = held.tile([P, PASSES, N], U8, name="w4_s", align_bytes=64)
         tab_w = [held.tile([P, T], U32, name=f"tab_w{a}", tag=f"page{a}", align_bytes=64) for a in range(PASSES)]
         tab2_w = [held.tile([P, T2], U32, name=f"tab2_w{a}", tag=f"wide{a}", align_bytes=64) for a in range(PASSES)]
-        w1_raw = [held.tile([P, PACK, N], F32, name=f"w1_raw{g}", tag=f"raw{g}", align_bytes=64) for g in range(PASSES)]
+        w1_parts = [(g, n0) for g in range(PASSES) for n0 in range(0, N, W1_PART)]
+        w1_raw = [
+            held.tile([P, PACK, W1_PART], F32, name=f"w1_raw{part}", tag=f"raw{part}", align_bytes=64)
+            for part in range(len(w1_parts))
+        ]
         w4_w = held.tile([P, PASSES, 2 * N], U8, name="w4_w", align_bytes=64)
         lo_t = held.tile([P, PASSES, PACK], F32, name="lo_t")
         hi_t = held.tile([P, PASSES, PACK], F32, name="hi_t")
@@ -85,9 +90,10 @@ def tile_list_satellite_radiance_calibration_kernel(
         load_by_mode(gain_t, gain)
         load_by_mode(lo_t, lo)
         load_by_mode(hi_t, hi)
-        for g in range(PASSES):
-            nc.sync.dma_start(w1_raw[g][:], w1[g * PASS : (g + 1) * PASS, :].rearrange("(p j) n -> p j n", j=PACK))
         nc.sync.dma_start(w4_w[:].bitcast(I32), w4_words.rearrange("a p b -> p a b").bitcast(I32))
+        for part, (g, n0) in enumerate(w1_parts):
+            rows = w1[g * PASS : (g + 1) * PASS, n0 : n0 + W1_PART]
+            nc.sync.dma_start(w1_raw[part][:], rows.rearrange("(p j) n -> p j n", j=PACK))
         for q in range(QUADRANTS):
             nc.sync.dma_start(
                 w4_s[32 * q : 32 * q + 4, :, :].bitcast(I32),
@@ -130,10 +136,11 @@ def tile_list_satellite_radiance_calibration_kernel(
         w1_s = [held.tile([P, N], U8, name=f"w1_s{g}", align_bytes=64) for g in range(PASSES)]
         y_s = held.tile([P, S2], U8, name="y_s", align_bytes=64)
 
-        def round_w1(g):
+        def round_w1(part):
+            g, n0 = w1_parts[part]
             dst = w1_b[g][:].rearrange("p (u e m j) -> p u m j e", u=2, e=2, j=PACK)
-            src = w1_raw[g][:].rearrange("p j (m u e) -> p u m j e", u=2, e=2)
-            nc.scalar.copy(dst, src)
+            src = w1_raw[part][:].rearrange("p j (m u e) -> p u m j e", u=2, e=2)
+            nc.scalar.copy(dst[:, :, n0 // PACK : (n0 + W1_PART) // PACK], src)
 
         def quantise_w1(g):
             nc.vector.quantize_mx(w1_q[g][:].bitcast(FP8X4), w1_s[g][:], w1_b[g][:])
@@ -155,7 +162,7 @@ def tile_list_satellite_radiance_calibration_kernel(
             c32[field] = held.tile([P, PACK, BANK], F32, name=f"c32_{f}", tag="page0" if reuse else "wide1" if f == 0 else f"c{f}", align_bytes=64)
             h32[field] = held.tile([P, PACK, BANK], F32, name=f"h32_{f}", tag="page1" if reuse else f"h{f}", align_bytes=64)
         y_q = [
-            held.tile([P, BANK], U32, name=f"y_q{half}", tag="page1" if half else "y_q", align_bytes=64)
+            held.tile([P, BANK], U32, name=f"y_q{half}", tag=f"page{half}", align_bytes=64)
             for half in range(HALVES)
         ]
         sums = {}
@@ -201,7 +208,7 @@ def tile_list_satellite_radiance_calibration_kernel(
             w = CHUNKS[c]
             half, j0 = divmod(starts[c], BANK)
             if j0 == 0:
-                tag = f"raw{1 - g}" if half == 0 else f"late{g}"
+                tag = f"raw{len(w1_parts) - 1 - g}" if half == 0 else f"late{g}"
                 woven_field[half, g] = held.tile([P, 2 * BANK * PACK], BF16, name=f"both{half}{g}", tag=tag, align_bytes=64)
             rounded[c, g] = woven_field[half, g][:, 2 * PACK * j0 : 2 * PACK * (j0 + w)]
 
@@ -301,13 +308,14 @@ def tile_list_satellite_radiance_calibration_kernel(
         for piece in pieces:
             place(*piece)
 
+        deal(nc.scalar.copy, w4_wd[:].bitcast(U16), w4_w[:].rearrange("p a b -> p (a b)").bitcast(U16), 8)
+        for part in range(len(w1_parts)):
+            round_w1(part)
+
         for t in range(EARLY_SUMS):
             first_pass(0, 0, t, 0, True)
         for f, (half, g) in enumerate(fields):
-            if f < PASSES:
-                round_w1(f)
             if f == PASSES:
-                deal(nc.scalar.copy, w4_wd[:].bitcast(U16), w4_w[:].rearrange("p a b -> p (a b)").bitcast(U16), 8)
                 weave_h(0, 0)
                 weave_h(0, 1)
             for t in range(PACK):
@@ -319,8 +327,7 @@ def tile_list_satellite_radiance_calibration_kernel(
                 clamp_and_gain(f, t)
 
         deal(nc.vector.tensor_copy, w4_sd[:], w4_s[:].rearrange("p a n -> p (a n)"), 16)
-        wide = [piece for piece in pieces if CHUNKS[piece[0]] * PACK > BANK]
-        for piece in wide[PASSES:]:
+        for piece in pieces[PASSES:]:
             weave_h(*piece)
         for step in range(len(pieces) + 1):
             if step < len(pieces):
@@ -333,17 +340,10 @@ def tile_list_satellite_radiance_calibration_kernel(
                 second_passes(c, g)
                 if g == PASSES - 1:
                     hand_out(c)
-                    if c == 0:
-                        for piece in pieces[len(wide) :]:
-                            weave_h(*piece)
-                    if c - 1 in Y_WEAVES_ON_SCALAR:
-                        weave_y(c - 1)
-                    if c == CODE_STORES[0][-1] + 2:
-                        planes(CODE_STORES[0])
-                    if c == CODE_STORES[1][-1] + 2:
-                        planes(CODE_STORES[1])
+                    if c in Y_WEAVES_ON_SCALAR:
+                        weave_y(c)
 
-        for group in CODE_STORES[2:]:
+        for group in CODE_STORES:
             planes(group)
 
         for q in range(QUADRANTS):

@@ -26,7 +26,7 @@ HALVES = S2 // BANK
 CHUNKS = (256, 256, 128, 128, 128, 128)
 GPSIMD_SLICES = (3, 4, 3, 1)
 Y_WEAVES_ON_SCALAR = (0, 1, 2, 3, 4)
-EARLY_SUMS = 2
+EARLY_SUMS = 4
 W1_PART = 256
 CODE_STORES = ((0, 1), (2, 3, 4), (5,))
 
@@ -44,7 +44,7 @@ def tile_list_satellite_radiance_calibration_kernel(
         list1 = held.tile([P, S // 16], U16, name="list1")
         list2 = held.tile([P, S2 // 16], U16, name="list2")
         tab_s = held.tile([P, T], U8, name="tab_s", align_bytes=64)
-        tab2_s = held.tile([P, T2], U8, name="tab2_s", tag="relay", align_bytes=64)
+        tab2_s = held.tile([P, T2], U8, name="tab2_s", align_bytes=64)
         w4_s = held.tile([P, PASSES, N], U8, name="w4_s", align_bytes=64)
         tab_w = [held.tile([P, T], U32, name=f"tab_w{a}", tag=f"page{a}", align_bytes=64) for a in range(PASSES)]
         tab2_w = [held.tile([P, T2], U32, name=f"tab2_w{a}", tag=f"wide{a}", align_bytes=64) for a in range(PASSES)]
@@ -58,7 +58,7 @@ def tile_list_satellite_radiance_calibration_kernel(
         hi_t = held.tile([P, PASSES, PACK], F32, name="hi_t")
         gain_t = held.tile([P, PASSES, PACK], F32, name="gain_t")
 
-        nc.vector.memset(tab_s[:].bitcast(I32), 0)
+        nc.gpsimd.memset(tab_s[:].bitcast(I32), 0)
         nc.vector.memset(tab2_s[:].bitcast(I32), 0)
         nc.vector.memset(w4_s[:].rearrange("p a n -> p (a n)").bitcast(I32), 0)
 
@@ -73,19 +73,24 @@ def tile_list_satellite_radiance_calibration_kernel(
             nc.sync.dma_start(dst[:], src.rearrange("(g p t) -> p g t", g=PASSES, t=PACK))
 
         nc.sync.dma_start(list1[:], offs)
-        load_words(tab_w[0], tab_words, 0)
         nc.sync.dma_start(list2[:], offs2)
         for q in range(QUADRANTS):
             nc.sync.dma_start(
                 tab_s[32 * q : 32 * q + 4 * PASSES, :].bitcast(I32), tab_scales[:, 4 * q : 4 * q + 4, :].bitcast(I32)
             )
-        load_words(tab_w[1], tab_words, 1)
+        load_words(tab_w[0], tab_words, 0)
         row_groups = [(q, a) for q in range(QUADRANTS) for a in range(PASSES)]
-        for q, a in row_groups[:2]:
+        for q, a in row_groups[:3]:
+            load_tab2_scale_rows(q, a)
+        load_words(tab_w[1], tab_words, 1)
+        for q, a in row_groups[3:]:
             load_tab2_scale_rows(q, a)
         load_words(tab2_w[0], tab2_words, 0)
-        for q, a in row_groups[2:]:
-            load_tab2_scale_rows(q, a)
+        for q in range(QUADRANTS):
+            nc.sync.dma_start(
+                w4_s[32 * q : 32 * q + 4, :, :].bitcast(I32),
+                w4_scales[:, 4 * q : 4 * q + 4, :].rearrange("a r n -> r a n").bitcast(I32),
+            )
         load_words(tab2_w[1], tab2_words, 1)
         load_by_mode(gain_t, gain)
         load_by_mode(lo_t, lo)
@@ -94,19 +99,14 @@ def tile_list_satellite_radiance_calibration_kernel(
         for part, (g, n0) in enumerate(w1_parts):
             rows = w1[g * PASS : (g + 1) * PASS, n0 : n0 + W1_PART]
             nc.sync.dma_start(w1_raw[part][:], rows.rearrange("(p j) n -> p j n", j=PACK))
-        for q in range(QUADRANTS):
-            nc.sync.dma_start(
-                w4_s[32 * q : 32 * q + 4, :, :].bitcast(I32),
-                w4_scales[:, 4 * q : 4 * q + 4, :].rearrange("a r n -> r a n").bitcast(I32),
-            )
 
         v_sg = held.tile([P, S], U8, name="v_sg", align_bytes=64)
         v_s = held.tile([P, S], U8, name="v_s", align_bytes=64)
         v_w = [held.tile([P, S], U32, name=f"v_w{a}", align_bytes=64) for a in range(PASSES)]
         v2_s = held.tile([P, S2], U8, name="v2_s", align_bytes=64)
-        v2_w = [held.tile([P, S2], U32, name=f"v2_w{a}", tag="relay" if a else "v2_w", align_bytes=64) for a in range(PASSES)]
+        v2_w = [held.tile([P, S2], U32, name=f"v2_w{a}", align_bytes=64) for a in range(PASSES)]
         w4_wd = held.tile([P, PASSES * 2 * N], U8, name="w4_wd", align_bytes=64)
-        w4_sd = held.tile([P, PASSES * N], U8, name="w4_sd", tag="relay", align_bytes=64)
+        w4_sd = held.tile([P, PASSES * N], U8, name="w4_sd", align_bytes=64)
 
         def deal(copy, dst, src, run):
             copy(
@@ -119,12 +119,13 @@ def tile_list_satellite_radiance_calibration_kernel(
                 v_w[a][:].rearrange("p (g t m) -> p g m t", g=PASSES, t=PACK), tab_w[a][:].indirect(list1[:])
             )
 
-        gather_v_words(0)
         nc.vector.tensor_copy(v_sg[:], tab_s[:].indirect(list1[:]))
-        gather_v_words(1)
+        gather_v_words(0)
         deal(nc.vector.tensor_copy, v_s[:], v_sg[:], 16)
-        nc.vector.tensor_copy(v2_w[0][:], tab2_w[0][:].indirect(list2[:]))
+        gather_v_words(1)
         nc.vector.tensor_copy(v2_s[:], tab2_s[:].indirect(list2[:]))
+        nc.vector.tensor_copy(v2_w[0][:], tab2_w[0][:].indirect(list2[:]))
+        deal(nc.vector.tensor_copy, w4_sd[:], w4_s[:].rearrange("p a n -> p (a n)"), 16)
         for half in range(HALVES):
             nc.vector.tensor_copy(
                 v2_w[1][:, half * BANK : (half + 1) * BANK],
@@ -326,7 +327,6 @@ def tile_list_satellite_radiance_calibration_kernel(
                     first_pass(half, g, t, 0, False)
                 clamp_and_gain(f, t)
 
-        deal(nc.vector.tensor_copy, w4_sd[:], w4_s[:].rearrange("p a n -> p (a n)"), 16)
         for piece in pieces[PASSES:]:
             weave_h(*piece)
         for step in range(len(pieces) + 1):

@@ -25,8 +25,9 @@ BANK = 512
 HALVES = S2 // BANK
 CHUNKS = (256, 256, 128, 128, 128, 128)
 GPSIMD_SLICES = (3, 4, 3, 1)
-Y_WEAVES_ON_SCALAR = (0, 1, 2, 3, 4)
+Y_WEAVES_ON_SCALAR = (0, 1, 2)
 EARLY_SUMS = 4
+WHOLE_CHUNKS = 0
 W1_PART = 256
 CODE_STORES = ((0, 1), (2, 3, 4), (5,))
 
@@ -132,19 +133,19 @@ def tile_list_satellite_radiance_calibration_kernel(
                 tab2_w[1][:].indirect(list2[:, half * BANK // 16 : (half + 1) * BANK // 16]),
             )
 
-        w1_b = [held.tile([P, N * PACK], BF16, name=f"w1_b{g}", align_bytes=64) for g in range(PASSES)]
-        w1_q = [held.tile([P, N], U32, name=f"w1_q{g}", align_bytes=64) for g in range(PASSES)]
-        w1_s = [held.tile([P, N], U8, name=f"w1_s{g}", align_bytes=64) for g in range(PASSES)]
+        w1_b = held.tile([P, PASSES, N * PACK], BF16, name="w1_b", align_bytes=64)
+        w1_q = held.tile([P, PASSES * N], U32, name="w1_q", align_bytes=64)
+        w1_s = held.tile([P, PASSES * N], U8, name="w1_s", align_bytes=64)
         y_s = held.tile([P, S2], U8, name="y_s", align_bytes=64)
 
         def round_w1(part):
             g, n0 = w1_parts[part]
-            dst = w1_b[g][:].rearrange("p (u e m j) -> p u m j e", u=2, e=2, j=PACK)
+            dst = w1_b[:, g, :].rearrange("p (u e m j) -> p u m j e", u=2, e=2, j=PACK)
             src = w1_raw[part][:].rearrange("p j (m u e) -> p u m j e", u=2, e=2)
             nc.scalar.copy(dst[:, :, n0 // PACK : (n0 + W1_PART) // PACK], src)
 
-        def quantise_w1(g):
-            nc.vector.quantize_mx(w1_q[g][:].bitcast(FP8X4), w1_s[g][:], w1_b[g][:])
+        def quantise_w1():
+            nc.vector.quantize_mx(w1_q[:].bitcast(FP8X4), w1_s[:], w1_b[:].rearrange("p g n -> p (g n)"))
 
         def woven(ap):
             return ap.rearrange("p (b i t) -> p b t i", i=4, t=PACK)
@@ -167,12 +168,11 @@ def tile_list_satellite_radiance_calibration_kernel(
             for half in range(HALVES)
         ]
         sums = {}
-        woven_field = {}
+        woven_chunk = {}
         rounded = {}
         quantised = {}
         banks = {}
         results = {}
-        rounded_y = {}
 
         def first_pass(half, g, t, a, opens):
             if opens:
@@ -207,11 +207,10 @@ def tile_list_satellite_radiance_calibration_kernel(
 
         def place(c, g):
             w = CHUNKS[c]
-            half, j0 = divmod(starts[c], BANK)
-            if j0 == 0:
-                tag = f"raw{len(w1_parts) - 1 - g}" if half == 0 else f"late{g}"
-                woven_field[half, g] = held.tile([P, 2 * BANK * PACK], BF16, name=f"both{half}{g}", tag=tag, align_bytes=64)
-            rounded[c, g] = woven_field[half, g][:, 2 * PACK * j0 : 2 * PACK * (j0 + w)]
+            if g == 0:
+                tag = f"raw{len(w1_parts) - 1 - c}" if c < 2 else f"late{c}"
+                woven_chunk[c] = held.tile([P, PASSES * 2 * w * PACK], BF16, name=f"both{c}", tag=tag, align_bytes=64)
+            rounded[c, g] = woven_chunk[c][:, g * 2 * w * PACK : (g + 1) * 2 * w * PACK]
 
         def weave_h(c, g):
             w = CHUNKS[c]
@@ -223,18 +222,16 @@ def tile_list_satellite_radiance_calibration_kernel(
                 woven(rounded[c, g][:, w * PACK :]), signal(h32, c, g), signal(c32, c, g), ALU.mult
             )
 
-        def quantise(c, g):
+        def quantise(c, first, count):
             w = CHUNKS[c]
-            codes = work.tile([P, 2 * w], U32, name="h_q", align_bytes=64, bufs=4)
-            scales = work.tile([P, 2 * w], U8, name="h_s", align_bytes=64, bufs=4)
-            if (c, g) == pieces[-1]:
-                for part in range(2):
-                    cols = slice(part * w, (part + 1) * w)
-                    source = rounded[c, g][:, part * w * PACK : (part + 1) * w * PACK]
-                    nc.vector.quantize_mx(codes[:, cols].bitcast(FP8X4), scales[:, cols], source)
-            else:
-                nc.vector.quantize_mx(codes[:].bitcast(FP8X4), scales[:], rounded[c, g])
-            quantised[c, g] = (codes, scales)
+            if first == 0:
+                codes = work.tile([P, PASSES * 2 * w], U32, name="h_q", align_bytes=64, bufs=3)
+                scales = work.tile([P, PASSES * 2 * w], U8, name="h_s", align_bytes=64, bufs=3)
+                quantised[c] = (codes, scales)
+            codes, scales = quantised[c]
+            cols = slice(first * w, (first + count) * w)
+            source = woven_chunk[c][:, cols.start * PACK : cols.stop * PACK]
+            nc.vector.quantize_mx(codes[:, cols].bitcast(FP8X4), scales[:, cols], source)
 
         def bank_slices(c):
             if CHUNKS[c] * PACK > BANK:
@@ -243,7 +240,9 @@ def tile_list_satellite_radiance_calibration_kernel(
 
         def second_passes(c, g):
             w = CHUNKS[c]
-            codes, scales = quantised[c, g]
+            codes, scales = quantised[c]
+            h_cols = slice(2 * g * w, (2 * g + 1) * w)
+            h2_cols = slice((2 * g + 1) * w, (2 * g + 2) * w)
             for bank, slices in enumerate(bank_slices(c)):
                 if g == 0:
                     banks[c, bank] = psum.tile([P, len(slices), w], F32, name="acc")
@@ -251,10 +250,10 @@ def tile_list_satellite_radiance_calibration_kernel(
                 for s, t in enumerate(slices):
                     nc.tensor.matmul_mx(
                         banks[c, bank][:, s, :],
-                        lhsT=w1_q[g][:, t * P : (t + 1) * P].bitcast(FP8X4),
-                        lhsT_scale=w1_s[g][:, t * P : (t + 1) * P],
-                        rhs=codes[:, :w].bitcast(FP8X4),
-                        rhs_scale=scales[:, :w],
+                        lhsT=w1_q[:, g * N + t * P : g * N + (t + 1) * P].bitcast(FP8X4),
+                        lhsT_scale=w1_s[:, g * N + t * P : g * N + (t + 1) * P],
+                        rhs=codes[:, h_cols].bitcast(FP8X4),
+                        rhs_scale=scales[:, h_cols],
                         start=(g == 0 and s == 0),
                         stop=False,
                     )
@@ -265,8 +264,8 @@ def tile_list_satellite_radiance_calibration_kernel(
                         banks[c, bank][:, s, :],
                         lhsT=w4_wd[:, 2 * n0 : 2 * (n0 + P)].bitcast(FP4X4),
                         lhsT_scale=w4_sd[:, n0 : n0 + P],
-                        rhs=codes[:, w:].bitcast(FP8X4),
-                        rhs_scale=scales[:, w:],
+                        rhs=codes[:, h2_cols].bitcast(FP8X4),
+                        rhs_scale=scales[:, h2_cols],
                         start=False,
                         stop=(g == PASSES - 1 and s == len(slices) - 1),
                     )
@@ -282,17 +281,14 @@ def tile_list_satellite_radiance_calibration_kernel(
                 nc.scalar.copy(dst, banks[c, bank][:])
             nc.sync.dma_start(out_rows[:, :, starts[c] : starts[c] + w], y32[:])
 
-        def weave_y(c):
-            rounded_y[c] = held.tile([P, CHUNKS[c] * PACK], BF16, name=f"yb_{c}", align_bytes=64)
-            if c in Y_WEAVES_ON_SCALAR:
-                nc.scalar.copy(woven(rounded_y[c][:]), in_pairs(results[c][:]))
-            else:
-                nc.vector.tensor_copy(woven(rounded_y[c][:]), in_pairs(results[c][:]))
+        y_b = held.tile([P, S2 * PACK], BF16, name="y_b", align_bytes=64)
 
-        def quantise_y(c):
-            js = slice(starts[c], starts[c] + CHUNKS[c])
-            half, j0 = divmod(starts[c], BANK)
-            nc.vector.quantize_mx(y_q[half][:, j0 : j0 + CHUNKS[c]].bitcast(FP8X4), y_s[:, js], rounded_y[c][:])
+        def weave_y(c):
+            dst = woven(y_b[:, starts[c] * PACK : (starts[c] + CHUNKS[c]) * PACK])
+            if c in Y_WEAVES_ON_SCALAR:
+                nc.scalar.copy(dst, in_pairs(results[c][:]))
+            else:
+                nc.vector.tensor_copy(dst, in_pairs(results[c][:]))
 
         out_words = out_1[0].rearrange("p m t -> p (m t)").bitcast(I32)
 
@@ -300,11 +296,12 @@ def tile_list_satellite_radiance_calibration_kernel(
             for c in group:
                 if c not in Y_WEAVES_ON_SCALAR:
                     weave_y(c)
-                quantise_y(c)
             js = slice(starts[group[0]], starts[group[-1]] + CHUNKS[group[-1]])
             half = js.start // BANK
+            codes = y_q[half][:, js.start - half * BANK : js.stop - half * BANK]
+            nc.vector.quantize_mx(codes.bitcast(FP8X4), y_s[:, js], y_b[:, js.start * PACK : js.stop * PACK])
             queue = nc.scalar if last in group else nc.sync
-            queue.dma_start(out_words[:, js], y_q[half][:, js.start - half * BANK : js.stop - half * BANK].bitcast(I32))
+            queue.dma_start(out_words[:, js], codes.bitcast(I32))
 
         for piece in pieces:
             place(*piece)
@@ -332,12 +329,22 @@ def tile_list_satellite_radiance_calibration_kernel(
         for step in range(len(pieces) + 1):
             if step < len(pieces):
                 weave_h2(*pieces[step])
-            if step < PASSES:
-                quantise_w1(step)
+            if step == 0:
+                quantise_w1()
             if step >= 1:
                 c, g = pieces[step - 1]
-                quantise(c, g)
-                second_passes(c, g)
+                if c < WHOLE_CHUNKS:
+                    if g == PASSES - 1:
+                        quantise(c, 0, 2 * PASSES)
+                        for half_of_modes in range(PASSES):
+                            second_passes(c, half_of_modes)
+                else:
+                    if (c, g) == pieces[-1]:
+                        quantise(c, 2 * g, 1)
+                        quantise(c, 2 * g + 1, 1)
+                    else:
+                        quantise(c, 2 * g, 2)
+                    second_passes(c, g)
                 if g == PASSES - 1:
                     hand_out(c)
                     if c in Y_WEAVES_ON_SCALAR:

@@ -24,7 +24,7 @@ QUADRANTS = 4
 BANK = 512
 HALVES = S2 // BANK
 CHUNKS = (256, 256, 128, 128, 128, 128)
-GPSIMD_SLICES = (3, 4, 3, 1)
+GPSIMD_SLICES = (3, 4, 3, 0)
 Y_WEAVES_ON_SCALAR = (0, 1, 2)
 EARLY_SUMS = 4
 WHOLE_CHUNKS = 0
@@ -40,6 +40,7 @@ def tile_list_satellite_radiance_calibration_kernel(
     with ExitStack() as ctx:
         held = ctx.enter_context(tc.tile_pool(name="held", bufs=1))
         work = ctx.enter_context(tc.tile_pool(name="work", bufs=6))
+        page = ctx.enter_context(tc.tile_pool(name="page", bufs=1))
         psum = ctx.enter_context(tc.psum_pool(name="psum", bufs=8))
 
         list1 = held.tile([P, S // 16], U16, name="list1")
@@ -48,7 +49,10 @@ def tile_list_satellite_radiance_calibration_kernel(
         tab2_s = held.tile([P, T2], U8, name="tab2_s", align_bytes=64)
         w4_s = held.tile([P, PASSES, N], U8, name="w4_s", align_bytes=64)
         tab_w = [held.tile([P, T], U32, name=f"tab_w{a}", tag=f"page{a}", align_bytes=64) for a in range(PASSES)]
-        tab2_w = [held.tile([P, T2], U32, name=f"tab2_w{a}", tag=f"wide{a}", align_bytes=64) for a in range(PASSES)]
+        tab2_w = [
+            held.tile([P, T2], U32, name="tab2_w0", align_bytes=64),
+            page.tile([P, T2], U32, name="tab2_w1", align_bytes=64, offset=0),
+        ]
         w1_parts = [(g, n0) for g in range(PASSES) for n0 in range(0, N, W1_PART)]
         w1_raw = [
             held.tile([P, PACK, W1_PART], F32, name=f"w1_raw{part}", tag=f"raw{part}", align_bytes=64)
@@ -107,7 +111,7 @@ def tile_list_satellite_radiance_calibration_kernel(
         v2_s = held.tile([P, S2], U8, name="v2_s", align_bytes=64)
         v2_w = [held.tile([P, S2], U32, name=f"v2_w{a}", align_bytes=64) for a in range(PASSES)]
         w4_wd = held.tile([P, PASSES * 2 * N], U8, name="w4_wd", align_bytes=64)
-        w4_sd = held.tile([P, PASSES * N], U8, name="w4_sd", align_bytes=64)
+        w4_sd = page.tile([P, PASSES * N], U8, name="w4_sd", align_bytes=64, offset=PACK * BANK * 4)
 
         def deal(copy, dst, src, run):
             copy(
@@ -126,7 +130,6 @@ def tile_list_satellite_radiance_calibration_kernel(
         gather_v_words(1)
         nc.vector.tensor_copy(v2_s[:], tab2_s[:].indirect(list2[:]))
         nc.vector.tensor_copy(v2_w[0][:], tab2_w[0][:].indirect(list2[:]))
-        deal(nc.vector.tensor_copy, w4_sd[:], w4_s[:].rearrange("p a n -> p (a n)"), 16)
         for half in range(HALVES):
             nc.vector.tensor_copy(
                 v2_w[1][:, half * BANK : (half + 1) * BANK],
@@ -161,7 +164,10 @@ def tile_list_satellite_radiance_calibration_kernel(
         h32 = {}
         for f, field in enumerate(fields):
             reuse = f == len(fields) - 1
-            c32[field] = held.tile([P, PACK, BANK], F32, name=f"c32_{f}", tag="page0" if reuse else "wide1" if f == 0 else f"c{f}", align_bytes=64)
+            if f == 0:
+                c32[field] = page.tile([P, PACK, BANK], F32, name="c32_0", align_bytes=64, offset=0)
+            else:
+                c32[field] = held.tile([P, PACK, BANK], F32, name=f"c32_{f}", tag="page0" if reuse else f"c{f}", align_bytes=64)
             h32[field] = held.tile([P, PACK, BANK], F32, name=f"h32_{f}", tag="page1" if reuse else f"h{f}", align_bytes=64)
         y_q = [
             held.tile([P, BANK], U32, name=f"y_q{half}", tag=f"page{half}", align_bytes=64)
@@ -309,6 +315,11 @@ def tile_list_satellite_radiance_calibration_kernel(
         deal(nc.scalar.copy, w4_wd[:].bitcast(U16), w4_w[:].rearrange("p a b -> p (a b)").bitcast(U16), 8)
         for part in range(len(w1_parts)):
             round_w1(part)
+
+        nc.gpsimd.tensor_copy(
+            w4_sd[:].rearrange("p (g t m) -> p g t m", g=PASSES, t=PACK),
+            w4_s[:].rearrange("p g (m t) -> p g t m", t=PACK),
+        )
 
         for t in range(EARLY_SUMS):
             first_pass(0, 0, t, 0, True)

@@ -24,12 +24,14 @@ QUADRANTS = 4
 BANK = 512
 HALVES = S2 // BANK
 CHUNKS = (256, 256, 128, 128, 128, 128)
-GPSIMD_SLICES = (3, 4, 3, 0)
-Y_WEAVES_ON_SCALAR = (0, 1, 2)
-EARLY_SUMS = 4
-WHOLE_CHUNKS = 0
+GAINS_ON_SCALAR = (PACK - 1,)
+Y_WEAVES_ON_SCALAR = (0, 1, 2, 3, 4)
+H_RUNS = ((0, 0, 512), (0, 512, 512), (1, 0, 256), (1, 256, 256), (1, 512, 512))
+H2_SLOTS = 3
+EARLY_RUNS = 2
 W1_PART = 256
 CODE_STORES = ((0, 1), (2, 3, 4), (5,))
+KIB = 1024
 
 
 def tile_list_satellite_radiance_calibration_kernel(
@@ -39,25 +41,26 @@ def tile_list_satellite_radiance_calibration_kernel(
     nc = tc.nc
     with ExitStack() as ctx:
         held = ctx.enter_context(tc.tile_pool(name="held", bufs=1))
-        work = ctx.enter_context(tc.tile_pool(name="work", bufs=6))
+        work = ctx.enter_context(tc.tile_pool(name="work", bufs=3))
         page = ctx.enter_context(tc.tile_pool(name="page", bufs=1))
         psum = ctx.enter_context(tc.psum_pool(name="psum", bufs=8))
+
+        def placed(shape, dtype, name, kib):
+            return page.tile(shape, dtype, name=name, align_bytes=64, offset=kib * KIB)
 
         list1 = held.tile([P, S // 16], U16, name="list1")
         list2 = held.tile([P, S2 // 16], U16, name="list2")
         tab_s = held.tile([P, T], U8, name="tab_s", align_bytes=64)
         tab2_s = held.tile([P, T2], U8, name="tab2_s", align_bytes=64)
         w4_s = held.tile([P, PASSES, N], U8, name="w4_s", align_bytes=64)
-        tab_w = [held.tile([P, T], U32, name=f"tab_w{a}", tag=f"page{a}", align_bytes=64) for a in range(PASSES)]
-        tab2_w = [
-            held.tile([P, T2], U32, name="tab2_w0", align_bytes=64),
-            page.tile([P, T2], U32, name="tab2_w1", align_bytes=64, offset=0),
-        ]
+        tab_w = [placed([P, T], U32, f"tab_w{a}", 8 * a) for a in range(PASSES)]
+        tab2_w = [placed([P, T2], U32, f"tab2_w{a}", 16 + 16 * a) for a in range(PASSES)]
+        w4_sd = placed([P, PASSES * N], U8, "w4_sd", 32)
+        c32 = [placed([P, PACK, S2], F32, "c32_0", 33), placed([P, PACK, S2], F32, "c32_1", 0)]
+        h32 = [placed([P, PACK, S2], F32, "h32_0", 16), placed([P, PACK, S2], F32, "h32_1", 49)]
+        y_q = [placed([P, BANK], U32, f"y_q{half}", 2 * half) for half in range(HALVES)]
         w1_parts = [(g, n0) for g in range(PASSES) for n0 in range(0, N, W1_PART)]
-        w1_raw = [
-            held.tile([P, PACK, W1_PART], F32, name=f"w1_raw{part}", tag=f"raw{part}", align_bytes=64)
-            for part in range(len(w1_parts))
-        ]
+        w1_raw = [placed([P, PACK, W1_PART], F32, f"w1_raw{part}", 65 + 4 * part) for part in range(len(w1_parts))]
         w4_w = held.tile([P, PASSES, 2 * N], U8, name="w4_w", align_bytes=64)
         lo_t = held.tile([P, PASSES, PACK], F32, name="lo_t")
         hi_t = held.tile([P, PASSES, PACK], F32, name="hi_t")
@@ -111,7 +114,6 @@ def tile_list_satellite_radiance_calibration_kernel(
         v2_s = held.tile([P, S2], U8, name="v2_s", align_bytes=64)
         v2_w = [held.tile([P, S2], U32, name=f"v2_w{a}", align_bytes=64) for a in range(PASSES)]
         w4_wd = held.tile([P, PASSES * 2 * N], U8, name="w4_wd", align_bytes=64)
-        w4_sd = page.tile([P, PASSES * N], U8, name="w4_sd", align_bytes=64, offset=PACK * BANK * 4)
 
         def deal(copy, dst, src, run):
             copy(
@@ -124,17 +126,20 @@ def tile_list_satellite_radiance_calibration_kernel(
                 v_w[a][:].rearrange("p (g t m) -> p g m t", g=PASSES, t=PACK), tab_w[a][:].indirect(list1[:])
             )
 
+        def gather_v2_words(a, half):
+            nc.vector.tensor_copy(
+                v2_w[a][:, half * BANK : (half + 1) * BANK],
+                tab2_w[a][:].indirect(list2[:, half * BANK // 16 : (half + 1) * BANK // 16]),
+            )
+
         nc.vector.tensor_copy(v_sg[:], tab_s[:].indirect(list1[:]))
         gather_v_words(0)
         deal(nc.vector.tensor_copy, v_s[:], v_sg[:], 16)
         gather_v_words(1)
         nc.vector.tensor_copy(v2_s[:], tab2_s[:].indirect(list2[:]))
-        nc.vector.tensor_copy(v2_w[0][:], tab2_w[0][:].indirect(list2[:]))
-        for half in range(HALVES):
-            nc.vector.tensor_copy(
-                v2_w[1][:, half * BANK : (half + 1) * BANK],
-                tab2_w[1][:].indirect(list2[:, half * BANK // 16 : (half + 1) * BANK // 16]),
-            )
+        for a in range(PASSES):
+            for half in range(HALVES):
+                gather_v2_words(a, half)
 
         w1_b = held.tile([P, PASSES, N * PACK], BF16, name="w1_b", align_bytes=64)
         w1_q = held.tile([P, PASSES * N], U32, name="w1_q", align_bytes=64)
@@ -153,40 +158,25 @@ def tile_list_satellite_radiance_calibration_kernel(
         def woven(ap):
             return ap.rearrange("p (b i t) -> p b t i", i=4, t=PACK)
 
-        def in_pairs(ap):
+        def by_fours(ap):
             return ap.rearrange("p t (b i) -> p b t i", i=4)
 
         last = len(CHUNKS) - 1
         starts = [sum(CHUNKS[:c]) for c in range(len(CHUNKS))]
         pieces = [(c, g) for c in range(len(CHUNKS)) for g in range(PASSES)]
-        fields = [(half, g) for half in range(HALVES) for g in range(PASSES)]
-        c32 = {}
-        h32 = {}
-        for f, field in enumerate(fields):
-            reuse = f == len(fields) - 1
-            if f == 0:
-                c32[field] = page.tile([P, PACK, BANK], F32, name="c32_0", align_bytes=64, offset=0)
-            else:
-                c32[field] = held.tile([P, PACK, BANK], F32, name=f"c32_{f}", tag="page0" if reuse else f"c{f}", align_bytes=64)
-            h32[field] = held.tile([P, PACK, BANK], F32, name=f"h32_{f}", tag="page1" if reuse else f"h{f}", align_bytes=64)
-        y_q = [
-            held.tile([P, BANK], U32, name=f"y_q{half}", tag=f"page{half}", align_bytes=64)
-            for half in range(HALVES)
-        ]
         sums = {}
-        woven_chunk = {}
         rounded = {}
         quantised = {}
         banks = {}
         results = {}
 
-        def first_pass(half, g, t, a, opens):
+        def first_pass(g, t, half, a, opens):
             if opens:
-                sums[half, g, t] = psum.tile([P, BANK], F32, name="acc")
+                sums[g, t, half] = psum.tile([P, BANK], F32, name="acc")
             cols = slice(g * PASS + t * P, g * PASS + (t + 1) * P)
             js = slice(half * BANK, (half + 1) * BANK)
             nc.tensor.matmul_mx(
-                sums[half, g, t][:],
+                sums[g, t, half][:],
                 lhsT=v_w[a][:, cols].bitcast(FP8X4),
                 lhsT_scale=v_s[4 * a : P, cols],
                 rhs=v2_w[a][:, js].bitcast(FP8X4),
@@ -195,49 +185,59 @@ def tile_list_satellite_radiance_calibration_kernel(
                 stop=not opens,
             )
 
-        def clamp_and_gain(f, t):
-            half, g = fields[f]
-            c_row = c32[half, g][:, t, :]
-            h_row = h32[half, g][:, t, :]
+        def clamp(g, t, half):
             nc.vector.tensor_scalar(
-                c_row, sums[half, g, t][:], lo_t[:, g, t : t + 1], hi_t[:, g, t : t + 1], ALU.max, ALU.min
+                c32[g][:, t, half * BANK : (half + 1) * BANK], sums[g, t, half][:],
+                lo_t[:, g, t : t + 1], hi_t[:, g, t : t + 1], ALU.max, ALU.min,
             )
-            if t < GPSIMD_SLICES[f]:
-                nc.gpsimd.tensor_scalar(h_row, c_row, gain_t[:, g, t : t + 1], 0.0, ALU.mult, ALU.add)
+
+        def apply_gain(g, t):
+            if t in GAINS_ON_SCALAR:
+                scale = gain_t[:, g, t : t + 1]
+                if g == PASSES - 1:
+                    last_gain = placed([P, 1], F32, "last_gain", 77)
+                    nc.scalar.copy(last_gain[:], scale)
+                    scale = last_gain[:]
+                nc.scalar.activation(h32[g][:, t, :], c32[g][:, t, :], ACT.Copy, scale=scale)
             else:
-                nc.scalar.activation(h_row, c_row, ACT.Copy, scale=gain_t[:, g, t : t + 1])
+                nc.gpsimd.tensor_scalar(h32[g][:, t, :], c32[g][:, t, :], gain_t[:, g, t : t + 1], 0.0, ALU.mult, ALU.add)
 
-        def signal(tiles, c, g):
-            j0 = starts[c] % BANK
-            return in_pairs(tiles[starts[c] // BANK, g][:, :, j0 : j0 + CHUNKS[c]])
+        def signal(tiles, g, first, width):
+            return by_fours(tiles[g][:, :, first : first + width])
 
-        def place(c, g):
-            w = CHUNKS[c]
-            if g == 0:
-                tag = f"raw{len(w1_parts) - 1 - c}" if c < 2 else f"late{c}"
-                woven_chunk[c] = held.tile([P, PASSES * 2 * w * PACK], BF16, name=f"both{c}", tag=tag, align_bytes=64)
-            rounded[c, g] = woven_chunk[c][:, g * 2 * w * PACK : (g + 1) * 2 * w * PACK]
+        h_b = []
+        for run, (g, first, width) in enumerate(H_RUNS):
+            if run < EARLY_RUNS:
+                h_b.append(placed([P, width * PACK], BF16, f"h_b{run}", 77 - 4 * run))
+            else:
+                h_b.append(held.tile([P, width * PACK], BF16, name=f"h_b{run}", align_bytes=64))
+        h_q = [held.tile([P, run[2]], U32, name=f"h_q{k}", align_bytes=64) for k, run in enumerate(H_RUNS)]
+        h_s = [held.tile([P, run[2]], U8, name=f"h_s{k}", align_bytes=64) for k, run in enumerate(H_RUNS)]
 
-        def weave_h(c, g):
-            w = CHUNKS[c]
-            nc.scalar.copy(woven(rounded[c, g][:, : w * PACK]), signal(h32, c, g))
+        def run_of(c, g):
+            return [
+                k for k, (group, first, width) in enumerate(H_RUNS) if group == g and first <= starts[c] < first + width
+            ][0]
+
+        def weave_h(run):
+            nc.scalar.copy(woven(h_b[run][:]), signal(h32, *H_RUNS[run]))
+
+        def quantise_h(run):
+            nc.vector.quantize_mx(h_q[run][:].bitcast(FP8X4), h_s[run][:], h_b[run][:])
 
         def weave_h2(c, g):
-            w = CHUNKS[c]
+            slot = pieces.index((c, g)) % H2_SLOTS
+            rounded[c, g] = placed([P, CHUNKS[c] * PACK], BF16, f"h2_b{c}_{g}", (78, 82, 80)[slot])
             nc.vector.tensor_tensor(
-                woven(rounded[c, g][:, w * PACK :]), signal(h32, c, g), signal(c32, c, g), ALU.mult
+                woven(rounded[c, g][:]), signal(h32, g, starts[c], CHUNKS[c]), signal(c32, g, starts[c], CHUNKS[c]), ALU.mult
             )
 
-        def quantise(c, first, count):
+        def quantise_h2(c, g):
             w = CHUNKS[c]
-            if first == 0:
-                codes = work.tile([P, PASSES * 2 * w], U32, name="h_q", align_bytes=64, bufs=3)
-                scales = work.tile([P, PASSES * 2 * w], U8, name="h_s", align_bytes=64, bufs=3)
-                quantised[c] = (codes, scales)
-            codes, scales = quantised[c]
-            cols = slice(first * w, (first + count) * w)
-            source = woven_chunk[c][:, cols.start * PACK : cols.stop * PACK]
-            nc.vector.quantize_mx(codes[:, cols].bitcast(FP8X4), scales[:, cols], source)
+            codes = work.tile([P, w], U32, name="h2_q", align_bytes=64, bufs=4)
+            scales = work.tile([P, w], U8, name="h2_s", align_bytes=64, bufs=4)
+            quantised[c, g] = (codes, scales)
+            nc.vector.quantize_mx(codes[:].bitcast(FP8X4), scales[:], rounded[c, g][:])
 
         def bank_slices(c):
             if CHUNKS[c] * PACK > BANK:
@@ -246,20 +246,21 @@ def tile_list_satellite_radiance_calibration_kernel(
 
         def second_passes(c, g):
             w = CHUNKS[c]
-            codes, scales = quantised[c]
-            h_cols = slice(2 * g * w, (2 * g + 1) * w)
-            h2_cols = slice((2 * g + 1) * w, (2 * g + 2) * w)
-            for bank, slices in enumerate(bank_slices(c)):
-                if g == 0:
+            codes, scales = quantised[c, g]
+            run = run_of(c, g)
+            js = slice(starts[c] - H_RUNS[run][1], starts[c] - H_RUNS[run][1] + w)
+            if g == 0:
+                for bank, slices in enumerate(bank_slices(c)):
                     banks[c, bank] = psum.tile([P, len(slices), w], F32, name="acc")
             for bank, slices in enumerate(bank_slices(c)):
                 for s, t in enumerate(slices):
+                    n0 = g * N + t * P
                     nc.tensor.matmul_mx(
                         banks[c, bank][:, s, :],
-                        lhsT=w1_q[:, g * N + t * P : g * N + (t + 1) * P].bitcast(FP8X4),
-                        lhsT_scale=w1_s[:, g * N + t * P : g * N + (t + 1) * P],
-                        rhs=codes[:, h_cols].bitcast(FP8X4),
-                        rhs_scale=scales[:, h_cols],
+                        lhsT=w1_q[:, n0 : n0 + P].bitcast(FP8X4),
+                        lhsT_scale=w1_s[:, n0 : n0 + P],
+                        rhs=h_q[run][:, js].bitcast(FP8X4),
+                        rhs_scale=h_s[run][:, js],
                         start=(g == 0 and s == 0),
                         stop=False,
                     )
@@ -270,8 +271,8 @@ def tile_list_satellite_radiance_calibration_kernel(
                         banks[c, bank][:, s, :],
                         lhsT=w4_wd[:, 2 * n0 : 2 * (n0 + P)].bitcast(FP4X4),
                         lhsT_scale=w4_sd[:, n0 : n0 + P],
-                        rhs=codes[:, h2_cols].bitcast(FP8X4),
-                        rhs_scale=scales[:, h2_cols],
+                        rhs=codes[:].bitcast(FP8X4),
+                        rhs_scale=scales[:],
                         start=False,
                         stop=(g == PASSES - 1 and s == len(slices) - 1),
                     )
@@ -283,8 +284,7 @@ def tile_list_satellite_radiance_calibration_kernel(
             y32 = held.tile([P, PACK, w], F32, name=f"y32_{c}", align_bytes=64)
             results[c] = y32
             for bank, slices in enumerate(bank_slices(c)):
-                dst = y32[:, slices[0] : slices[-1] + 1, :]
-                nc.scalar.copy(dst, banks[c, bank][:])
+                nc.scalar.copy(y32[:, slices[0] : slices[-1] + 1, :], banks[c, bank][:])
             nc.sync.dma_start(out_rows[:, :, starts[c] : starts[c] + w], y32[:])
 
         y_b = held.tile([P, S2 * PACK], BF16, name="y_b", align_bytes=64)
@@ -292,9 +292,9 @@ def tile_list_satellite_radiance_calibration_kernel(
         def weave_y(c):
             dst = woven(y_b[:, starts[c] * PACK : (starts[c] + CHUNKS[c]) * PACK])
             if c in Y_WEAVES_ON_SCALAR:
-                nc.scalar.copy(dst, in_pairs(results[c][:]))
+                nc.scalar.copy(dst, by_fours(results[c][:]))
             else:
-                nc.vector.tensor_copy(dst, in_pairs(results[c][:]))
+                nc.vector.tensor_copy(dst, by_fours(results[c][:]))
 
         out_words = out_1[0].rearrange("p m t -> p (m t)").bitcast(I32)
 
@@ -309,9 +309,6 @@ def tile_list_satellite_radiance_calibration_kernel(
             queue = nc.scalar if last in group else nc.sync
             queue.dma_start(out_words[:, js], codes.bitcast(I32))
 
-        for piece in pieces:
-            place(*piece)
-
         deal(nc.scalar.copy, w4_wd[:].bitcast(U16), w4_w[:].rearrange("p a b -> p (a b)").bitcast(U16), 8)
         for part in range(len(w1_parts)):
             round_w1(part)
@@ -321,22 +318,25 @@ def tile_list_satellite_radiance_calibration_kernel(
             w4_s[:].rearrange("p g (m t) -> p g t m", t=PACK),
         )
 
-        for t in range(EARLY_SUMS):
-            first_pass(0, 0, t, 0, True)
-        for f, (half, g) in enumerate(fields):
-            if f == PASSES:
-                weave_h(0, 0)
-                weave_h(0, 1)
+        for a in range(PASSES):
+            for half in range(HALVES):
+                for t in range(PACK):
+                    first_pass(0, t, half, a, a == 0)
+        for g in range(PASSES):
             for t in range(PACK):
-                if f == 0 and t < EARLY_SUMS:
-                    first_pass(half, g, t, 1, False)
-                else:
-                    first_pass(half, g, t, 1, True)
-                    first_pass(half, g, t, 0, False)
-                clamp_and_gain(f, t)
+                for half in range(HALVES):
+                    if g > 0:
+                        first_pass(g, t, half, 0, True)
+                        first_pass(g, t, half, 1, False)
+                    clamp(g, t, half)
+                if (g, t) == (PASSES - 1, PACK - 1):
+                    for run in range(EARLY_RUNS):
+                        weave_h(run)
+                    quantise_h(0)
+                apply_gain(g, t)
 
-        for piece in pieces[PASSES:]:
-            weave_h(*piece)
+        for run in range(EARLY_RUNS, len(H_RUNS)):
+            weave_h(run)
         for step in range(len(pieces) + 1):
             if step < len(pieces):
                 weave_h2(*pieces[step])
@@ -344,18 +344,10 @@ def tile_list_satellite_radiance_calibration_kernel(
                 quantise_w1()
             if step >= 1:
                 c, g = pieces[step - 1]
-                if c < WHOLE_CHUNKS:
-                    if g == PASSES - 1:
-                        quantise(c, 0, 2 * PASSES)
-                        for half_of_modes in range(PASSES):
-                            second_passes(c, half_of_modes)
-                else:
-                    if (c, g) == pieces[-1]:
-                        quantise(c, 2 * g, 1)
-                        quantise(c, 2 * g + 1, 1)
-                    else:
-                        quantise(c, 2 * g, 2)
-                    second_passes(c, g)
+                if step > 1 and starts[c] == H_RUNS[run_of(c, g)][1]:
+                    quantise_h(run_of(c, g))
+                quantise_h2(c, g)
+                second_passes(c, g)
                 if g == PASSES - 1:
                     hand_out(c)
                     if c in Y_WEAVES_ON_SCALAR:

@@ -24,14 +24,15 @@ QUADRANTS = 4
 BANK = 512
 HALVES = S2 // BANK
 CHUNKS = (256, 256, 128, 128, 128, 128)
-GAINS_ON_SCALAR = (PACK - 1,)
-Y_WEAVES_ON_SCALAR = (0, 1, 2, 3, 4)
-H_RUNS = ((0, 0, 512), (0, 512, 512), (1, 0, 256), (1, 256, 256), (1, 512, 512))
+GPSIMD_SLICES = (3, 4, 3, 0)
+Y_WEAVES_ON_SCALAR = (0, 1, 2)
+H_RUNS = ((0, 0, 256), (1, 0, 256), (0, 256, 256), (1, 256, 256), (0, 512, 512), (1, 512, 512))
 H2_SLOTS = 3
 EARLY_RUNS = 2
 W1_PART = 256
 CODE_STORES = ((0, 1), (2, 3, 4), (5,))
 KIB = 1024
+WIDE_ROW = 96
 
 
 def tile_list_satellite_radiance_calibration_kernel(
@@ -46,28 +47,35 @@ def tile_list_satellite_radiance_calibration_kernel(
         psum = ctx.enter_context(tc.psum_pool(name="psum", bufs=8))
 
         def placed(shape, dtype, name, kib):
-            return page.tile(shape, dtype, name=name, align_bytes=64, offset=kib * KIB)
+            return page.tile(shape, dtype, name=name, align_bytes=64, offset=int(kib * KIB))
 
         list1 = held.tile([P, S // 16], U16, name="list1")
         list2 = held.tile([P, S2 // 16], U16, name="list2")
-        tab_s = held.tile([P, T], U8, name="tab_s", align_bytes=64)
         tab2_s = held.tile([P, T2], U8, name="tab2_s", align_bytes=64)
         w4_s = held.tile([P, PASSES, N], U8, name="w4_s", align_bytes=64)
-        tab_w = [placed([P, T], U32, f"tab_w{a}", 8 * a) for a in range(PASSES)]
-        tab2_w = [placed([P, T2], U32, f"tab2_w{a}", 16 + 16 * a) for a in range(PASSES)]
-        w4_sd = placed([P, PASSES * N], U8, "w4_sd", 32)
-        c32 = [placed([P, PACK, S2], F32, "c32_0", 33), placed([P, PACK, S2], F32, "c32_1", 0)]
-        h32 = [placed([P, PACK, S2], F32, "h32_0", 16), placed([P, PACK, S2], F32, "h32_1", 49)]
-        y_q = [placed([P, BANK], U32, f"y_q{half}", 2 * half) for half in range(HALVES)]
+        tab_s = placed([P, T], U8, "tab_s", 41)
+        v_sg = placed([P, S], U8, "v_sg", 40)
+        tab_w = [placed([P, T], U32, f"tab_w{a}", 4 + 8 * a) for a in range(PASSES)]
+        tab2_w = [placed([P, T2], U32, f"tab2_w{a}", 24 + 16 * a) for a in range(PASSES)]
+        w4_sd = placed([P, PASSES * N], U8, "w4_sd", 40)
+        fields = [(half, g) for half in range(HALVES) for g in range(PASSES)]
+        c32 = {field: placed([P, PACK, BANK], F32, f"c32_{f}", (41, 49, 57, 73)[f]) for f, field in enumerate(fields)}
+        h32 = {field: placed([P, PACK, BANK], F32, f"h32_{f}", (24, 32, 65, 81)[f]) for f, field in enumerate(fields)}
+        y_q = [placed([P, BANK], U32, f"y_q{half}", 73 + 8 * half) for half in range(HALVES)]
         w1_parts = [(g, n0) for g in range(PASSES) for n0 in range(0, N, W1_PART)]
-        w1_raw = [placed([P, PACK, W1_PART], F32, f"w1_raw{part}", 65 + 4 * part) for part in range(len(w1_parts))]
-        w4_w = held.tile([P, PASSES, 2 * N], U8, name="w4_w", align_bytes=64)
+        w1_raw = [placed([P, PACK, W1_PART], F32, f"w1_raw{part}", 5 + 4 * part) for part in range(len(w1_parts))]
+        w4_w = placed([P, PASSES, 2 * N], U8, "w4_w", 2.5)
         lo_t = held.tile([P, PASSES, PACK], F32, name="lo_t")
-        hi_t = held.tile([P, PASSES, PACK], F32, name="hi_t")
+        hi_t = placed([P, PASSES, PACK], F32, "hi_t", 4.5)
         gain_t = held.tile([P, PASSES, PACK], F32, name="gain_t")
 
-        nc.gpsimd.memset(tab_s[:].bitcast(I32), 0)
+        v_sd = held.tile([P, S], U8, name="v_sd", align_bytes=64)
+        v_s = [held.tile([P, S], U8, name=f"v_s{a}", align_bytes=64) for a in range(PASSES)]
+
         nc.vector.memset(tab2_s[:].bitcast(I32), 0)
+        nc.vector.memset(tab_s[0:WIDE_ROW, :].bitcast(I32), 0)
+        for a in range(PASSES):
+            nc.vector.memset(v_s[a][:].bitcast(I32), 0)
         nc.vector.memset(w4_s[:].rearrange("p a n -> p (a n)").bitcast(I32), 0)
 
         def load_words(dst, words, a):
@@ -80,36 +88,17 @@ def tile_list_satellite_radiance_calibration_kernel(
         def load_by_mode(dst, src):
             nc.sync.dma_start(dst[:], src.rearrange("(g p t) -> p g t", g=PASSES, t=PACK))
 
-        nc.sync.dma_start(list1[:], offs)
-        nc.sync.dma_start(list2[:], offs2)
-        for q in range(QUADRANTS):
-            nc.sync.dma_start(
-                tab_s[32 * q : 32 * q + 4 * PASSES, :].bitcast(I32), tab_scales[:, 4 * q : 4 * q + 4, :].bitcast(I32)
-            )
-        load_words(tab_w[0], tab_words, 0)
-        row_groups = [(q, a) for q in range(QUADRANTS) for a in range(PASSES)]
-        for q, a in row_groups[:3]:
-            load_tab2_scale_rows(q, a)
-        load_words(tab_w[1], tab_words, 1)
-        for q, a in row_groups[3:]:
-            load_tab2_scale_rows(q, a)
-        load_words(tab2_w[0], tab2_words, 0)
-        for q in range(QUADRANTS):
+        def load_w4_scale_rows(q):
             nc.sync.dma_start(
                 w4_s[32 * q : 32 * q + 4, :, :].bitcast(I32),
                 w4_scales[:, 4 * q : 4 * q + 4, :].rearrange("a r n -> r a n").bitcast(I32),
             )
-        load_words(tab2_w[1], tab2_words, 1)
-        load_by_mode(gain_t, gain)
-        load_by_mode(lo_t, lo)
-        load_by_mode(hi_t, hi)
-        nc.sync.dma_start(w4_w[:].bitcast(I32), w4_words.rearrange("a p b -> p a b").bitcast(I32))
-        for part, (g, n0) in enumerate(w1_parts):
-            rows = w1[g * PASS : (g + 1) * PASS, n0 : n0 + W1_PART]
-            nc.sync.dma_start(w1_raw[part][:], rows.rearrange("(p j) n -> p j n", j=PACK))
 
-        v_sg = held.tile([P, S], U8, name="v_sg", align_bytes=64)
-        v_s = held.tile([P, S], U8, name="v_s", align_bytes=64)
+        def carry_scale_rows(a):
+            for q in range(QUADRANTS):
+                row = WIDE_ROW + 16 * a + 4 * q
+                nc.sync.dma_start(v_s[a][32 * q : 32 * q + 4, :].bitcast(I32), v_sd[row : row + 4, :].bitcast(I32))
+
         v_w = [held.tile([P, S], U32, name=f"v_w{a}", align_bytes=64) for a in range(PASSES)]
         v2_s = held.tile([P, S2], U8, name="v2_s", align_bytes=64)
         v2_w = [held.tile([P, S2], U32, name=f"v2_w{a}", align_bytes=64) for a in range(PASSES)]
@@ -132,10 +121,34 @@ def tile_list_satellite_radiance_calibration_kernel(
                 tab2_w[a][:].indirect(list2[:, half * BANK // 16 : (half + 1) * BANK // 16]),
             )
 
+        nc.sync.dma_start(tab_s[WIDE_ROW:P, :].bitcast(I32), tab_scales.rearrange("a r t -> (a r) t").bitcast(I32))
+        nc.sync.dma_start(list1[:], offs)
+        load_words(tab_w[0], tab_words, 0)
+        nc.sync.dma_start(list2[:], offs2)
+        row_groups = [(q, a) for q in range(QUADRANTS) for a in range(PASSES)]
+        for q, a in row_groups[:6]:
+            load_tab2_scale_rows(q, a)
+        load_words(tab_w[1], tab_words, 1)
+        for q, a in row_groups[6:]:
+            load_tab2_scale_rows(q, a)
+        for q in range(QUADRANTS):
+            load_w4_scale_rows(q)
+        load_words(tab2_w[0], tab2_words, 0)
+
         nc.vector.tensor_copy(v_sg[:], tab_s[:].indirect(list1[:]))
+        deal(nc.vector.tensor_copy, v_sd[:], v_sg[:], 16)
+        carry_scale_rows(0)
+        load_by_mode(gain_t, gain)
+        load_by_mode(lo_t, lo)
+        load_words(tab2_w[1], tab2_words, 1)
+        carry_scale_rows(1)
         gather_v_words(0)
-        deal(nc.vector.tensor_copy, v_s[:], v_sg[:], 16)
+        load_by_mode(hi_t, hi)
+        nc.sync.dma_start(w4_w[:].bitcast(I32), w4_words.rearrange("a p b -> p a b").bitcast(I32))
         gather_v_words(1)
+        for part, (g, n0) in enumerate(w1_parts):
+            rows = w1[g * PASS : (g + 1) * PASS, n0 : n0 + W1_PART]
+            nc.sync.dma_start(w1_raw[part][:], rows.rearrange("(p j) n -> p j n", j=PACK))
         nc.vector.tensor_copy(v2_s[:], tab2_s[:].indirect(list2[:]))
         for a in range(PASSES):
             for half in range(HALVES):
@@ -178,7 +191,7 @@ def tile_list_satellite_radiance_calibration_kernel(
             nc.tensor.matmul_mx(
                 sums[g, t, half][:],
                 lhsT=v_w[a][:, cols].bitcast(FP8X4),
-                lhsT_scale=v_s[4 * a : P, cols],
+                lhsT_scale=v_s[a][:, cols],
                 rhs=v2_w[a][:, js].bitcast(FP8X4),
                 rhs_scale=v2_s[8 + 4 * a : P, js],
                 start=opens,
@@ -187,28 +200,25 @@ def tile_list_satellite_radiance_calibration_kernel(
 
         def clamp(g, t, half):
             nc.vector.tensor_scalar(
-                c32[g][:, t, half * BANK : (half + 1) * BANK], sums[g, t, half][:],
+                c32[half, g][:, t, :], sums[g, t, half][:],
                 lo_t[:, g, t : t + 1], hi_t[:, g, t : t + 1], ALU.max, ALU.min,
             )
 
-        def apply_gain(g, t):
-            if t in GAINS_ON_SCALAR:
-                scale = gain_t[:, g, t : t + 1]
-                if g == PASSES - 1:
-                    last_gain = placed([P, 1], F32, "last_gain", 77)
-                    nc.scalar.copy(last_gain[:], scale)
-                    scale = last_gain[:]
-                nc.scalar.activation(h32[g][:, t, :], c32[g][:, t, :], ACT.Copy, scale=scale)
+        def apply_gain(g, t, half):
+            c_row = c32[half, g][:, t, :]
+            h_row = h32[half, g][:, t, :]
+            if t < GPSIMD_SLICES[fields.index((half, g))]:
+                nc.gpsimd.tensor_scalar(h_row, c_row, gain_t[:, g, t : t + 1], 0.0, ALU.mult, ALU.add)
             else:
-                nc.gpsimd.tensor_scalar(h32[g][:, t, :], c32[g][:, t, :], gain_t[:, g, t : t + 1], 0.0, ALU.mult, ALU.add)
+                nc.scalar.activation(h_row, c_row, ACT.Copy, scale=gain_t[:, g, t : t + 1])
 
         def signal(tiles, g, first, width):
-            return by_fours(tiles[g][:, :, first : first + width])
+            return by_fours(tiles[first // BANK, g][:, :, first % BANK : first % BANK + width])
 
         h_b = []
         for run, (g, first, width) in enumerate(H_RUNS):
             if run < EARLY_RUNS:
-                h_b.append(placed([P, width * PACK], BF16, f"h_b{run}", 77 - 4 * run))
+                h_b.append(placed([P, width * PACK], BF16, f"h_b{run}", 17 - 4 * run))
             else:
                 h_b.append(held.tile([P, width * PACK], BF16, name=f"h_b{run}", align_bytes=64))
         h_q = [held.tile([P, run[2]], U32, name=f"h_q{k}", align_bytes=64) for k, run in enumerate(H_RUNS)]
@@ -227,7 +237,7 @@ def tile_list_satellite_radiance_calibration_kernel(
 
         def weave_h2(c, g):
             slot = pieces.index((c, g)) % H2_SLOTS
-            rounded[c, g] = placed([P, CHUNKS[c] * PACK], BF16, f"h2_b{c}_{g}", (78, 82, 80)[slot])
+            rounded[c, g] = placed([P, CHUNKS[c] * PACK], BF16, f"h2_b{c}_{g}", 89 + 2 * slot)
             nc.vector.tensor_tensor(
                 woven(rounded[c, g][:]), signal(h32, g, starts[c], CHUNKS[c]), signal(c32, g, starts[c], CHUNKS[c]), ALU.mult
             )
@@ -319,21 +329,19 @@ def tile_list_satellite_radiance_calibration_kernel(
         )
 
         for a in range(PASSES):
-            for half in range(HALVES):
+            for g in range(PASSES):
                 for t in range(PACK):
-                    first_pass(0, t, half, a, a == 0)
-        for g in range(PASSES):
+                    first_pass(g, t, 0, a, a == 0)
+        for half, g in fields:
+            if (half, g) == (1, 0):
+                for run in range(EARLY_RUNS):
+                    weave_h(run)
             for t in range(PACK):
-                for half in range(HALVES):
-                    if g > 0:
-                        first_pass(g, t, half, 0, True)
-                        first_pass(g, t, half, 1, False)
-                    clamp(g, t, half)
-                if (g, t) == (PASSES - 1, PACK - 1):
-                    for run in range(EARLY_RUNS):
-                        weave_h(run)
-                    quantise_h(0)
-                apply_gain(g, t)
+                if half > 0:
+                    first_pass(g, t, half, 0, True)
+                    first_pass(g, t, half, 1, False)
+                clamp(g, t, half)
+                apply_gain(g, t, half)
 
         for run in range(EARLY_RUNS, len(H_RUNS)):
             weave_h(run)
@@ -344,7 +352,7 @@ def tile_list_satellite_radiance_calibration_kernel(
                 quantise_w1()
             if step >= 1:
                 c, g = pieces[step - 1]
-                if step > 1 and starts[c] == H_RUNS[run_of(c, g)][1]:
+                if starts[c] == H_RUNS[run_of(c, g)][1]:
                     quantise_h(run_of(c, g))
                 quantise_h2(c, g)
                 second_passes(c, g)

@@ -33,6 +33,7 @@ W1_PART = 256
 CODE_STORES = ((0, 1), (2, 3, 4), (5,))
 KIB = 1024
 WIDE_ROW = 96
+V2_PLANE = 8
 
 
 def tile_list_satellite_radiance_calibration_kernel(
@@ -51,39 +52,35 @@ def tile_list_satellite_radiance_calibration_kernel(
 
         list1 = held.tile([P, S // 16], U16, name="list1")
         list2 = held.tile([P, S2 // 16], U16, name="list2")
-        tab2_s = held.tile([P, T2], U8, name="tab2_s", align_bytes=64)
         w4_s = held.tile([P, PASSES, N], U8, name="w4_s", align_bytes=64)
-        tab_s = placed([P, T], U8, "tab_s", 41)
-        v_sg = placed([P, S], U8, "v_sg", 40)
+        tab_s = held.tile([P, T], U8, name="tab_s", align_bytes=64)
+        v_sg = held.tile([P, S], U8, name="v_sg", align_bytes=64)
+        tab2_s = placed([P, T2], U8, "tab2_s", 53)
+        rows_of_pass = [held.tile([P, S], U8, name="rows0", align_bytes=64), placed([P, S], U8, "rows1", 56)]
         tab_w = [placed([P, T], U32, f"tab_w{a}", 4 + 8 * a) for a in range(PASSES)]
-        tab2_w = [placed([P, T2], U32, f"tab2_w{a}", 24 + 16 * a) for a in range(PASSES)]
-        w4_sd = placed([P, PASSES * N], U8, "w4_sd", 40)
+        tab2_w = [placed([P, T2], U32, f"tab2_w{a}", (23, 39)[a]) for a in range(PASSES)]
+        w4_sd = placed([P, PASSES * N], U8, "w4_sd", 39)
         fields = [(half, g) for half in range(HALVES) for g in range(PASSES)]
-        c32 = {field: placed([P, PACK, BANK], F32, f"c32_{f}", (41, 49, 57, 73)[f]) for f, field in enumerate(fields)}
-        h32 = {field: placed([P, PACK, BANK], F32, f"h32_{f}", (24, 32, 65, 81)[f]) for f, field in enumerate(fields)}
+        c32 = {field: placed([P, PACK, BANK], F32, f"c32_{f}", (40, 48, 57, 73)[f]) for f, field in enumerate(fields)}
+        h32 = {field: placed([P, PACK, BANK], F32, f"h32_{f}", (23, 31, 65, 81)[f]) for f, field in enumerate(fields)}
         y_q = [placed([P, BANK], U32, f"y_q{half}", 73 + 8 * half) for half in range(HALVES)]
         w1_parts = [(g, n0) for g in range(PASSES) for n0 in range(0, N, W1_PART)]
         w1_raw = [placed([P, PACK, W1_PART], F32, f"w1_raw{part}", 5 + 4 * part) for part in range(len(w1_parts))]
         w4_w = placed([P, PASSES, 2 * N], U8, "w4_w", 2.5)
         lo_t = held.tile([P, PASSES, PACK], F32, name="lo_t")
-        hi_t = placed([P, PASSES, PACK], F32, "hi_t", 4.5)
+        hi_t = held.tile([P, PASSES, PACK], F32, name="hi_t")
         gain_t = held.tile([P, PASSES, PACK], F32, name="gain_t")
 
         v_sd = held.tile([P, S], U8, name="v_sd", align_bytes=64)
-        v_s = [held.tile([P, S], U8, name=f"v_s{a}", align_bytes=64) for a in range(PASSES)]
 
-        nc.vector.memset(tab2_s[:].bitcast(I32), 0)
-        nc.vector.memset(tab_s[0:WIDE_ROW, :].bitcast(I32), 0)
-        for a in range(PASSES):
-            nc.vector.memset(v_s[a][:].bitcast(I32), 0)
         nc.vector.memset(w4_s[:].rearrange("p a n -> p (a n)").bitcast(I32), 0)
+        nc.vector.memset(tab_s[32:64, :].bitcast(I32), 0)
+        nc.vector.memset(tab_s[64:P, :].bitcast(I32), 0)
+        nc.vector.memset(tab2_s[0:WIDE_ROW, :].bitcast(I32), 0)
+        nc.vector.memset(rows_of_pass[0][:].bitcast(I32), 0)
 
         def load_words(dst, words, a):
             nc.sync.dma_start(dst[:].bitcast(I32), words[a].rearrange("p t i -> p (t i)").bitcast(I32))
-
-        def load_tab2_scale_rows(q, a):
-            row = 32 * q + 8 + 4 * a
-            nc.sync.dma_start(tab2_s[row : row + 4, :].bitcast(I32), tab2_scales[a, 4 * q : 4 * q + 4, :].bitcast(I32))
 
         def load_by_mode(dst, src):
             nc.sync.dma_start(dst[:], src.rearrange("(g p t) -> p g t", g=PASSES, t=PACK))
@@ -94,10 +91,16 @@ def tile_list_satellite_radiance_calibration_kernel(
                 w4_scales[:, 4 * q : 4 * q + 4, :].rearrange("a r n -> r a n").bitcast(I32),
             )
 
-        def carry_scale_rows(a):
-            for q in range(QUADRANTS):
-                row = WIDE_ROW + 16 * a + 4 * q
-                nc.sync.dma_start(v_s[a][32 * q : 32 * q + 4, :].bitcast(I32), v_sd[row : row + 4, :].bitcast(I32))
+        def carry_scale_rows(gathered, first_row, plane, a, quadrants):
+            for q in quadrants:
+                row = first_row + 16 * a + 4 * q
+                dst = rows_of_pass[a][32 * q + plane : 32 * q + plane + 4, :]
+                nc.sync.dma_start(dst.bitcast(I32), gathered[row : row + 4, :].bitcast(I32))
+
+        def load_word_half(a, half):
+            cols = slice(half * T2 // 2, (half + 1) * T2 // 2)
+            words = tab2_words[a].rearrange("p t i -> p (t i)").bitcast(I32)
+            nc.sync.dma_start(tab2_w[a][:, cols].bitcast(I32), words[:, cols])
 
         v_w = [held.tile([P, S], U32, name=f"v_w{a}", align_bytes=64) for a in range(PASSES)]
         v2_s = held.tile([P, S2], U8, name="v2_s", align_bytes=64)
@@ -121,35 +124,36 @@ def tile_list_satellite_radiance_calibration_kernel(
                 tab2_w[a][:].indirect(list2[:, half * BANK // 16 : (half + 1) * BANK // 16]),
             )
 
-        nc.sync.dma_start(tab_s[WIDE_ROW:P, :].bitcast(I32), tab_scales.rearrange("a r t -> (a r) t").bitcast(I32))
+        nc.sync.dma_start(tab_s[0:32, :].bitcast(I32), tab_scales.rearrange("a r t -> (a r) t").bitcast(I32))
         nc.sync.dma_start(list1[:], offs)
         load_words(tab_w[0], tab_words, 0)
         nc.sync.dma_start(list2[:], offs2)
-        row_groups = [(q, a) for q in range(QUADRANTS) for a in range(PASSES)]
-        for q, a in row_groups[:6]:
-            load_tab2_scale_rows(q, a)
-        load_words(tab_w[1], tab_words, 1)
-        for q, a in row_groups[6:]:
-            load_tab2_scale_rows(q, a)
+        nc.sync.dma_start(tab2_s[WIDE_ROW:P, :].bitcast(I32), tab2_scales.rearrange("a r t -> (a r) t").bitcast(I32))
         for q in range(QUADRANTS):
             load_w4_scale_rows(q)
+        load_words(tab_w[1], tab_words, 1)
+        load_by_mode(gain_t, gain)
+        load_by_mode(lo_t, lo)
+        load_by_mode(hi_t, hi)
         load_words(tab2_w[0], tab2_words, 0)
 
         nc.vector.tensor_copy(v_sg[:], tab_s[:].indirect(list1[:]))
         deal(nc.vector.tensor_copy, v_sd[:], v_sg[:], 16)
-        carry_scale_rows(0)
-        load_by_mode(gain_t, gain)
-        load_by_mode(lo_t, lo)
-        load_words(tab2_w[1], tab2_words, 1)
-        carry_scale_rows(1)
+        carry_scale_rows(v_sd, 0, 0, 0, range(QUADRANTS))
+        nc.vector.tensor_copy(v2_s[:], tab2_s[:].indirect(list2[:]))
+        nc.vector.memset(rows_of_pass[1][:].bitcast(I32), 0)
+        carry_scale_rows(v2_s, WIDE_ROW, V2_PLANE, 0, (0, 1))
+        load_word_half(1, 0)
+        carry_scale_rows(v2_s, WIDE_ROW, V2_PLANE, 0, (2, 3))
+        carry_scale_rows(v_sd, 0, 0, 1, range(QUADRANTS))
+        load_word_half(1, 1)
+        carry_scale_rows(v2_s, WIDE_ROW, V2_PLANE, 1, range(QUADRANTS))
         gather_v_words(0)
-        load_by_mode(hi_t, hi)
         nc.sync.dma_start(w4_w[:].bitcast(I32), w4_words.rearrange("a p b -> p a b").bitcast(I32))
         gather_v_words(1)
         for part, (g, n0) in enumerate(w1_parts):
             rows = w1[g * PASS : (g + 1) * PASS, n0 : n0 + W1_PART]
             nc.sync.dma_start(w1_raw[part][:], rows.rearrange("(p j) n -> p j n", j=PACK))
-        nc.vector.tensor_copy(v2_s[:], tab2_s[:].indirect(list2[:]))
         for a in range(PASSES):
             for half in range(HALVES):
                 gather_v2_words(a, half)
@@ -191,9 +195,9 @@ def tile_list_satellite_radiance_calibration_kernel(
             nc.tensor.matmul_mx(
                 sums[g, t, half][:],
                 lhsT=v_w[a][:, cols].bitcast(FP8X4),
-                lhsT_scale=v_s[a][:, cols],
+                lhsT_scale=rows_of_pass[a][:, cols],
                 rhs=v2_w[a][:, js].bitcast(FP8X4),
-                rhs_scale=v2_s[8 + 4 * a : P, js],
+                rhs_scale=rows_of_pass[a][V2_PLANE:P, js],
                 start=opens,
                 stop=not opens,
             )

@@ -54,22 +54,23 @@ def tile_list_satellite_radiance_calibration_kernel(
         list2 = held.tile([P, S2 // 16], U16, name="list2")
         w4_s = held.tile([P, PASSES, N], U8, name="w4_s", align_bytes=64)
         tab_s = held.tile([P, T], U8, name="tab_s", align_bytes=64)
-        v_sg = held.tile([P, S], U8, name="v_sg", align_bytes=64)
-        tab2_s = placed([P, T2], U8, "tab2_s", 53)
-        rows_of_pass = [held.tile([P, S], U8, name="rows0", align_bytes=64), placed([P, S], U8, "rows1", 56)]
-        tab_w = [placed([P, T], U32, f"tab_w{a}", 4 + 8 * a) for a in range(PASSES)]
-        tab2_w = [placed([P, T2], U32, f"tab2_w{a}", (23, 39)[a]) for a in range(PASSES)]
-        w4_sd = placed([P, PASSES * N], U8, "w4_sd", 39)
+        v_sg = placed([P, S], U8, "v_sg", 28)
+        v2_s = placed([P, S2], U8, "v2_s", 16.5)
+        tab2_s = placed([P, T2], U8, "tab2_s", 59)
+        rows_of_pass = [held.tile([P, S], U8, name=f"rows{a}", align_bytes=64) for a in range(PASSES)]
+        tab_w = [placed([P, T], U32, f"tab_w{a}", (4, 21)[a]) for a in range(PASSES)]
+        tab2_w = [placed([P, T2], U32, f"tab2_w{a}", (29, 45)[a]) for a in range(PASSES)]
+        w4_sd = placed([P, PASSES * N], U8, "w4_sd", 45)
         fields = [(half, g) for half in range(HALVES) for g in range(PASSES)]
-        c32 = {field: placed([P, PACK, BANK], F32, f"c32_{f}", (40, 48, 57, 73)[f]) for f, field in enumerate(fields)}
-        h32 = {field: placed([P, PACK, BANK], F32, f"h32_{f}", (23, 31, 65, 81)[f]) for f, field in enumerate(fields)}
-        y_q = [placed([P, BANK], U32, f"y_q{half}", 73 + 8 * half) for half in range(HALVES)]
+        c32 = {field: placed([P, PACK, BANK], F32, f"c32_{f}", (46, 54, 63, 79)[f]) for f, field in enumerate(fields)}
+        h32 = {field: placed([P, PACK, BANK], F32, f"h32_{f}", (29, 37, 71, 87)[f]) for f, field in enumerate(fields)}
+        y_q = [placed([P, BANK], U32, f"y_q{half}", 79 + 8 * half) for half in range(HALVES)]
         w1_parts = [(g, n0) for g in range(PASSES) for n0 in range(0, N, W1_PART)]
         w1_raw = [placed([P, PACK, W1_PART], F32, f"w1_raw{part}", 5 + 4 * part) for part in range(len(w1_parts))]
         w4_w = placed([P, PASSES, 2 * N], U8, "w4_w", 2.5)
-        lo_t = held.tile([P, PASSES, PACK], F32, name="lo_t")
-        hi_t = held.tile([P, PASSES, PACK], F32, name="hi_t")
-        gain_t = held.tile([P, PASSES, PACK], F32, name="gain_t")
+        lo_t = placed([P, PASSES, PACK], F32, "lo_t", 4.5)
+        hi_t = placed([P, PASSES, PACK], F32, "hi_t", 4.625)
+        gain_t = placed([P, PASSES, PACK], F32, "gain_t", 4.75)
 
         v_sd = held.tile([P, S], U8, name="v_sd", align_bytes=64)
 
@@ -77,7 +78,8 @@ def tile_list_satellite_radiance_calibration_kernel(
         nc.vector.memset(tab_s[32:64, :].bitcast(I32), 0)
         nc.vector.memset(tab_s[64:P, :].bitcast(I32), 0)
         nc.vector.memset(tab2_s[0:WIDE_ROW, :].bitcast(I32), 0)
-        nc.vector.memset(rows_of_pass[0][:].bitcast(I32), 0)
+        for a in range(PASSES):
+            nc.vector.memset(rows_of_pass[a][:].bitcast(I32), 0)
 
         def load_words(dst, words, a):
             nc.sync.dma_start(dst[:].bitcast(I32), words[a].rearrange("p t i -> p (t i)").bitcast(I32))
@@ -103,7 +105,6 @@ def tile_list_satellite_radiance_calibration_kernel(
             nc.sync.dma_start(tab2_w[a][:, cols].bitcast(I32), words[:, cols])
 
         v_w = [held.tile([P, S], U32, name=f"v_w{a}", align_bytes=64) for a in range(PASSES)]
-        v2_s = held.tile([P, S2], U8, name="v2_s", align_bytes=64)
         v2_w = [held.tile([P, S2], U32, name=f"v2_w{a}", align_bytes=64) for a in range(PASSES)]
         w4_wd = held.tile([P, PASSES * 2 * N], U8, name="w4_wd", align_bytes=64)
 
@@ -131,32 +132,31 @@ def tile_list_satellite_radiance_calibration_kernel(
         nc.sync.dma_start(tab2_s[WIDE_ROW:P, :].bitcast(I32), tab2_scales.rearrange("a r t -> (a r) t").bitcast(I32))
         for q in range(QUADRANTS):
             load_w4_scale_rows(q)
-        load_words(tab_w[1], tab_words, 1)
-        load_by_mode(gain_t, gain)
-        load_by_mode(lo_t, lo)
-        load_by_mode(hi_t, hi)
         load_words(tab2_w[0], tab2_words, 0)
 
         nc.vector.tensor_copy(v_sg[:], tab_s[:].indirect(list1[:]))
         deal(nc.vector.tensor_copy, v_sd[:], v_sg[:], 16)
         carry_scale_rows(v_sd, 0, 0, 0, range(QUADRANTS))
+        carry_scale_rows(v_sd, 0, 0, 1, (0, 1))
+        load_words(tab_w[1], tab_words, 1)
+        carry_scale_rows(v_sd, 0, 0, 1, (2, 3))
         nc.vector.tensor_copy(v2_s[:], tab2_s[:].indirect(list2[:]))
-        nc.vector.memset(rows_of_pass[1][:].bitcast(I32), 0)
-        carry_scale_rows(v2_s, WIDE_ROW, V2_PLANE, 0, (0, 1))
-        load_word_half(1, 0)
-        carry_scale_rows(v2_s, WIDE_ROW, V2_PLANE, 0, (2, 3))
-        carry_scale_rows(v_sd, 0, 0, 1, range(QUADRANTS))
-        load_word_half(1, 1)
-        carry_scale_rows(v2_s, WIDE_ROW, V2_PLANE, 1, range(QUADRANTS))
+        for a in range(PASSES):
+            carry_scale_rows(v2_s, WIDE_ROW, V2_PLANE, a, range(QUADRANTS))
+            load_word_half(1, a)
         gather_v_words(0)
+        load_by_mode(lo_t, lo)
+        load_by_mode(hi_t, hi)
+        load_by_mode(gain_t, gain)
         nc.sync.dma_start(w4_w[:].bitcast(I32), w4_words.rearrange("a p b -> p a b").bitcast(I32))
-        gather_v_words(1)
         for part, (g, n0) in enumerate(w1_parts):
             rows = w1[g * PASS : (g + 1) * PASS, n0 : n0 + W1_PART]
             nc.sync.dma_start(w1_raw[part][:], rows.rearrange("(p j) n -> p j n", j=PACK))
-        for a in range(PASSES):
-            for half in range(HALVES):
-                gather_v2_words(a, half)
+        for half in range(HALVES):
+            gather_v2_words(0, half)
+        gather_v_words(1)
+        for half in range(HALVES):
+            gather_v2_words(1, half)
 
         w1_b = held.tile([P, PASSES, N * PACK], BF16, name="w1_b", align_bytes=64)
         w1_q = held.tile([P, PASSES * N], U32, name="w1_q", align_bytes=64)
@@ -241,7 +241,7 @@ def tile_list_satellite_radiance_calibration_kernel(
 
         def weave_h2(c, g):
             slot = pieces.index((c, g)) % H2_SLOTS
-            rounded[c, g] = placed([P, CHUNKS[c] * PACK], BF16, f"h2_b{c}_{g}", 89 + 2 * slot)
+            rounded[c, g] = placed([P, CHUNKS[c] * PACK], BF16, f"h2_b{c}_{g}", 95 + 2 * slot)
             nc.vector.tensor_tensor(
                 woven(rounded[c, g][:]), signal(h32, g, starts[c], CHUNKS[c]), signal(c32, g, starts[c], CHUNKS[c]), ALU.mult
             )

@@ -53,8 +53,7 @@ def tile_list_satellite_radiance_calibration_kernel(
         list1 = held.tile([P, S // 16], U16, name="list1")
         list2 = held.tile([P, S2 // 16], U16, name="list2")
         w4_s = held.tile([P, PASSES, N], U8, name="w4_s", align_bytes=64)
-        tab_s = held.tile([P, T], U8, name="tab_s", align_bytes=64)
-        v_sg = placed([P, S], U8, "v_sg", 28)
+        tab_s = placed([P, T], U8, "tab_s", 27)
         v2_s = placed([P, S2], U8, "v2_s", 16.5)
         tab2_s = placed([P, T2], U8, "tab2_s", 59)
         rows_of_pass = [held.tile([P, S], U8, name=f"rows{a}", align_bytes=64) for a in range(PASSES)]
@@ -134,8 +133,9 @@ def tile_list_satellite_radiance_calibration_kernel(
             load_w4_scale_rows(q)
         load_words(tab2_w[0], tab2_words, 0)
 
-        nc.vector.tensor_copy(v_sg[:], tab_s[:].indirect(list1[:]))
-        deal(nc.vector.tensor_copy, v_sd[:], v_sg[:], 16)
+        nc.vector.tensor_copy(
+            v_sd[:].rearrange("p (g t m) -> p g m t", g=PASSES, t=PACK), tab_s[:].indirect(list1[:])
+        )
         carry_scale_rows(v_sd, 0, 0, 0, range(QUADRANTS))
         carry_scale_rows(v_sd, 0, 0, 1, (0, 1))
         load_words(tab_w[1], tab_words, 1)

@@ -24,11 +24,11 @@ QUADRANTS = 4
 BANK = 512
 HALVES = S2 // BANK
 CHUNKS = (256, 256, 128, 128, 128, 128)
-GPSIMD_SLICES = (3, 4, 3, 0)
-Y_WEAVES_ON_SCALAR = (0, 1, 2)
+GPSIMD_SLICES = (3, 4, 4, 0)
+Y_WEAVES_ON_SCALAR = (0, 1, 2, 3)
 H_RUNS = ((0, 0, 256), (1, 0, 256), (0, 256, 256), (1, 256, 256), (0, 512, 512), (1, 512, 512))
-H2_SLOTS = 3
-EARLY_RUNS = 2
+H2_SLOTS = 4
+EARLY_RUNS = 4
 W1_PART = 256
 CODE_STORES = ((0, 1), (2, 3, 4), (5,))
 KIB = 1024
@@ -59,11 +59,11 @@ def tile_list_satellite_radiance_calibration_kernel(
         rows_of_pass = [held.tile([P, S], U8, name=f"rows{a}", align_bytes=64) for a in range(PASSES)]
         tab_w = [placed([P, T], U32, f"tab_w{a}", (4, 21)[a]) for a in range(PASSES)]
         tab2_w = [placed([P, T2], U32, f"tab2_w{a}", (29, 45)[a]) for a in range(PASSES)]
-        w4_sd = placed([P, PASSES * N], U8, "w4_sd", 45)
+        w4_sd = held.tile([P, PASSES * N], U8, name="w4_sd", align_bytes=64)
         fields = [(half, g) for half in range(HALVES) for g in range(PASSES)]
-        c32 = {field: placed([P, PACK, BANK], F32, f"c32_{f}", (46, 54, 63, 79)[f]) for f, field in enumerate(fields)}
-        h32 = {field: placed([P, PACK, BANK], F32, f"h32_{f}", (29, 37, 71, 87)[f]) for f, field in enumerate(fields)}
-        y_q = [placed([P, BANK], U32, f"y_q{half}", 79 + 8 * half) for half in range(HALVES)]
+        c32 = {field: placed([P, PACK, BANK], F32, f"c32_{f}", (45, 53, 63, 79)[f]) for f, field in enumerate(fields)}
+        h32 = {field: placed([P, PACK, BANK], F32, f"h32_{f}", (29, 37, 71, 20.75)[f]) for f, field in enumerate(fields)}
+        y_q = [placed([P, BANK], U32, f"y_q{half}", (79, 20.75)[half]) for half in range(HALVES)]
         w1_parts = [(g, n0) for g in range(PASSES) for n0 in range(0, N, W1_PART)]
         w1_raw = [placed([P, PACK, W1_PART], F32, f"w1_raw{part}", 5 + 4 * part) for part in range(len(w1_parts))]
         w4_w = placed([P, PASSES, 2 * N], U8, "w4_w", 2.5)
@@ -155,12 +155,13 @@ def tile_list_satellite_radiance_calibration_kernel(
         for half in range(HALVES):
             gather_v2_words(0, half)
         gather_v_words(1)
+        deal(nc.vector.tensor_copy, w4_sd[:], w4_s[:].rearrange("p a n -> p (a n)"), 16)
         for half in range(HALVES):
             gather_v2_words(1, half)
 
         w1_b = held.tile([P, PASSES, N * PACK], BF16, name="w1_b", align_bytes=64)
         w1_q = held.tile([P, PASSES * N], U32, name="w1_q", align_bytes=64)
-        w1_s = held.tile([P, PASSES * N], U8, name="w1_s", align_bytes=64)
+        w1_s = placed([P, PASSES * N], U8, "w1_s", 15.25)
         y_s = held.tile([P, S2], U8, name="y_s", align_bytes=64)
 
         def round_w1(part):
@@ -222,11 +223,12 @@ def tile_list_satellite_radiance_calibration_kernel(
         h_b = []
         for run, (g, first, width) in enumerate(H_RUNS):
             if run < EARLY_RUNS:
-                h_b.append(placed([P, width * PACK], BF16, f"h_b{run}", 17 - 4 * run))
+                h_b.append(placed([P, width * PACK], BF16, f"h_b{run}", (15, 19, 95, 97)[run]))
             else:
                 h_b.append(held.tile([P, width * PACK], BF16, name=f"h_b{run}", align_bytes=64))
         h_q = [held.tile([P, run[2]], U32, name=f"h_q{k}", align_bytes=64) for k, run in enumerate(H_RUNS)]
-        h_s = [held.tile([P, run[2]], U8, name=f"h_s{k}", align_bytes=64) for k, run in enumerate(H_RUNS)]
+        h_s = [placed([P, H_RUNS[0][2]], U8, "h_s0", 19)]
+        h_s.extend(held.tile([P, H_RUNS[k][2]], U8, name=f"h_s{k}", align_bytes=64) for k in range(1, len(H_RUNS)))
 
         def run_of(c, g):
             return [
@@ -241,7 +243,7 @@ def tile_list_satellite_radiance_calibration_kernel(
 
         def weave_h2(c, g):
             slot = pieces.index((c, g)) % H2_SLOTS
-            rounded[c, g] = placed([P, CHUNKS[c] * PACK], BF16, f"h2_b{c}_{g}", 95 + 2 * slot)
+            rounded[c, g] = placed([P, CHUNKS[c] * PACK], BF16, f"h2_b{c}_{g}", (13.25, 16.25, 95, 97)[slot])
             nc.vector.tensor_tensor(
                 woven(rounded[c, g][:]), signal(h32, g, starts[c], CHUNKS[c]), signal(c32, g, starts[c], CHUNKS[c]), ALU.mult
             )
@@ -258,9 +260,8 @@ def tile_list_satellite_radiance_calibration_kernel(
                 return [(0, 1), (2, 3)]
             return [(0, 1, 2, 3)]
 
-        def second_passes(c, g):
+        def linear_passes(c, g):
             w = CHUNKS[c]
-            codes, scales = quantised[c, g]
             run = run_of(c, g)
             js = slice(starts[c] - H_RUNS[run][1], starts[c] - H_RUNS[run][1] + w)
             if g == 0:
@@ -278,6 +279,9 @@ def tile_list_satellite_radiance_calibration_kernel(
                         start=(g == 0 and s == 0),
                         stop=False,
                     )
+
+        def quadratic_passes(c, g):
+            codes, scales = quantised[c, g]
             for bank, slices in enumerate(bank_slices(c)):
                 for s, t in enumerate(slices):
                     n0 = g * N + t * P
@@ -327,11 +331,6 @@ def tile_list_satellite_radiance_calibration_kernel(
         for part in range(len(w1_parts)):
             round_w1(part)
 
-        nc.gpsimd.tensor_copy(
-            w4_sd[:].rearrange("p (g t m) -> p g t m", g=PASSES, t=PACK),
-            w4_s[:].rearrange("p g (m t) -> p g t m", t=PACK),
-        )
-
         for a in range(PASSES):
             for g in range(PASSES):
                 for t in range(PACK):
@@ -349,21 +348,20 @@ def tile_list_satellite_radiance_calibration_kernel(
 
         for run in range(EARLY_RUNS, len(H_RUNS)):
             weave_h(run)
-        for step in range(len(pieces) + 1):
-            if step < len(pieces):
-                weave_h2(*pieces[step])
-            if step == 0:
-                quantise_w1()
-            if step >= 1:
-                c, g = pieces[step - 1]
-                if starts[c] == H_RUNS[run_of(c, g)][1]:
+        quantise_h(1)
+        quantise_w1()
+        for c in range(len(CHUNKS)):
+            for g in range(PASSES):
+                if starts[c] == H_RUNS[run_of(c, g)][1] and (c, g) != (0, 1):
                     quantise_h(run_of(c, g))
+                linear_passes(c, g)
+                weave_h2(c, g)
+            for g in range(PASSES):
                 quantise_h2(c, g)
-                second_passes(c, g)
-                if g == PASSES - 1:
-                    hand_out(c)
-                    if c in Y_WEAVES_ON_SCALAR:
-                        weave_y(c)
+                quadratic_passes(c, g)
+            hand_out(c)
+            if c in Y_WEAVES_ON_SCALAR:
+                weave_y(c)
 
         for group in CODE_STORES:
             planes(group)

@@ -24,7 +24,7 @@ QUADRANTS = 4
 BANK = 512
 HALVES = S2 // BANK
 CHUNKS = (256, 256, 128, 128, 128, 128)
-GPSIMD_SLICES = (3, 4, 4, 0)
+GPSIMD_SLICES = (3, 3, 4, 0)
 Y_WEAVES_ON_SCALAR = (0, 1, 2, 3)
 H_RUNS = ((0, 0, 256), (1, 0, 256), (0, 256, 256), (1, 256, 256), (0, 512, 512), (1, 512, 512))
 H2_SLOTS = 4
@@ -59,9 +59,9 @@ def tile_list_satellite_radiance_calibration_kernel(
         rows_of_pass = [held.tile([P, S], U8, name=f"rows{a}", align_bytes=64) for a in range(PASSES)]
         tab_w = [placed([P, T], U32, f"tab_w{a}", (4, 21)[a]) for a in range(PASSES)]
         tab2_w = [placed([P, T2], U32, f"tab2_w{a}", (29, 45)[a]) for a in range(PASSES)]
-        w4_sd = held.tile([P, PASSES * N], U8, name="w4_sd", align_bytes=64)
+        w4_sd = placed([P, PASSES * N], U8, "w4_sd", 45)
         fields = [(half, g) for half in range(HALVES) for g in range(PASSES)]
-        c32 = {field: placed([P, PACK, BANK], F32, f"c32_{f}", (45, 53, 63, 79)[f]) for f, field in enumerate(fields)}
+        c32 = {field: placed([P, PACK, BANK], F32, f"c32_{f}", (46, 54, 63, 79)[f]) for f, field in enumerate(fields)}
         h32 = {field: placed([P, PACK, BANK], F32, f"h32_{f}", (29, 37, 71, 20.75)[f]) for f, field in enumerate(fields)}
         y_q = [placed([P, BANK], U32, f"y_q{half}", (79, 20.75)[half]) for half in range(HALVES)]
         w1_parts = [(g, n0) for g in range(PASSES) for n0 in range(0, N, W1_PART)]
@@ -155,7 +155,6 @@ def tile_list_satellite_radiance_calibration_kernel(
         for half in range(HALVES):
             gather_v2_words(0, half)
         gather_v_words(1)
-        deal(nc.vector.tensor_copy, w4_sd[:], w4_s[:].rearrange("p a n -> p (a n)"), 16)
         for half in range(HALVES):
             gather_v2_words(1, half)
 
@@ -330,6 +329,11 @@ def tile_list_satellite_radiance_calibration_kernel(
         deal(nc.scalar.copy, w4_wd[:].bitcast(U16), w4_w[:].rearrange("p a b -> p (a b)").bitcast(U16), 8)
         for part in range(len(w1_parts)):
             round_w1(part)
+
+        nc.gpsimd.tensor_copy(
+            w4_sd[:].rearrange("p (g t m) -> p g t m", g=PASSES, t=PACK),
+            w4_s[:].rearrange("p g (m t) -> p g t m", t=PACK),
+        )
 
         for a in range(PASSES):
             for g in range(PASSES):

@@ -56,7 +56,8 @@ def tile_list_satellite_radiance_calibration_kernel(
         tab_s = placed([P, T], U8, "tab_s", 27)
         v2_s = placed([P, S2], U8, "v2_s", 16.5)
         tab2_s = placed([P, T2], U8, "tab2_s", 59)
-        rows_of_pass = [held.tile([P, S], U8, name=f"rows{a}", align_bytes=64) for a in range(PASSES)]
+        rows = held.tile([P, PASSES * S], U8, name="rows", align_bytes=64)
+        rows_of_pass = [rows[:, a * S : (a + 1) * S] for a in range(PASSES)]
         tab_w = [placed([P, T], U32, f"tab_w{a}", (4, 21)[a]) for a in range(PASSES)]
         tab2_w = [placed([P, T2], U32, f"tab2_w{a}", (29, 45)[a]) for a in range(PASSES)]
         w4_sd = placed([P, PASSES * N], U8, "w4_sd", 45)
@@ -74,11 +75,9 @@ def tile_list_satellite_radiance_calibration_kernel(
         v_sd = held.tile([P, S], U8, name="v_sd", align_bytes=64)
 
         nc.vector.memset(w4_s[:].rearrange("p a n -> p (a n)").bitcast(I32), 0)
-        nc.vector.memset(tab_s[32:64, :].bitcast(I32), 0)
-        nc.vector.memset(tab_s[64:P, :].bitcast(I32), 0)
-        nc.vector.memset(tab2_s[0:WIDE_ROW, :].bitcast(I32), 0)
-        for a in range(PASSES):
-            nc.vector.memset(rows_of_pass[a][:].bitcast(I32), 0)
+        nc.vector.memset(tab2_s[:].bitcast(I32), 0)
+        nc.vector.memset(tab_s[0:WIDE_ROW, :].bitcast(I32), 0)
+        nc.vector.memset(rows[:].bitcast(I32), 0)
 
         def load_words(dst, words, a):
             nc.sync.dma_start(dst[:].bitcast(I32), words[a].rearrange("p t i -> p (t i)").bitcast(I32))
@@ -92,11 +91,11 @@ def tile_list_satellite_radiance_calibration_kernel(
                 w4_scales[:, 4 * q : 4 * q + 4, :].rearrange("a r n -> r a n").bitcast(I32),
             )
 
-        def carry_scale_rows(gathered, first_row, plane, a, quadrants):
+        def carry_scale_rows(gathered, first_row, step, plane, a, quadrants):
             for q in quadrants:
-                row = first_row + 16 * a + 4 * q
+                row = first_row + step * (16 * a + 4 * q)
                 dst = rows_of_pass[a][32 * q + plane : 32 * q + plane + 4, :]
-                nc.sync.dma_start(dst.bitcast(I32), gathered[row : row + 4, :].bitcast(I32))
+                nc.sync.dma_start(dst.bitcast(I32), gathered[row : row + 4 * step : step, :].bitcast(I32))
 
         def load_word_half(a, half):
             cols = slice(half * T2 // 2, (half + 1) * T2 // 2)
@@ -124,25 +123,25 @@ def tile_list_satellite_radiance_calibration_kernel(
                 tab2_w[a][:].indirect(list2[:, half * BANK // 16 : (half + 1) * BANK // 16]),
             )
 
-        nc.sync.dma_start(tab_s[0:32, :].bitcast(I32), tab_scales.rearrange("a r t -> (a r) t").bitcast(I32))
+        nc.sync.dma_start(tab_s[WIDE_ROW:P, :].bitcast(I32), tab_scales.rearrange("a r t -> (a r) t").bitcast(I32))
         nc.sync.dma_start(list1[:], offs)
         load_words(tab_w[0], tab_words, 0)
         nc.sync.dma_start(list2[:], offs2)
-        nc.sync.dma_start(tab2_s[WIDE_ROW:P, :].bitcast(I32), tab2_scales.rearrange("a r t -> (a r) t").bitcast(I32))
         for q in range(QUADRANTS):
             load_w4_scale_rows(q)
+        nc.sync.dma_start(tab2_s[0:P:4, :].bitcast(I32), tab2_scales.rearrange("a r t -> (a r) t").bitcast(I32))
         load_words(tab2_w[0], tab2_words, 0)
 
         nc.vector.tensor_copy(
             v_sd[:].rearrange("p (g t m) -> p g m t", g=PASSES, t=PACK), tab_s[:].indirect(list1[:])
         )
-        carry_scale_rows(v_sd, 0, 0, 0, range(QUADRANTS))
-        carry_scale_rows(v_sd, 0, 0, 1, (0, 1))
+        carry_scale_rows(v_sd, WIDE_ROW, 1, 0, 0, range(QUADRANTS))
+        carry_scale_rows(v_sd, WIDE_ROW, 1, 0, 1, (0, 1))
         load_words(tab_w[1], tab_words, 1)
-        carry_scale_rows(v_sd, 0, 0, 1, (2, 3))
+        carry_scale_rows(v_sd, WIDE_ROW, 1, 0, 1, (2, 3))
         nc.vector.tensor_copy(v2_s[:], tab2_s[:].indirect(list2[:]))
         for a in range(PASSES):
-            carry_scale_rows(v2_s, WIDE_ROW, V2_PLANE, a, range(QUADRANTS))
+            carry_scale_rows(v2_s, 0, 4, V2_PLANE, a, range(QUADRANTS))
             load_word_half(1, a)
         gather_v_words(0)
         load_by_mode(lo_t, lo)
@@ -150,8 +149,8 @@ def tile_list_satellite_radiance_calibration_kernel(
         load_by_mode(gain_t, gain)
         nc.sync.dma_start(w4_w[:].bitcast(I32), w4_words.rearrange("a p b -> p a b").bitcast(I32))
         for part, (g, n0) in enumerate(w1_parts):
-            rows = w1[g * PASS : (g + 1) * PASS, n0 : n0 + W1_PART]
-            nc.sync.dma_start(w1_raw[part][:], rows.rearrange("(p j) n -> p j n", j=PACK))
+            part_rows = w1[g * PASS : (g + 1) * PASS, n0 : n0 + W1_PART]
+            nc.sync.dma_start(w1_raw[part][:], part_rows.rearrange("(p j) n -> p j n", j=PACK))
         for half in range(HALVES):
             gather_v2_words(0, half)
         gather_v_words(1)

@@ -24,7 +24,7 @@ QUADRANTS = 4
 BANK = 512
 HALVES = S2 // BANK
 CHUNKS = (256, 256, 128, 128, 128, 128)
-GPSIMD_SLICES = (3, 3, 4, 0)
+GPSIMD_SLICES = (3, 4, 4, 0)
 Y_WEAVES_ON_SCALAR = (0, 1, 2, 3)
 H_RUNS = ((0, 0, 256), (1, 0, 256), (0, 256, 256), (1, 256, 256), (0, 512, 512), (1, 512, 512))
 H2_SLOTS = 4
@@ -60,9 +60,9 @@ def tile_list_satellite_radiance_calibration_kernel(
         rows_of_pass = [rows[:, a * S : (a + 1) * S] for a in range(PASSES)]
         tab_w = [placed([P, T], U32, f"tab_w{a}", (4, 21)[a]) for a in range(PASSES)]
         tab2_w = [placed([P, T2], U32, f"tab2_w{a}", (29, 45)[a]) for a in range(PASSES)]
-        w4_sd = placed([P, PASSES * N], U8, "w4_sd", 45)
+        w4_sd = held.tile([P, PASSES * N], U8, name="w4_sd", align_bytes=64)
         fields = [(half, g) for half in range(HALVES) for g in range(PASSES)]
-        c32 = {field: placed([P, PACK, BANK], F32, f"c32_{f}", (46, 54, 63, 79)[f]) for f, field in enumerate(fields)}
+        c32 = {field: placed([P, PACK, BANK], F32, f"c32_{f}", (45, 53, 63, 79)[f]) for f, field in enumerate(fields)}
         h32 = {field: placed([P, PACK, BANK], F32, f"h32_{f}", (29, 37, 71, 20.75)[f]) for f, field in enumerate(fields)}
         y_q = [placed([P, BANK], U32, f"y_q{half}", (79, 20.75)[half]) for half in range(HALVES)]
         w1_parts = [(g, n0) for g in range(PASSES) for n0 in range(0, N, W1_PART)]
@@ -315,9 +315,8 @@ def tile_list_satellite_radiance_calibration_kernel(
         out_words = out_1[0].rearrange("p m t -> p (m t)").bitcast(I32)
 
         def planes(group):
-            for c in group:
-                if c not in Y_WEAVES_ON_SCALAR:
-                    weave_y(c)
+            if last in group:
+                weave_y(last)
             js = slice(starts[group[0]], starts[group[-1]] + CHUNKS[group[-1]])
             half = js.start // BANK
             codes = y_q[half][:, js.start - half * BANK : js.stop - half * BANK]
@@ -366,6 +365,9 @@ def tile_list_satellite_radiance_calibration_kernel(
             if c in Y_WEAVES_ON_SCALAR:
                 weave_y(c)
 
+        for c in range(last):
+            if c not in Y_WEAVES_ON_SCALAR:
+                weave_y(c)
         for group in CODE_STORES:
             planes(group)
 

@@ -24,7 +24,7 @@ QUADRANTS = 4
 BANK = 512
 HALVES = S2 // BANK
 CHUNKS = (256, 256, 128, 128, 128, 128)
-GPSIMD_SLICES = (3, 4, 4, 0)
+GPSIMD_SLICES = (3, 3, 4, 0)
 Y_WEAVES_ON_SCALAR = (0, 1, 2, 3)
 H_RUNS = ((0, 0, 256), (1, 0, 256), (0, 256, 256), (1, 256, 256), (0, 512, 512), (1, 512, 512))
 H2_SLOTS = 4
@@ -32,8 +32,7 @@ EARLY_RUNS = 4
 W1_PART = 256
 CODE_STORES = ((0, 1), (2, 3, 4), (5,))
 KIB = 1024
-WIDE_ROW = 96
-V2_PLANE = 8
+LEAD = T // 4
 
 
 def tile_list_satellite_radiance_calibration_kernel(
@@ -53,11 +52,11 @@ def tile_list_satellite_radiance_calibration_kernel(
         list1 = held.tile([P, S // 16], U16, name="list1")
         list2 = held.tile([P, S2 // 16], U16, name="list2")
         w4_s = held.tile([P, PASSES, N], U8, name="w4_s", align_bytes=64)
-        tab_s = placed([P, T], U8, "tab_s", 27)
-        v2_s = placed([P, S2], U8, "v2_s", 16.5)
+        tab_s = held.tile([P, T], U8, name="tab_s", align_bytes=64)
+        picked = placed([P, S + S2], U8, "picked", 16)
         tab2_s = placed([P, T2], U8, "tab2_s", 59)
-        rows = held.tile([P, PASSES * S], U8, name="rows", align_bytes=64)
-        rows_of_pass = [rows[:, a * S : (a + 1) * S] for a in range(PASSES)]
+        rows = held.tile([P, PASSES * (S + S2)], U8, name="rows", align_bytes=64)
+        rows_of_pass = [rows[:, a * (S + S2) : (a + 1) * (S + S2)] for a in range(PASSES)]
         tab_w = [placed([P, T], U32, f"tab_w{a}", (4, 21)[a]) for a in range(PASSES)]
         tab2_w = [placed([P, T2], U32, f"tab2_w{a}", (29, 45)[a]) for a in range(PASSES)]
         w4_sd = held.tile([P, PASSES * N], U8, name="w4_sd", align_bytes=64)
@@ -72,11 +71,9 @@ def tile_list_satellite_radiance_calibration_kernel(
         hi_t = placed([P, PASSES, PACK], F32, "hi_t", 4.625)
         gain_t = placed([P, PASSES, PACK], F32, "gain_t", 4.75)
 
-        v_sd = held.tile([P, S], U8, name="v_sd", align_bytes=64)
-
+        nc.vector.memset(tab_s[:].bitcast(I32), 0)
         nc.vector.memset(w4_s[:].rearrange("p a n -> p (a n)").bitcast(I32), 0)
         nc.vector.memset(tab2_s[:].bitcast(I32), 0)
-        nc.vector.memset(tab_s[0:WIDE_ROW, :].bitcast(I32), 0)
         nc.vector.memset(rows[:].bitcast(I32), 0)
 
         def load_words(dst, words, a):
@@ -91,16 +88,15 @@ def tile_list_satellite_radiance_calibration_kernel(
                 w4_scales[:, 4 * q : 4 * q + 4, :].rearrange("a r n -> r a n").bitcast(I32),
             )
 
-        def carry_scale_rows(gathered, first_row, step, plane, a, quadrants):
-            for q in quadrants:
-                row = first_row + step * (16 * a + 4 * q)
-                dst = rows_of_pass[a][32 * q + plane : 32 * q + plane + 4, :]
-                nc.sync.dma_start(dst.bitcast(I32), gathered[row : row + 4 * step : step, :].bitcast(I32))
+        def carry_scale_rows(a):
+            for q in range(QUADRANTS):
+                row = 4 * (16 * a + 4 * q)
+                dst = rows_of_pass[a][32 * q : 32 * q + 4, :]
+                nc.sync.dma_start(dst.bitcast(I32), picked[row : row + 16 : 4, :].bitcast(I32))
 
-        def load_word_half(a, half):
-            cols = slice(half * T2 // 2, (half + 1) * T2 // 2)
-            words = tab2_words[a].rearrange("p t i -> p (t i)").bitcast(I32)
-            nc.sync.dma_start(tab2_w[a][:, cols].bitcast(I32), words[:, cols])
+        def load_first_words(cols):
+            words = tab_words[0].rearrange("p t i -> p (t i)").bitcast(I32)
+            nc.sync.dma_start(tab_w[0][:, cols].bitcast(I32), words[:, cols])
 
         v_w = [held.tile([P, S], U32, name=f"v_w{a}", align_bytes=64) for a in range(PASSES)]
         v2_w = [held.tile([P, S2], U32, name=f"v2_w{a}", align_bytes=64) for a in range(PASSES)]
@@ -123,31 +119,29 @@ def tile_list_satellite_radiance_calibration_kernel(
                 tab2_w[a][:].indirect(list2[:, half * BANK // 16 : (half + 1) * BANK // 16]),
             )
 
-        nc.sync.dma_start(tab_s[WIDE_ROW:P, :].bitcast(I32), tab_scales.rearrange("a r t -> (a r) t").bitcast(I32))
+        load_first_words(slice(0, LEAD))
         nc.sync.dma_start(list1[:], offs)
-        load_words(tab_w[0], tab_words, 0)
         nc.sync.dma_start(list2[:], offs2)
+        nc.sync.dma_start(tab_s[0:P:4, :].bitcast(I32), tab_scales.rearrange("a r t -> (a r) t").bitcast(I32))
+        load_first_words(slice(LEAD, T))
         for q in range(QUADRANTS):
             load_w4_scale_rows(q)
         nc.sync.dma_start(tab2_s[0:P:4, :].bitcast(I32), tab2_scales.rearrange("a r t -> (a r) t").bitcast(I32))
         load_words(tab2_w[0], tab2_words, 0)
+        load_words(tab_w[1], tab_words, 1)
 
         nc.vector.tensor_copy(
-            v_sd[:].rearrange("p (g t m) -> p g m t", g=PASSES, t=PACK), tab_s[:].indirect(list1[:])
+            picked[:, :S].rearrange("p (g t m) -> p g m t", g=PASSES, t=PACK), tab_s[:].indirect(list1[:])
         )
-        carry_scale_rows(v_sd, WIDE_ROW, 1, 0, 0, range(QUADRANTS))
-        carry_scale_rows(v_sd, WIDE_ROW, 1, 0, 1, (0, 1))
-        load_words(tab_w[1], tab_words, 1)
-        carry_scale_rows(v_sd, WIDE_ROW, 1, 0, 1, (2, 3))
-        nc.vector.tensor_copy(v2_s[:], tab2_s[:].indirect(list2[:]))
-        for a in range(PASSES):
-            carry_scale_rows(v2_s, 0, 4, V2_PLANE, a, range(QUADRANTS))
-            load_word_half(1, a)
+        nc.vector.tensor_copy(picked[:, S:], tab2_s[:].indirect(list2[:]))
+        carry_scale_rows(0)
+        load_words(tab2_w[1], tab2_words, 1)
+        carry_scale_rows(1)
         gather_v_words(0)
         load_by_mode(lo_t, lo)
         load_by_mode(hi_t, hi)
-        load_by_mode(gain_t, gain)
         nc.sync.dma_start(w4_w[:].bitcast(I32), w4_words.rearrange("a p b -> p a b").bitcast(I32))
+        load_by_mode(gain_t, gain)
         for part, (g, n0) in enumerate(w1_parts):
             part_rows = w1[g * PASS : (g + 1) * PASS, n0 : n0 + W1_PART]
             nc.sync.dma_start(w1_raw[part][:], part_rows.rearrange("(p j) n -> p j n", j=PACK))
@@ -196,7 +190,7 @@ def tile_list_satellite_radiance_calibration_kernel(
                 lhsT=v_w[a][:, cols].bitcast(FP8X4),
                 lhsT_scale=rows_of_pass[a][:, cols],
                 rhs=v2_w[a][:, js].bitcast(FP8X4),
-                rhs_scale=rows_of_pass[a][V2_PLANE:P, js],
+                rhs_scale=rows_of_pass[a][:, S + js.start : S + js.stop],
                 start=opens,
                 stop=not opens,
             )

@@ -67,8 +67,8 @@ def tile_list_satellite_radiance_calibration_kernel(
         w1_parts = [(g, n0) for g in range(PASSES) for n0 in range(0, N, W1_PART)]
         w1_raw = [placed([P, PACK, W1_PART], F32, f"w1_raw{part}", 5 + 4 * part) for part in range(len(w1_parts))]
         w4_w = placed([P, PASSES, 2 * N], U8, "w4_w", 2.5)
-        lo_t = placed([P, PASSES, PACK], F32, "lo_t", 4.5)
-        hi_t = placed([P, PASSES, PACK], F32, "hi_t", 4.625)
+        lo_t = held.tile([P, PASSES, PACK], F32, name="lo_t")
+        hi_t = held.tile([P, PASSES, PACK], F32, name="hi_t")
         gain_t = placed([P, PASSES, PACK], F32, "gain_t", 4.75)
 
         nc.vector.memset(tab_s[:].bitcast(I32), 0)
@@ -129,6 +129,8 @@ def tile_list_satellite_radiance_calibration_kernel(
         nc.sync.dma_start(tab2_s[0:P:4, :].bitcast(I32), tab2_scales.rearrange("a r t -> (a r) t").bitcast(I32))
         load_words(tab2_w[0], tab2_words, 0)
         load_words(tab_w[1], tab_words, 1)
+        load_by_mode(lo_t, lo)
+        load_by_mode(hi_t, hi)
 
         nc.vector.tensor_copy(
             picked[:, :S].rearrange("p (g t m) -> p g m t", g=PASSES, t=PACK), tab_s[:].indirect(list1[:])
@@ -138,10 +140,8 @@ def tile_list_satellite_radiance_calibration_kernel(
         load_words(tab2_w[1], tab2_words, 1)
         carry_scale_rows(1)
         gather_v_words(0)
-        load_by_mode(lo_t, lo)
-        load_by_mode(hi_t, hi)
-        nc.sync.dma_start(w4_w[:].bitcast(I32), w4_words.rearrange("a p b -> p a b").bitcast(I32))
         load_by_mode(gain_t, gain)
+        nc.sync.dma_start(w4_w[:].bitcast(I32), w4_words.rearrange("a p b -> p a b").bitcast(I32))
         for part, (g, n0) in enumerate(w1_parts):
             part_rows = w1[g * PASS : (g + 1) * PASS, n0 : n0 + W1_PART]
             nc.sync.dma_start(w1_raw[part][:], part_rows.rearrange("(p j) n -> p j n", j=PACK))
@@ -151,9 +151,9 @@ def tile_list_satellite_radiance_calibration_kernel(
         for half in range(HALVES):
             gather_v2_words(1, half)
 
-        w1_b = held.tile([P, PASSES, N * PACK], BF16, name="w1_b", align_bytes=64)
+        w1_b = placed([P, PASSES, N * PACK], BF16, "w1_b", 99)
         w1_q = held.tile([P, PASSES * N], U32, name="w1_q", align_bytes=64)
-        w1_s = placed([P, PASSES * N], U8, "w1_s", 15.25)
+        w1_s = placed([P, PASSES * N], U8, "w1_s", 19.25)
         y_s = held.tile([P, S2], U8, name="y_s", align_bytes=64)
 
         def round_w1(part):
@@ -219,8 +219,7 @@ def tile_list_satellite_radiance_calibration_kernel(
             else:
                 h_b.append(held.tile([P, width * PACK], BF16, name=f"h_b{run}", align_bytes=64))
         h_q = [held.tile([P, run[2]], U32, name=f"h_q{k}", align_bytes=64) for k, run in enumerate(H_RUNS)]
-        h_s = [placed([P, H_RUNS[0][2]], U8, "h_s0", 19)]
-        h_s.extend(held.tile([P, H_RUNS[k][2]], U8, name=f"h_s{k}", align_bytes=64) for k in range(1, len(H_RUNS)))
+        h_s = [held.tile([P, run[2]], U8, name=f"h_s{k}", align_bytes=64) for k, run in enumerate(H_RUNS)]
 
         def run_of(c, g):
             return [
@@ -235,7 +234,7 @@ def tile_list_satellite_radiance_calibration_kernel(
 
         def weave_h2(c, g):
             slot = pieces.index((c, g)) % H2_SLOTS
-            rounded[c, g] = placed([P, CHUNKS[c] * PACK], BF16, f"h2_b{c}_{g}", (13.25, 16.25, 95, 97)[slot])
+            rounded[c, g] = placed([P, CHUNKS[c] * PACK], BF16, f"h2_b{c}_{g}", (17.25, 99, 101, 97)[slot])
             nc.vector.tensor_tensor(
                 woven(rounded[c, g][:]), signal(h32, g, starts[c], CHUNKS[c]), signal(c32, g, starts[c], CHUNKS[c]), ALU.mult
             )
@@ -344,11 +343,12 @@ def tile_list_satellite_radiance_calibration_kernel(
 
         for run in range(EARLY_RUNS, len(H_RUNS)):
             weave_h(run)
-        quantise_h(1)
+        for run in (0, 2, 1):
+            quantise_h(run)
         quantise_w1()
         for c in range(len(CHUNKS)):
             for g in range(PASSES):
-                if starts[c] == H_RUNS[run_of(c, g)][1] and (c, g) != (0, 1):
+                if starts[c] == H_RUNS[run_of(c, g)][1] and run_of(c, g) > 2:
                     quantise_h(run_of(c, g))
                 linear_passes(c, g)
                 weave_h2(c, g)

@@ -32,6 +32,8 @@ EARLY_RUNS = 4
 W1_PART = 256
 CODE_STORES = ((0, 1), (2, 3, 4), (5,))
 KIB = 1024
+SCALAR_WALK = 2
+VECTOR_WALK = 4
 LEAD = T // 4
 
 
@@ -165,11 +167,11 @@ def tile_list_satellite_radiance_calibration_kernel(
         def quantise_w1():
             nc.vector.quantize_mx(w1_q[:].bitcast(FP8X4), w1_s[:], w1_b[:].rearrange("p g n -> p (g n)"))
 
-        def woven(ap):
-            return ap.rearrange("p (b i t) -> p b t i", i=4, t=PACK)
+        def woven(ap, walk):
+            return ap.rearrange("p (b i t) -> p b t i", i=walk, t=PACK)
 
-        def by_fours(ap):
-            return ap.rearrange("p t (b i) -> p b t i", i=4)
+        def by_rows(ap, walk):
+            return ap.rearrange("p t (b i) -> p b t i", i=walk)
 
         last = len(CHUNKS) - 1
         starts = [sum(CHUNKS[:c]) for c in range(len(CHUNKS))]
@@ -209,8 +211,8 @@ def tile_list_satellite_radiance_calibration_kernel(
             else:
                 nc.scalar.activation(h_row, c_row, ACT.Copy, scale=gain_t[:, g, t : t + 1])
 
-        def signal(tiles, g, first, width):
-            return by_fours(tiles[first // BANK, g][:, :, first % BANK : first % BANK + width])
+        def signal(tiles, g, first, width, walk):
+            return by_rows(tiles[first // BANK, g][:, :, first % BANK : first % BANK + width], walk)
 
         h_b = []
         for run, (g, first, width) in enumerate(H_RUNS):
@@ -227,7 +229,7 @@ def tile_list_satellite_radiance_calibration_kernel(
             ][0]
 
         def weave_h(run):
-            nc.scalar.copy(woven(h_b[run][:]), signal(h32, *H_RUNS[run]))
+            nc.scalar.copy(woven(h_b[run][:], SCALAR_WALK), signal(h32, *H_RUNS[run], SCALAR_WALK))
 
         def quantise_h(run):
             nc.vector.quantize_mx(h_q[run][:].bitcast(FP8X4), h_s[run][:], h_b[run][:])
@@ -236,7 +238,10 @@ def tile_list_satellite_radiance_calibration_kernel(
             slot = pieces.index((c, g)) % H2_SLOTS
             rounded[c, g] = placed([P, CHUNKS[c] * PACK], BF16, f"h2_b{c}_{g}", (17.25, 99, 101, 97)[slot])
             nc.vector.tensor_tensor(
-                woven(rounded[c, g][:]), signal(h32, g, starts[c], CHUNKS[c]), signal(c32, g, starts[c], CHUNKS[c]), ALU.mult
+                woven(rounded[c, g][:], VECTOR_WALK),
+                signal(h32, g, starts[c], CHUNKS[c], VECTOR_WALK),
+                signal(c32, g, starts[c], CHUNKS[c], VECTOR_WALK),
+                ALU.mult,
             )
 
         def quantise_h2(c, g):
@@ -299,11 +304,11 @@ def tile_list_satellite_radiance_calibration_kernel(
         y_b = held.tile([P, S2 * PACK], BF16, name="y_b", align_bytes=64)
 
         def weave_y(c):
-            dst = woven(y_b[:, starts[c] * PACK : (starts[c] + CHUNKS[c]) * PACK])
+            dst = y_b[:, starts[c] * PACK : (starts[c] + CHUNKS[c]) * PACK]
             if c in Y_WEAVES_ON_SCALAR:
-                nc.scalar.copy(dst, by_fours(results[c][:]))
+                nc.scalar.copy(woven(dst, SCALAR_WALK), by_rows(results[c][:], SCALAR_WALK))
             else:
-                nc.vector.tensor_copy(dst, by_fours(results[c][:]))
+                nc.vector.tensor_copy(woven(dst, VECTOR_WALK), by_rows(results[c][:], VECTOR_WALK))
 
         out_words = out_1[0].rearrange("p m t -> p (m t)").bitcast(I32)
 

@@ -26,15 +26,13 @@ HALVES = S2 // BANK
 CHUNKS = (256, 256, 128, 128, 128, 128)
 GPSIMD_SLICES = (3, 3, 4, 0)
 Y_WEAVES_ON_SCALAR = (0, 1, 2, 3)
-H_RUNS = ((0, 0, 256), (1, 0, 256), (0, 256, 256), (1, 256, 256), (0, 512, 512), (1, 512, 512))
 H2_SLOTS = 4
-EARLY_RUNS = 4
 W1_PART = 256
 CODE_STORES = ((0, 1), (2, 3, 4), (5,))
 KIB = 1024
+ROW_ALIGN = 256
 SCALAR_WALK = 2
 VECTOR_WALK = 4
-LEAD = T // 4
 
 
 def tile_list_satellite_radiance_calibration_kernel(
@@ -43,52 +41,58 @@ def tile_list_satellite_radiance_calibration_kernel(
 ):
     nc = tc.nc
     with ExitStack() as ctx:
+        lists = ctx.enter_context(tc.tile_pool(name="lists", bufs=1))
         held = ctx.enter_context(tc.tile_pool(name="held", bufs=1))
-        work = ctx.enter_context(tc.tile_pool(name="work", bufs=3))
+        work = ctx.enter_context(tc.tile_pool(name="work", bufs=4))
         page = ctx.enter_context(tc.tile_pool(name="page", bufs=1))
         psum = ctx.enter_context(tc.psum_pool(name="psum", bufs=8))
 
-        def placed(shape, dtype, name, kib):
-            return page.tile(shape, dtype, name=name, align_bytes=64, offset=int(kib * KIB))
+        def kept(shape, dtype, name):
+            return held.tile(shape, dtype, name=name, align_bytes=ROW_ALIGN)
 
-        list1 = held.tile([P, S // 16], U16, name="list1")
-        list2 = held.tile([P, S2 // 16], U16, name="list2")
-        w4_s = held.tile([P, PASSES, N], U8, name="w4_s", align_bytes=64)
-        tab_s = held.tile([P, T], U8, name="tab_s", align_bytes=64)
-        picked = placed([P, S + S2], U8, "picked", 16)
-        tab2_s = placed([P, T2], U8, "tab2_s", 59)
-        rows = held.tile([P, PASSES * (S + S2)], U8, name="rows", align_bytes=64)
-        rows_of_pass = [rows[:, a * (S + S2) : (a + 1) * (S + S2)] for a in range(PASSES)]
-        tab_w = [placed([P, T], U32, f"tab_w{a}", (4, 21)[a]) for a in range(PASSES)]
-        tab2_w = [placed([P, T2], U32, f"tab2_w{a}", (29, 45)[a]) for a in range(PASSES)]
-        w4_sd = held.tile([P, PASSES * N], U8, name="w4_sd", align_bytes=64)
+        def placed(shape, dtype, name, kib):
+            return page.tile(shape, dtype, name=name, align_bytes=ROW_ALIGN, offset=int(kib * KIB))
+
         fields = [(half, g) for half in range(HALVES) for g in range(PASSES)]
-        c32 = {field: placed([P, PACK, BANK], F32, f"c32_{f}", (45, 53, 63, 79)[f]) for f, field in enumerate(fields)}
-        h32 = {field: placed([P, PACK, BANK], F32, f"h32_{f}", (29, 37, 71, 20.75)[f]) for f, field in enumerate(fields)}
-        y_q = [placed([P, BANK], U32, f"y_q{half}", (79, 20.75)[half]) for half in range(HALVES)]
         w1_parts = [(g, n0) for g in range(PASSES) for n0 in range(0, N, W1_PART)]
-        w1_raw = [placed([P, PACK, W1_PART], F32, f"w1_raw{part}", 5 + 4 * part) for part in range(len(w1_parts))]
-        w4_w = placed([P, PASSES, 2 * N], U8, "w4_w", 2.5)
-        lo_t = held.tile([P, PASSES, PACK], F32, name="lo_t")
-        hi_t = held.tile([P, PASSES, PACK], F32, name="hi_t")
-        gain_t = placed([P, PASSES, PACK], F32, "gain_t", 4.75)
+
+        list1 = lists.tile([P, S // 16], U16, name="list1")
+        list2 = lists.tile([P, S2 // 16], U16, name="list2")
+        tab_w = [placed([P, T], U32, f"tab_w{a}", (0, 8)[a]) for a in range(PASSES)]
+        tab2_w = [placed([P, T2], U32, f"tab2_w{a}", (16, 32)[a]) for a in range(PASSES)]
+        tab_s = kept([P, T], U8, "tab_s")
+        tab2_s = placed([P, T2], U8, "tab2_s", 46)
+        v_w = [placed([P, S], U32, f"v_w{a}", (48, 52)[a]) for a in range(PASSES)]
+        v2_w = [kept([P, S2], U32, f"v2_w{a}") for a in range(PASSES)]
+        picked = kept([P, S + S2], U8, "picked")
+        rows = placed([P, PASSES * (S + S2)], U8, "rows", 56)
+        rows_of_pass = [rows[:, a * (S + S2) : (a + 1) * (S + S2)] for a in range(PASSES)]
+        w4_w = kept([P, PASSES, 2 * N], U8, "w4_w")
+        w4_s = kept([P, PASSES, N], U8, "w4_s")
+        w4_wd = kept([P, PASSES * 2 * N], U8, "w4_wd")
+        w4_sd = kept([P, PASSES * N], U8, "w4_sd")
+        lo_t = kept([P, PASSES, PACK], F32, "lo_t")
+        hi_t = kept([P, PASSES, PACK], F32, "hi_t")
+        gain_t = placed([P, PASSES, PACK], F32, "gain_t", 24)
+        w1_raw = [
+            placed([P, PACK, W1_PART], F32, f"w1_raw{part}", (16, 20, 8, 12)[part]) for part in range(len(w1_parts))
+        ]
+        c32 = {field: placed([P, PACK, BANK], F32, f"c32_{f}", 60 + 8 * f) for f, field in enumerate(fields)}
+        h32 = {field: placed([P, PACK, BANK], F32, f"h32_{f}", 92 + 8 * f) for f, field in enumerate(fields)}
 
         nc.vector.memset(tab_s[:].bitcast(I32), 0)
-        nc.vector.memset(w4_s[:].rearrange("p a n -> p (a n)").bitcast(I32), 0)
         nc.vector.memset(tab2_s[:].bitcast(I32), 0)
+        nc.vector.memset(w4_s[:].rearrange("p a n -> p (a n)").bitcast(I32), 0)
         nc.vector.memset(rows[:].bitcast(I32), 0)
 
         def load_words(dst, words, a):
             nc.sync.dma_start(dst[:].bitcast(I32), words[a].rearrange("p t i -> p (t i)").bitcast(I32))
 
+        def load_scale_rows(dst, scales):
+            nc.sync.dma_start(dst[0:P:4, :].bitcast(I32), scales.rearrange("a r t -> (a r) t").bitcast(I32))
+
         def load_by_mode(dst, src):
             nc.sync.dma_start(dst[:], src.rearrange("(g p t) -> p g t", g=PASSES, t=PACK))
-
-        def load_w4_scale_rows(q):
-            nc.sync.dma_start(
-                w4_s[32 * q : 32 * q + 4, :, :].bitcast(I32),
-                w4_scales[:, 4 * q : 4 * q + 4, :].rearrange("a r n -> r a n").bitcast(I32),
-            )
 
         def carry_scale_rows(a):
             for q in range(QUADRANTS):
@@ -96,24 +100,8 @@ def tile_list_satellite_radiance_calibration_kernel(
                 dst = rows_of_pass[a][32 * q : 32 * q + 4, :]
                 nc.sync.dma_start(dst.bitcast(I32), picked[row : row + 16 : 4, :].bitcast(I32))
 
-        def load_first_words(cols):
-            words = tab_words[0].rearrange("p t i -> p (t i)").bitcast(I32)
-            nc.sync.dma_start(tab_w[0][:, cols].bitcast(I32), words[:, cols])
-
-        v_w = [held.tile([P, S], U32, name=f"v_w{a}", align_bytes=64) for a in range(PASSES)]
-        v2_w = [held.tile([P, S2], U32, name=f"v2_w{a}", align_bytes=64) for a in range(PASSES)]
-        w4_wd = held.tile([P, PASSES * 2 * N], U8, name="w4_wd", align_bytes=64)
-
-        def deal(copy, dst, src, run):
-            copy(
-                dst.rearrange("p (g t b i) -> p g b t i", g=PASSES, t=PACK, i=run),
-                src.rearrange("p (g b i t) -> p g b t i", g=PASSES, t=PACK, i=run),
-            )
-
-        def gather_v_words(a):
-            nc.vector.tensor_copy(
-                v_w[a][:].rearrange("p (g t m) -> p g m t", g=PASSES, t=PACK), tab_w[a][:].indirect(list1[:])
-            )
+        def dealt(ap):
+            return ap.rearrange("p (g t m) -> p g m t", g=PASSES, t=PACK)
 
         def gather_v2_words(a, half):
             nc.vector.tensor_copy(
@@ -121,51 +109,52 @@ def tile_list_satellite_radiance_calibration_kernel(
                 tab2_w[a][:].indirect(list2[:, half * BANK // 16 : (half + 1) * BANK // 16]),
             )
 
-        load_first_words(slice(0, LEAD))
+        nc.sync.dma_start(w4_w[:].bitcast(I32), w4_words.rearrange("a p b -> p a b").bitcast(I32))
         nc.sync.dma_start(list1[:], offs)
         nc.sync.dma_start(list2[:], offs2)
-        nc.sync.dma_start(tab_s[0:P:4, :].bitcast(I32), tab_scales.rearrange("a r t -> (a r) t").bitcast(I32))
-        load_first_words(slice(LEAD, T))
+        load_scale_rows(tab_s, tab_scales)
+        load_words(tab_w[0], tab_words, 0)
+        load_scale_rows(tab2_s, tab2_scales)
         for q in range(QUADRANTS):
-            load_w4_scale_rows(q)
-        nc.sync.dma_start(tab2_s[0:P:4, :].bitcast(I32), tab2_scales.rearrange("a r t -> (a r) t").bitcast(I32))
+            nc.sync.dma_start(
+                w4_s[32 * q : 32 * q + 4, :, :].bitcast(I32),
+                w4_scales[:, 4 * q : 4 * q + 4, :].rearrange("a r n -> r a n").bitcast(I32),
+            )
         load_words(tab2_w[0], tab2_words, 0)
         load_words(tab_w[1], tab_words, 1)
         load_by_mode(lo_t, lo)
         load_by_mode(hi_t, hi)
 
-        nc.vector.tensor_copy(
-            picked[:, :S].rearrange("p (g t m) -> p g m t", g=PASSES, t=PACK), tab_s[:].indirect(list1[:])
-        )
+        nc.vector.tensor_copy(dealt(picked[:, :S]), tab_s[:].indirect(list1[:]))
         nc.vector.tensor_copy(picked[:, S:], tab2_s[:].indirect(list2[:]))
         carry_scale_rows(0)
         load_words(tab2_w[1], tab2_words, 1)
         carry_scale_rows(1)
-        gather_v_words(0)
+        nc.vector.tensor_copy(dealt(v_w[0][:]), tab_w[0][:].indirect(list1[:]))
+        for half in range(HALVES):
+            gather_v2_words(0, half)
+        nc.vector.tensor_copy(dealt(v_w[1][:]), tab_w[1][:].indirect(list1[:]))
         load_by_mode(gain_t, gain)
-        nc.sync.dma_start(w4_w[:].bitcast(I32), w4_words.rearrange("a p b -> p a b").bitcast(I32))
         for part, (g, n0) in enumerate(w1_parts):
             part_rows = w1[g * PASS : (g + 1) * PASS, n0 : n0 + W1_PART]
             nc.sync.dma_start(w1_raw[part][:], part_rows.rearrange("(p j) n -> p j n", j=PACK))
         for half in range(HALVES):
-            gather_v2_words(0, half)
-        gather_v_words(1)
-        for half in range(HALVES):
             gather_v2_words(1, half)
 
-        w1_b = placed([P, PASSES, N * PACK], BF16, "w1_b", 99)
-        w1_q = held.tile([P, PASSES * N], U32, name="w1_q", align_bytes=64)
-        w1_s = placed([P, PASSES * N], U8, "w1_s", 19.25)
-        y_s = held.tile([P, S2], U8, name="y_s", align_bytes=64)
+        nc.scalar.copy(
+            w4_wd[:].bitcast(U16).rearrange("p (g t b i) -> p g b t i", g=PASSES, t=PACK, i=8),
+            w4_w[:].rearrange("p a b -> p (a b)").bitcast(U16).rearrange("p (g b i t) -> p g b t i", g=PASSES, t=PACK, i=8),
+        )
+        nc.gpsimd.tensor_copy(
+            w4_sd[:].rearrange("p (g t m) -> p g t m", g=PASSES, t=PACK),
+            w4_s[:].rearrange("p g (m t) -> p g t m", t=PACK),
+        )
 
-        def round_w1(part):
-            g, n0 = w1_parts[part]
+        w1_b = kept([P, PASSES, N * PACK], BF16, "w1_b")
+        for part, (g, n0) in enumerate(w1_parts):
             dst = w1_b[:, g, :].rearrange("p (u e m j) -> p u m j e", u=2, e=2, j=PACK)
             src = w1_raw[part][:].rearrange("p j (m u e) -> p u m j e", u=2, e=2)
             nc.scalar.copy(dst[:, :, n0 // PACK : (n0 + W1_PART) // PACK], src)
-
-        def quantise_w1():
-            nc.vector.quantize_mx(w1_q[:].bitcast(FP8X4), w1_s[:], w1_b[:].rearrange("p g n -> p (g n)"))
 
         def woven(ap, walk):
             return ap.rearrange("p (b i t) -> p b t i", i=walk, t=PACK)
@@ -173,17 +162,10 @@ def tile_list_satellite_radiance_calibration_kernel(
         def by_rows(ap, walk):
             return ap.rearrange("p t (b i) -> p b t i", i=walk)
 
-        last = len(CHUNKS) - 1
-        starts = [sum(CHUNKS[:c]) for c in range(len(CHUNKS))]
-        pieces = [(c, g) for c in range(len(CHUNKS)) for g in range(PASSES)]
         sums = {}
-        rounded = {}
-        quantised = {}
-        banks = {}
-        results = {}
 
-        def first_pass(g, t, half, a, opens):
-            if opens:
+        def first_pass(g, t, half, a):
+            if a == 0:
                 sums[g, t, half] = psum.tile([P, BANK], F32, name="acc")
             cols = slice(g * PASS + t * P, g * PASS + (t + 1) * P)
             js = slice(half * BANK, (half + 1) * BANK)
@@ -193,63 +175,62 @@ def tile_list_satellite_radiance_calibration_kernel(
                 lhsT_scale=rows_of_pass[a][:, cols],
                 rhs=v2_w[a][:, js].bitcast(FP8X4),
                 rhs_scale=rows_of_pass[a][:, S + js.start : S + js.stop],
-                start=opens,
-                stop=not opens,
+                start=(a == 0),
+                stop=(a == PASSES - 1),
             )
 
-        def clamp(g, t, half):
-            nc.vector.tensor_scalar(
-                c32[half, g][:, t, :], sums[g, t, half][:],
-                lo_t[:, g, t : t + 1], hi_t[:, g, t : t + 1], ALU.max, ALU.min,
-            )
+        h_b = {field: kept([P, BANK * PACK], BF16, f"h_b{f}") for f, field in enumerate(fields)}
 
-        def apply_gain(g, t, half):
-            c_row = c32[half, g][:, t, :]
-            h_row = h32[half, g][:, t, :]
-            if t < GPSIMD_SLICES[fields.index((half, g))]:
-                nc.gpsimd.tensor_scalar(h_row, c_row, gain_t[:, g, t : t + 1], 0.0, ALU.mult, ALU.add)
-            else:
-                nc.scalar.activation(h_row, c_row, ACT.Copy, scale=gain_t[:, g, t : t + 1])
+        for a in range(PASSES):
+            for g in range(PASSES):
+                for t in range(PACK):
+                    first_pass(g, t, 0, a)
+        for f, (half, g) in enumerate(fields):
+            for t in range(PACK):
+                if half > 0:
+                    for a in range(PASSES):
+                        first_pass(g, t, half, a)
+                c_row = c32[half, g][:, t, :]
+                h_row = h32[half, g][:, t, :]
+                nc.vector.tensor_scalar(
+                    c_row, sums[g, t, half][:], lo_t[:, g, t : t + 1], hi_t[:, g, t : t + 1], ALU.max, ALU.min
+                )
+                if t < GPSIMD_SLICES[f]:
+                    nc.gpsimd.tensor_scalar(h_row, c_row, gain_t[:, g, t : t + 1], 0.0, ALU.mult, ALU.add)
+                else:
+                    nc.scalar.activation(h_row, c_row, ACT.Copy, scale=gain_t[:, g, t : t + 1])
+            if half == 0:
+                nc.scalar.copy(woven(h_b[half, g][:], SCALAR_WALK), by_rows(h32[half, g][:], SCALAR_WALK))
+        for g in range(PASSES):
+            nc.scalar.copy(woven(h_b[1, g][:], SCALAR_WALK), by_rows(h32[1, g][:], SCALAR_WALK))
 
-        def signal(tiles, g, first, width, walk):
-            return by_rows(tiles[first // BANK, g][:, :, first % BANK : first % BANK + width], walk)
+        h_q = {field: kept([P, BANK], U32, f"h_q{f}") for f, field in enumerate(fields)}
+        h_s = {field: placed([P, BANK], U8, f"h_s{f}", 56 + 0.5 * f) for f, field in enumerate(fields)}
+        w1_q = kept([P, PASSES * N], U32, "w1_q")
+        w1_s = placed([P, PASSES * N], U8, "w1_s", 58)
+        y_b = kept([P, S2 * PACK], BF16, "y_b")
+        y_q = [placed([P, BANK], U32, f"y_q{half}", (84, 116)[half]) for half in range(HALVES)]
+        y_s = kept([P, S2], U8, "y_s")
 
-        h_b = []
-        for run, (g, first, width) in enumerate(H_RUNS):
-            if run < EARLY_RUNS:
-                h_b.append(placed([P, width * PACK], BF16, f"h_b{run}", (15, 19, 95, 97)[run]))
-            else:
-                h_b.append(held.tile([P, width * PACK], BF16, name=f"h_b{run}", align_bytes=64))
-        h_q = [held.tile([P, run[2]], U32, name=f"h_q{k}", align_bytes=64) for k, run in enumerate(H_RUNS)]
-        h_s = [held.tile([P, run[2]], U8, name=f"h_s{k}", align_bytes=64) for k, run in enumerate(H_RUNS)]
+        last = len(CHUNKS) - 1
+        starts = [sum(CHUNKS[:c]) for c in range(len(CHUNKS))]
+        rounded = {}
+        banks = {}
+        results = {}
 
-        def run_of(c, g):
-            return [
-                k for k, (group, first, width) in enumerate(H_RUNS) if group == g and first <= starts[c] < first + width
-            ][0]
+        def quantise_h(field):
+            nc.vector.quantize_mx(h_q[field][:].bitcast(FP8X4), h_s[field][:], h_b[field][:])
 
-        def weave_h(run):
-            nc.scalar.copy(woven(h_b[run][:], SCALAR_WALK), signal(h32, *H_RUNS[run], SCALAR_WALK))
-
-        def quantise_h(run):
-            nc.vector.quantize_mx(h_q[run][:].bitcast(FP8X4), h_s[run][:], h_b[run][:])
-
-        def weave_h2(c, g):
-            slot = pieces.index((c, g)) % H2_SLOTS
-            rounded[c, g] = placed([P, CHUNKS[c] * PACK], BF16, f"h2_b{c}_{g}", (17.25, 99, 101, 97)[slot])
+        def make_h2(c, g):
+            half, j0 = divmod(starts[c], BANK)
+            slot = (PASSES * c + g) % H2_SLOTS
+            rounded[c, g] = placed([P, CHUNKS[c] * PACK], BF16, f"h2_b{c}_{g}", 48 + 2 * slot)
             nc.vector.tensor_tensor(
                 woven(rounded[c, g][:], VECTOR_WALK),
-                signal(h32, g, starts[c], CHUNKS[c], VECTOR_WALK),
-                signal(c32, g, starts[c], CHUNKS[c], VECTOR_WALK),
+                by_rows(h32[half, g][:, :, j0 : j0 + CHUNKS[c]], VECTOR_WALK),
+                by_rows(c32[half, g][:, :, j0 : j0 + CHUNKS[c]], VECTOR_WALK),
                 ALU.mult,
             )
-
-        def quantise_h2(c, g):
-            w = CHUNKS[c]
-            codes = work.tile([P, w], U32, name="h2_q", align_bytes=64, bufs=4)
-            scales = work.tile([P, w], U8, name="h2_s", align_bytes=64, bufs=4)
-            quantised[c, g] = (codes, scales)
-            nc.vector.quantize_mx(codes[:].bitcast(FP8X4), scales[:], rounded[c, g][:])
 
         def bank_slices(c):
             if CHUNKS[c] * PACK > BANK:
@@ -257,27 +238,27 @@ def tile_list_satellite_radiance_calibration_kernel(
             return [(0, 1, 2, 3)]
 
         def linear_passes(c, g):
-            w = CHUNKS[c]
-            run = run_of(c, g)
-            js = slice(starts[c] - H_RUNS[run][1], starts[c] - H_RUNS[run][1] + w)
-            if g == 0:
-                for bank, slices in enumerate(bank_slices(c)):
-                    banks[c, bank] = psum.tile([P, len(slices), w], F32, name="acc")
+            half, j0 = divmod(starts[c], BANK)
+            js = slice(j0, j0 + CHUNKS[c])
             for bank, slices in enumerate(bank_slices(c)):
+                if g == 0:
+                    banks[c, bank] = psum.tile([P, len(slices), CHUNKS[c]], F32, name="acc")
                 for s, t in enumerate(slices):
                     n0 = g * N + t * P
                     nc.tensor.matmul_mx(
                         banks[c, bank][:, s, :],
                         lhsT=w1_q[:, n0 : n0 + P].bitcast(FP8X4),
                         lhsT_scale=w1_s[:, n0 : n0 + P],
-                        rhs=h_q[run][:, js].bitcast(FP8X4),
-                        rhs_scale=h_s[run][:, js],
+                        rhs=h_q[half, g][:, js].bitcast(FP8X4),
+                        rhs_scale=h_s[half, g][:, js],
                         start=(g == 0 and s == 0),
                         stop=False,
                     )
 
         def quadratic_passes(c, g):
-            codes, scales = quantised[c, g]
+            codes = work.tile([P, CHUNKS[c]], U32, name="h2_q", align_bytes=ROW_ALIGN)
+            scales = work.tile([P, CHUNKS[c]], U8, name="h2_s", align_bytes=ROW_ALIGN)
+            nc.vector.quantize_mx(codes[:].bitcast(FP8X4), scales[:], rounded[c, g][:])
             for bank, slices in enumerate(bank_slices(c)):
                 for s, t in enumerate(slices):
                     n0 = g * N + t * P
@@ -294,14 +275,10 @@ def tile_list_satellite_radiance_calibration_kernel(
         out_rows = out_0.rearrange("(p t) j -> p t j", t=PACK)
 
         def hand_out(c):
-            w = CHUNKS[c]
-            y32 = held.tile([P, PACK, w], F32, name=f"y32_{c}", align_bytes=64)
-            results[c] = y32
+            results[c] = kept([P, PACK, CHUNKS[c]], F32, f"y32_{c}")
             for bank, slices in enumerate(bank_slices(c)):
-                nc.scalar.copy(y32[:, slices[0] : slices[-1] + 1, :], banks[c, bank][:])
-            nc.sync.dma_start(out_rows[:, :, starts[c] : starts[c] + w], y32[:])
-
-        y_b = held.tile([P, S2 * PACK], BF16, name="y_b", align_bytes=64)
+                nc.scalar.copy(results[c][:, slices[0] : slices[-1] + 1, :], banks[c, bank][:])
+            nc.sync.dma_start(out_rows[:, :, starts[c] : starts[c] + CHUNKS[c]], results[c][:])
 
         def weave_y(c):
             dst = y_b[:, starts[c] * PACK : (starts[c] + CHUNKS[c]) * PACK]
@@ -310,9 +287,29 @@ def tile_list_satellite_radiance_calibration_kernel(
             else:
                 nc.vector.tensor_copy(woven(dst, VECTOR_WALK), by_rows(results[c][:], VECTOR_WALK))
 
-        out_words = out_1[0].rearrange("p m t -> p (m t)").bitcast(I32)
+        quantise_h((0, 0))
+        nc.vector.quantize_mx(w1_q[:].bitcast(FP8X4), w1_s[:], w1_b[:].rearrange("p g n -> p (g n)"))
+        for c in range(len(CHUNKS)):
+            half, j0 = divmod(starts[c], BANK)
+            if j0 == 0 and half > 0:
+                quantise_h((half, 0))
+            for g in range(PASSES):
+                make_h2(c, g)
+            linear_passes(c, 0)
+            quadratic_passes(c, 0)
+            if j0 == 0:
+                quantise_h((half, 1))
+            linear_passes(c, 1)
+            quadratic_passes(c, 1)
+            hand_out(c)
+            if c in Y_WEAVES_ON_SCALAR:
+                weave_y(c)
 
-        def planes(group):
+        for c in range(last):
+            if c not in Y_WEAVES_ON_SCALAR:
+                weave_y(c)
+        out_words = out_1[0].rearrange("p m t -> p (m t)").bitcast(I32)
+        for group in CODE_STORES:
             if last in group:
                 weave_y(last)
             js = slice(starts[group[0]], starts[group[-1]] + CHUNKS[group[-1]])
@@ -321,54 +318,6 @@ def tile_list_satellite_radiance_calibration_kernel(
             nc.vector.quantize_mx(codes.bitcast(FP8X4), y_s[:, js], y_b[:, js.start * PACK : js.stop * PACK])
             queue = nc.scalar if last in group else nc.sync
             queue.dma_start(out_words[:, js], codes.bitcast(I32))
-
-        deal(nc.scalar.copy, w4_wd[:].bitcast(U16), w4_w[:].rearrange("p a b -> p (a b)").bitcast(U16), 8)
-        for part in range(len(w1_parts)):
-            round_w1(part)
-
-        nc.gpsimd.tensor_copy(
-            w4_sd[:].rearrange("p (g t m) -> p g t m", g=PASSES, t=PACK),
-            w4_s[:].rearrange("p g (m t) -> p g t m", t=PACK),
-        )
-
-        for a in range(PASSES):
-            for g in range(PASSES):
-                for t in range(PACK):
-                    first_pass(g, t, 0, a, a == 0)
-        for half, g in fields:
-            if (half, g) == (1, 0):
-                for run in range(EARLY_RUNS):
-                    weave_h(run)
-            for t in range(PACK):
-                if half > 0:
-                    first_pass(g, t, half, 0, True)
-                    first_pass(g, t, half, 1, False)
-                clamp(g, t, half)
-                apply_gain(g, t, half)
-
-        for run in range(EARLY_RUNS, len(H_RUNS)):
-            weave_h(run)
-        for run in (0, 2, 1):
-            quantise_h(run)
-        quantise_w1()
-        for c in range(len(CHUNKS)):
-            for g in range(PASSES):
-                if starts[c] == H_RUNS[run_of(c, g)][1] and run_of(c, g) > 2:
-                    quantise_h(run_of(c, g))
-                linear_passes(c, g)
-                weave_h2(c, g)
-            for g in range(PASSES):
-                quantise_h2(c, g)
-                quadratic_passes(c, g)
-            hand_out(c)
-            if c in Y_WEAVES_ON_SCALAR:
-                weave_y(c)
-
-        for c in range(last):
-            if c not in Y_WEAVES_ON_SCALAR:
-                weave_y(c)
-        for group in CODE_STORES:
-            planes(group)
 
         for q in range(QUADRANTS):
             queue = nc.sync if q % 2 == 0 else nc.scalar

@@ -23,12 +23,12 @@ PASS = P * PACK
 QUADRANTS = 4
 BANK = 512
 HALVES = S2 // BANK
-CHUNKS = (256, 256, 128, 128, 128, 128)
+CHUNKS = (256, 256, 256, 128, 128)
 GPSIMD_SLICES = (3, 3, 4, 0)
-Y_WEAVES_ON_SCALAR = (0, 1, 2, 3)
+Y_WEAVES_ON_SCALAR = (0, 1, 2)
 H2_SLOTS = 4
 W1_PART = 256
-CODE_STORES = ((0, 1), (2, 3, 4), (5,))
+CODE_STORES = ((0, 1), (2,), (3, 4))
 KIB = 1024
 ROW_ALIGN = 256
 SCALAR_WALK = 2
@@ -70,12 +70,12 @@ def tile_list_satellite_radiance_calibration_kernel(
         w4_w = kept([P, PASSES, 2 * N], U8, "w4_w")
         w4_s = kept([P, PASSES, N], U8, "w4_s")
         w4_wd = kept([P, PASSES * 2 * N], U8, "w4_wd")
-        w4_sd = kept([P, PASSES * N], U8, "w4_sd")
-        lo_t = kept([P, PASSES, PACK], F32, "lo_t")
-        hi_t = kept([P, PASSES, PACK], F32, "hi_t")
-        gain_t = placed([P, PASSES, PACK], F32, "gain_t", 24)
+        w4_sd = placed([P, PASSES * N], U8, "w4_sd", 12)
+        lo_t = placed([P, PASSES, PACK], F32, "lo_t", 25)
+        hi_t = placed([P, PASSES, PACK], F32, "hi_t", 25.25)
+        gain_t = kept([P, PASSES, PACK], F32, "gain_t")
         w1_raw = [
-            placed([P, PACK, W1_PART], F32, f"w1_raw{part}", (16, 20, 8, 12)[part]) for part in range(len(w1_parts))
+            placed([P, PACK, W1_PART], F32, f"w1_raw{part}", (17, 21, 8, 13)[part]) for part in range(len(w1_parts))
         ]
         c32 = {field: placed([P, PACK, BANK], F32, f"c32_{f}", 60 + 8 * f) for f, field in enumerate(fields)}
         h32 = {field: placed([P, PACK, BANK], F32, f"h32_{f}", 92 + 8 * f) for f, field in enumerate(fields)}
@@ -115,15 +115,10 @@ def tile_list_satellite_radiance_calibration_kernel(
         load_scale_rows(tab_s, tab_scales)
         load_words(tab_w[0], tab_words, 0)
         load_scale_rows(tab2_s, tab2_scales)
-        for q in range(QUADRANTS):
-            nc.sync.dma_start(
-                w4_s[32 * q : 32 * q + 4, :, :].bitcast(I32),
-                w4_scales[:, 4 * q : 4 * q + 4, :].rearrange("a r n -> r a n").bitcast(I32),
-            )
+        nc.sync.dma_start(w4_s[4:P:8, :, :].bitcast(I32), w4_scales.rearrange("a r n -> r a n").bitcast(I32))
+        load_by_mode(gain_t, gain)
         load_words(tab2_w[0], tab2_words, 0)
         load_words(tab_w[1], tab_words, 1)
-        load_by_mode(lo_t, lo)
-        load_by_mode(hi_t, hi)
 
         nc.vector.tensor_copy(dealt(picked[:, :S]), tab_s[:].indirect(list1[:]))
         nc.vector.tensor_copy(picked[:, S:], tab2_s[:].indirect(list2[:]))
@@ -134,10 +129,12 @@ def tile_list_satellite_radiance_calibration_kernel(
         for half in range(HALVES):
             gather_v2_words(0, half)
         nc.vector.tensor_copy(dealt(v_w[1][:]), tab_w[1][:].indirect(list1[:]))
-        load_by_mode(gain_t, gain)
         for part, (g, n0) in enumerate(w1_parts):
             part_rows = w1[g * PASS : (g + 1) * PASS, n0 : n0 + W1_PART]
             nc.sync.dma_start(w1_raw[part][:], part_rows.rearrange("(p j) n -> p j n", j=PACK))
+            if part == 0:
+                load_by_mode(lo_t, lo)
+                load_by_mode(hi_t, hi)
         for half in range(HALVES):
             gather_v2_words(1, half)
 
@@ -149,6 +146,10 @@ def tile_list_satellite_radiance_calibration_kernel(
             w4_sd[:].rearrange("p (g t m) -> p g t m", g=PASSES, t=PACK),
             w4_s[:].rearrange("p g (m t) -> p g t m", t=PACK),
         )
+        for q in range(QUADRANTS):
+            nc.sync.dma_start(
+                w4_sd[32 * q : 32 * q + 4, :].bitcast(I32), w4_sd[32 * q + 4 : 32 * q + 32 : 8, :].bitcast(I32)
+            )
 
         w1_b = kept([P, PASSES, N * PACK], BF16, "w1_b")
         for part, (g, n0) in enumerate(w1_parts):
@@ -305,13 +306,11 @@ def tile_list_satellite_radiance_calibration_kernel(
             if c in Y_WEAVES_ON_SCALAR:
                 weave_y(c)
 
-        for c in range(last):
-            if c not in Y_WEAVES_ON_SCALAR:
-                weave_y(c)
         out_words = out_1[0].rearrange("p m t -> p (m t)").bitcast(I32)
         for group in CODE_STORES:
-            if last in group:
-                weave_y(last)
+            for c in group:
+                if c not in Y_WEAVES_ON_SCALAR:
+                    weave_y(c)
             js = slice(starts[group[0]], starts[group[-1]] + CHUNKS[group[-1]])
             half = js.start // BANK
             codes = y_q[half][:, js.start - half * BANK : js.stop - half * BANK]

@@ -28,7 +28,7 @@ GPSIMD_SLICES = (3, 3, 4, 0)
 Y_WEAVES_ON_SCALAR = (0, 1, 2)
 H2_SLOTS = 4
 W1_PART = 256
-CODE_STORES = ((0, 1), (2,), (3, 4))
+CODE_STORES = ((0, 1), (3, 4), (2,))
 KIB = 1024
 ROW_ALIGN = 256
 SCALAR_WALK = 2
@@ -213,7 +213,6 @@ def tile_list_satellite_radiance_calibration_kernel(
         y_q = [placed([P, BANK], U32, f"y_q{half}", (84, 116)[half]) for half in range(HALVES)]
         y_s = kept([P, S2], U8, "y_s")
 
-        last = len(CHUNKS) - 1
         starts = [sum(CHUNKS[:c]) for c in range(len(CHUNKS))]
         rounded = {}
         banks = {}
@@ -303,8 +302,8 @@ def tile_list_satellite_radiance_calibration_kernel(
             linear_passes(c, 1)
             quadratic_passes(c, 1)
             hand_out(c)
-            if c in Y_WEAVES_ON_SCALAR:
-                weave_y(c)
+        for c in Y_WEAVES_ON_SCALAR:
+            weave_y(c)
 
         out_words = out_1[0].rearrange("p m t -> p (m t)").bitcast(I32)
         for group in CODE_STORES:
@@ -315,7 +314,7 @@ def tile_list_satellite_radiance_calibration_kernel(
             half = js.start // BANK
             codes = y_q[half][:, js.start - half * BANK : js.stop - half * BANK]
             nc.vector.quantize_mx(codes.bitcast(FP8X4), y_s[:, js], y_b[:, js.start * PACK : js.stop * PACK])
-            queue = nc.scalar if last in group else nc.sync
+            queue = nc.scalar if group == CODE_STORES[-1] else nc.sync
             queue.dma_start(out_words[:, js], codes.bitcast(I32))
 
         for q in range(QUADRANTS):

@@ -31,6 +31,7 @@ W1_PART = 256
 CODE_STORES = ((0, 1), (3, 4), (2,))
 KIB = 1024
 ROW_ALIGN = 256
+LEAD = T // 4
 SCALAR_WALK = 2
 VECTOR_WALK = 4
 
@@ -62,14 +63,14 @@ def tile_list_satellite_radiance_calibration_kernel(
         tab2_w = [placed([P, T2], U32, f"tab2_w{a}", (16, 32)[a]) for a in range(PASSES)]
         tab_s = kept([P, T], U8, "tab_s")
         tab2_s = placed([P, T2], U8, "tab2_s", 46)
-        v_w = [placed([P, S], U32, f"v_w{a}", (48, 52)[a]) for a in range(PASSES)]
+        v_w = [placed([P, S], U32, f"v_w{a}", (49, 53)[a]) for a in range(PASSES)]
         v2_w = [kept([P, S2], U32, f"v2_w{a}") for a in range(PASSES)]
         picked = kept([P, S + S2], U8, "picked")
-        rows = placed([P, PASSES * (S + S2)], U8, "rows", 56)
+        rows = placed([P, PASSES * (S + S2)], U8, "rows", 57)
         rows_of_pass = [rows[:, a * (S + S2) : (a + 1) * (S + S2)] for a in range(PASSES)]
-        w4_w = kept([P, PASSES, 2 * N], U8, "w4_w")
+        w4_w = [kept([P, 2 * N], U8, "w4_w0"), placed([P, 2 * N], U8, "w4_w1", 48)]
         w4_s = kept([P, PASSES, N], U8, "w4_s")
-        w4_wd = kept([P, PASSES * 2 * N], U8, "w4_wd")
+        w4_wd = [kept([P, 2 * N], U8, f"w4_wd{g}") for g in range(PASSES)]
         w4_sd = placed([P, PASSES * N], U8, "w4_sd", 12)
         lo_t = placed([P, PASSES, PACK], F32, "lo_t", 25)
         hi_t = placed([P, PASSES, PACK], F32, "hi_t", 25.25)
@@ -77,16 +78,19 @@ def tile_list_satellite_radiance_calibration_kernel(
         w1_raw = [
             placed([P, PACK, W1_PART], F32, f"w1_raw{part}", (17, 21, 8, 13)[part]) for part in range(len(w1_parts))
         ]
-        c32 = {field: placed([P, PACK, BANK], F32, f"c32_{f}", 60 + 8 * f) for f, field in enumerate(fields)}
-        h32 = {field: placed([P, PACK, BANK], F32, f"h32_{f}", 92 + 8 * f) for f, field in enumerate(fields)}
+        c32 = {field: placed([P, PACK, BANK], F32, f"c32_{f}", 61 + 8 * f) for f, field in enumerate(fields)}
+        h32 = {field: placed([P, PACK, BANK], F32, f"h32_{f}", 93 + 8 * f) for f, field in enumerate(fields)}
 
         nc.vector.memset(tab_s[:].bitcast(I32), 0)
         nc.vector.memset(tab2_s[:].bitcast(I32), 0)
         nc.vector.memset(w4_s[:].rearrange("p a n -> p (a n)").bitcast(I32), 0)
         nc.vector.memset(rows[:].bitcast(I32), 0)
 
-        def load_words(dst, words, a):
-            nc.sync.dma_start(dst[:].bitcast(I32), words[a].rearrange("p t i -> p (t i)").bitcast(I32))
+        def load_words(dst, words, a, cols=slice(None)):
+            nc.sync.dma_start(dst[:, cols].bitcast(I32), words[a].rearrange("p t i -> p (t i)").bitcast(I32)[:, cols])
+
+        def load_w4_words(g):
+            nc.sync.dma_start(w4_w[g][:].bitcast(I32), w4_words[g].bitcast(I32))
 
         def load_scale_rows(dst, scales):
             nc.sync.dma_start(dst[0:P:4, :].bitcast(I32), scales.rearrange("a r t -> (a r) t").bitcast(I32))
@@ -109,14 +113,15 @@ def tile_list_satellite_radiance_calibration_kernel(
                 tab2_w[a][:].indirect(list2[:, half * BANK // 16 : (half + 1) * BANK // 16]),
             )
 
-        nc.sync.dma_start(w4_w[:].bitcast(I32), w4_words.rearrange("a p b -> p a b").bitcast(I32))
+        load_words(tab_w[0], tab_words, 0, slice(0, LEAD))
         nc.sync.dma_start(list1[:], offs)
         nc.sync.dma_start(list2[:], offs2)
         load_scale_rows(tab_s, tab_scales)
-        load_words(tab_w[0], tab_words, 0)
+        load_words(tab_w[0], tab_words, 0, slice(LEAD, T))
         load_scale_rows(tab2_s, tab2_scales)
         nc.sync.dma_start(w4_s[4:P:8, :, :].bitcast(I32), w4_scales.rearrange("a r n -> r a n").bitcast(I32))
         load_by_mode(gain_t, gain)
+        load_w4_words(0)
         load_words(tab2_w[0], tab2_words, 0)
         load_words(tab_w[1], tab_words, 1)
 
@@ -124,6 +129,7 @@ def tile_list_satellite_radiance_calibration_kernel(
         nc.vector.tensor_copy(picked[:, S:], tab2_s[:].indirect(list2[:]))
         carry_scale_rows(0)
         load_words(tab2_w[1], tab2_words, 1)
+        load_w4_words(1)
         carry_scale_rows(1)
         nc.vector.tensor_copy(dealt(v_w[0][:]), tab_w[0][:].indirect(list1[:]))
         for half in range(HALVES):
@@ -138,10 +144,11 @@ def tile_list_satellite_radiance_calibration_kernel(
         for half in range(HALVES):
             gather_v2_words(1, half)
 
-        nc.scalar.copy(
-            w4_wd[:].bitcast(U16).rearrange("p (g t b i) -> p g b t i", g=PASSES, t=PACK, i=8),
-            w4_w[:].rearrange("p a b -> p (a b)").bitcast(U16).rearrange("p (g b i t) -> p g b t i", g=PASSES, t=PACK, i=8),
-        )
+        for g in range(PASSES):
+            nc.scalar.copy(
+                w4_wd[g][:].bitcast(U16).rearrange("p (t b i) -> p b t i", t=PACK, i=8),
+                w4_w[g][:].bitcast(U16).rearrange("p (b i t) -> p b t i", t=PACK, i=8),
+            )
         nc.gpsimd.tensor_copy(
             w4_sd[:].rearrange("p (g t m) -> p g t m", g=PASSES, t=PACK),
             w4_s[:].rearrange("p g (m t) -> p g t m", t=PACK),
@@ -206,11 +213,11 @@ def tile_list_satellite_radiance_calibration_kernel(
             nc.scalar.copy(woven(h_b[1, g][:], SCALAR_WALK), by_rows(h32[1, g][:], SCALAR_WALK))
 
         h_q = {field: kept([P, BANK], U32, f"h_q{f}") for f, field in enumerate(fields)}
-        h_s = {field: placed([P, BANK], U8, f"h_s{f}", 56 + 0.5 * f) for f, field in enumerate(fields)}
+        h_s = {field: placed([P, BANK], U8, f"h_s{f}", 57 + 0.5 * f) for f, field in enumerate(fields)}
         w1_q = kept([P, PASSES * N], U32, "w1_q")
-        w1_s = placed([P, PASSES * N], U8, "w1_s", 58)
+        w1_s = placed([P, PASSES * N], U8, "w1_s", 59)
         y_b = kept([P, S2 * PACK], BF16, "y_b")
-        y_q = [placed([P, BANK], U32, f"y_q{half}", (84, 116)[half]) for half in range(HALVES)]
+        y_q = [placed([P, BANK], U32, f"y_q{half}", (85, 117)[half]) for half in range(HALVES)]
         y_s = kept([P, S2], U8, "y_s")
 
         starts = [sum(CHUNKS[:c]) for c in range(len(CHUNKS))]
@@ -224,7 +231,7 @@ def tile_list_satellite_radiance_calibration_kernel(
         def make_h2(c, g):
             half, j0 = divmod(starts[c], BANK)
             slot = (PASSES * c + g) % H2_SLOTS
-            rounded[c, g] = placed([P, CHUNKS[c] * PACK], BF16, f"h2_b{c}_{g}", 48 + 2 * slot)
+            rounded[c, g] = placed([P, CHUNKS[c] * PACK], BF16, f"h2_b{c}_{g}", 49 + 2 * slot)
             nc.vector.tensor_tensor(
                 woven(rounded[c, g][:], VECTOR_WALK),
                 by_rows(h32[half, g][:, :, j0 : j0 + CHUNKS[c]], VECTOR_WALK),
@@ -264,7 +271,7 @@ def tile_list_satellite_radiance_calibration_kernel(
                     n0 = g * N + t * P
                     nc.tensor.matmul_mx(
                         banks[c, bank][:, s, :],
-                        lhsT=w4_wd[:, 2 * n0 : 2 * (n0 + P)].bitcast(FP4X4),
+                        lhsT=w4_wd[g][:, 2 * t * P : 2 * (t + 1) * P].bitcast(FP4X4),
                         lhsT_scale=w4_sd[:, n0 : n0 + P],
                         rhs=codes[:].bitcast(FP8X4),
                         rhs_scale=scales[:],

@@ -25,10 +25,12 @@ BANK = 512
 HALVES = S2 // BANK
 CHUNKS = (256, 256, 256, 128, 128)
 GPSIMD_SLICES = (3, 3, 4, 0)
-Y_WEAVES_ON_SCALAR = (0, 1, 2)
+Y_EARLY = 640
+Y_RUNS_ON_SCALAR = ((0, 256), (256, 256), (512, 128), (640, 128), (896, 128))
+Y_RUN_ON_VECTOR = (768, 128)
 H2_SLOTS = 4
 W1_PART = 256
-CODE_STORES = ((0, 1), (3, 4), (2,))
+CODE_STORES = (((0, 256),), ((256, 256),), ((512, 128), (640, 256)), ((896, 128),))
 KIB = 1024
 ROW_ALIGN = 256
 LEAD = T // 4
@@ -159,10 +161,15 @@ def tile_list_satellite_radiance_calibration_kernel(
             )
 
         w1_b = kept([P, PASSES, N * PACK], BF16, "w1_b")
-        for part, (g, n0) in enumerate(w1_parts):
+
+        def round_w1(part):
+            g, n0 = w1_parts[part]
             dst = w1_b[:, g, :].rearrange("p (u e m j) -> p u m j e", u=2, e=2, j=PACK)
             src = w1_raw[part][:].rearrange("p j (m u e) -> p u m j e", u=2, e=2)
             nc.scalar.copy(dst[:, :, n0 // PACK : (n0 + W1_PART) // PACK], src)
+
+        for part in range(len(w1_parts) - 1):
+            round_w1(part)
 
         def woven(ap, walk):
             return ap.rearrange("p (b i t) -> p b t i", i=walk, t=PACK)
@@ -207,16 +214,18 @@ def tile_list_satellite_radiance_calibration_kernel(
                     nc.gpsimd.tensor_scalar(h_row, c_row, gain_t[:, g, t : t + 1], 0.0, ALU.mult, ALU.add)
                 else:
                     nc.scalar.activation(h_row, c_row, ACT.Copy, scale=gain_t[:, g, t : t + 1])
-            if half == 0:
-                nc.scalar.copy(woven(h_b[half, g][:], SCALAR_WALK), by_rows(h32[half, g][:], SCALAR_WALK))
-        for g in range(PASSES):
-            nc.scalar.copy(woven(h_b[1, g][:], SCALAR_WALK), by_rows(h32[1, g][:], SCALAR_WALK))
+            if f == 0:
+                round_w1(len(w1_parts) - 1)
+            if g == PASSES - 1:
+                for field in fields[f - 1 : f + 1]:
+                    nc.scalar.copy(woven(h_b[field][:], SCALAR_WALK), by_rows(h32[field][:], SCALAR_WALK))
 
         h_q = {field: kept([P, BANK], U32, f"h_q{f}") for f, field in enumerate(fields)}
         h_s = {field: placed([P, BANK], U8, f"h_s{f}", 57 + 0.5 * f) for f, field in enumerate(fields)}
         w1_q = kept([P, PASSES * N], U32, "w1_q")
         w1_s = placed([P, PASSES * N], U8, "w1_s", 59)
-        y_b = kept([P, S2 * PACK], BF16, "y_b")
+        y_early = kept([P, Y_EARLY * PACK], BF16, "y_early")
+        y_late = placed([P, (S2 - Y_EARLY) * PACK], BF16, "y_late", 128)
         y_q = [placed([P, BANK], U32, f"y_q{half}", (85, 117)[half]) for half in range(HALVES)]
         y_s = kept([P, S2], U8, "y_s")
 
@@ -263,7 +272,8 @@ def tile_list_satellite_radiance_calibration_kernel(
                     )
 
         def quadratic_passes(c, g):
-            codes = work.tile([P, CHUNKS[c]], U32, name="h2_q", align_bytes=ROW_ALIGN)
+            slot = (PASSES * c + g) % H2_SLOTS
+            codes = placed([P, CHUNKS[c]], U32, f"h2_q{c}_{g}", 125 + slot)
             scales = work.tile([P, CHUNKS[c]], U8, name="h2_s", align_bytes=ROW_ALIGN)
             nc.vector.quantize_mx(codes[:].bitcast(FP8X4), scales[:], rounded[c, g][:])
             for bank, slices in enumerate(bank_slices(c)):
@@ -283,16 +293,22 @@ def tile_list_satellite_radiance_calibration_kernel(
 
         def hand_out(c):
             results[c] = kept([P, PACK, CHUNKS[c]], F32, f"y32_{c}")
+            js = slice(starts[c], starts[c] + CHUNKS[c])
             for bank, slices in enumerate(bank_slices(c)):
-                nc.scalar.copy(results[c][:, slices[0] : slices[-1] + 1, :], banks[c, bank][:])
-            nc.sync.dma_start(out_rows[:, :, starts[c] : starts[c] + CHUNKS[c]], results[c][:])
+                ts = slice(slices[0], slices[-1] + 1)
+                nc.scalar.copy(results[c][:, ts, :], banks[c, bank][:])
+                nc.sync.dma_start(out_rows[:, ts, js], results[c][:, ts, :])
 
-        def weave_y(c):
-            dst = y_b[:, starts[c] * PACK : (starts[c] + CHUNKS[c]) * PACK]
-            if c in Y_WEAVES_ON_SCALAR:
-                nc.scalar.copy(woven(dst, SCALAR_WALK), by_rows(results[c][:], SCALAR_WALK))
-            else:
-                nc.vector.tensor_copy(woven(dst, VECTOR_WALK), by_rows(results[c][:], VECTOR_WALK))
+        def rounded_y(first, width):
+            if first < Y_EARLY:
+                return y_early[:, first * PACK : (first + width) * PACK]
+            return y_late[:, (first - Y_EARLY) * PACK : (first - Y_EARLY + width) * PACK]
+
+        def weave_y(copy, walk, first, width):
+            c = max(k for k in range(len(CHUNKS)) if starts[k] <= first)
+            src = banks[c, 0] if c == len(CHUNKS) - 1 else results[c]
+            j0 = first - starts[c]
+            copy(woven(rounded_y(first, width), walk), by_rows(src[:, :, j0 : j0 + width], walk))
 
         quantise_h((0, 0))
         nc.vector.quantize_mx(w1_q[:].bitcast(FP8X4), w1_s[:], w1_b[:].rearrange("p g n -> p (g n)"))
@@ -309,20 +325,25 @@ def tile_list_satellite_radiance_calibration_kernel(
             linear_passes(c, 1)
             quadratic_passes(c, 1)
             hand_out(c)
-        for c in Y_WEAVES_ON_SCALAR:
-            weave_y(c)
+        for run in Y_RUNS_ON_SCALAR:
+            weave_y(nc.scalar.copy, SCALAR_WALK, *run)
 
         out_words = out_1[0].rearrange("p m t -> p (m t)").bitcast(I32)
-        for group in CODE_STORES:
-            for c in group:
-                if c not in Y_WEAVES_ON_SCALAR:
-                    weave_y(c)
-            js = slice(starts[group[0]], starts[group[-1]] + CHUNKS[group[-1]])
-            half = js.start // BANK
-            codes = y_q[half][:, js.start - half * BANK : js.stop - half * BANK]
-            nc.vector.quantize_mx(codes.bitcast(FP8X4), y_s[:, js], y_b[:, js.start * PACK : js.stop * PACK])
-            queue = nc.scalar if group == CODE_STORES[-1] else nc.sync
-            queue.dma_start(out_words[:, js], codes.bitcast(I32))
+
+        def codes_of(first, width):
+            half, j0 = divmod(first, BANK)
+            return y_q[half][:, j0 : j0 + width]
+
+        for store in CODE_STORES:
+            for first, width in store:
+                nc.vector.quantize_mx(
+                    codes_of(first, width).bitcast(FP8X4), y_s[:, first : first + width], rounded_y(first, width)
+                )
+            first, width = store[0][0], sum(run[1] for run in store)
+            queue = nc.scalar if store == CODE_STORES[-1] else nc.sync
+            queue.dma_start(out_words[:, first : first + width], codes_of(first, width).bitcast(I32))
+            if store == CODE_STORES[1]:
+                weave_y(nc.vector.tensor_copy, VECTOR_WALK, *Y_RUN_ON_VECTOR)
 
         for q in range(QUADRANTS):
             queue = nc.sync if q % 2 == 0 else nc.scalar

@@ -70,13 +70,13 @@ def tile_list_satellite_radiance_calibration_kernel(
         picked = kept([P, S + S2], U8, "picked")
         rows = placed([P, PASSES * (S + S2)], U8, "rows", 57)
         rows_of_pass = [rows[:, a * (S + S2) : (a + 1) * (S + S2)] for a in range(PASSES)]
-        w4_w = [kept([P, 2 * N], U8, "w4_w0"), placed([P, 2 * N], U8, "w4_w1", 48)]
+        w4_w = [placed([P, 2 * N], U8, "w4_w0", 48), placed([P, 2 * N], U8, "w4_w1", 32)]
         w4_s = kept([P, PASSES, N], U8, "w4_s")
         w4_wd = [kept([P, 2 * N], U8, f"w4_wd{g}") for g in range(PASSES)]
         w4_sd = placed([P, PASSES * N], U8, "w4_sd", 12)
         lo_t = placed([P, PASSES, PACK], F32, "lo_t", 25)
         hi_t = placed([P, PASSES, PACK], F32, "hi_t", 25.25)
-        gain_t = kept([P, PASSES, PACK], F32, "gain_t")
+        gain_t = placed([P, PASSES, PACK], F32, "gain_t", 25.5)
         w1_raw = [
             placed([P, PACK, W1_PART], F32, f"w1_raw{part}", (17, 21, 8, 13)[part]) for part in range(len(w1_parts))
         ]
@@ -122,8 +122,6 @@ def tile_list_satellite_radiance_calibration_kernel(
         load_words(tab_w[0], tab_words, 0, slice(LEAD, T))
         load_scale_rows(tab2_s, tab2_scales)
         nc.sync.dma_start(w4_s[4:P:8, :, :].bitcast(I32), w4_scales.rearrange("a r n -> r a n").bitcast(I32))
-        load_by_mode(gain_t, gain)
-        load_w4_words(0)
         load_words(tab2_w[0], tab2_words, 0)
         load_words(tab_w[1], tab_words, 1)
 
@@ -131,7 +129,7 @@ def tile_list_satellite_radiance_calibration_kernel(
         nc.vector.tensor_copy(picked[:, S:], tab2_s[:].indirect(list2[:]))
         carry_scale_rows(0)
         load_words(tab2_w[1], tab2_words, 1)
-        load_w4_words(1)
+        load_w4_words(0)
         carry_scale_rows(1)
         nc.vector.tensor_copy(dealt(v_w[0][:]), tab_w[0][:].indirect(list1[:]))
         for half in range(HALVES):
@@ -143,14 +141,18 @@ def tile_list_satellite_radiance_calibration_kernel(
             if part == 0:
                 load_by_mode(lo_t, lo)
                 load_by_mode(hi_t, hi)
+                load_by_mode(gain_t, gain)
         for half in range(HALVES):
             gather_v2_words(1, half)
+        load_w4_words(1)
 
-        for g in range(PASSES):
+        def deal_w4_words(g):
             nc.scalar.copy(
                 w4_wd[g][:].bitcast(U16).rearrange("p (t b i) -> p b t i", t=PACK, i=8),
                 w4_w[g][:].bitcast(U16).rearrange("p (b i t) -> p b t i", t=PACK, i=8),
             )
+
+        deal_w4_words(0)
         nc.gpsimd.tensor_copy(
             w4_sd[:].rearrange("p (g t m) -> p g t m", g=PASSES, t=PACK),
             w4_s[:].rearrange("p g (m t) -> p g t m", t=PACK),
@@ -219,6 +221,8 @@ def tile_list_satellite_radiance_calibration_kernel(
             if g == PASSES - 1:
                 for field in fields[f - 1 : f + 1]:
                     nc.scalar.copy(woven(h_b[field][:], SCALAR_WALK), by_rows(h32[field][:], SCALAR_WALK))
+                if half == 0:
+                    deal_w4_words(1)
 
         h_q = {field: kept([P, BANK], U32, f"h_q{f}") for f, field in enumerate(fields)}
         h_s = {field: placed([P, BANK], U8, f"h_s{f}", 57 + 0.5 * f) for f, field in enumerate(fields)}

from contextlib import ExitStack

import concourse.mybir as mybir

K, T, S, T2, S2, N = 1024, 2048, 1024, 4096, 1024, 512
FLOPS = 2 * K * S * S2 + 2 * 2 * S * N * S2

F32 = mybir.dt.float32
BF16 = mybir.dt.bfloat16
I32 = mybir.dt.int32
U32 = mybir.dt.uint32
U16 = mybir.dt.uint16
U8 = mybir.dt.uint8
FP8X4 = mybir.dt.float8_e4m3fn_x4
FP4X4 = mybir.dt.float4_e2m1fn_x4
ALU = mybir.AluOpType
ACT = mybir.ActivationFunctionType

P = 128
PACK = 4
PASSES = 2
PASS = P * PACK
QUADRANTS = 4
BANK = 512
HALVES = S2 // BANK
CHUNKS = (256, 256, 256, 128, 128)
GPSIMD_SLICES = (3, 3, 4, 0)
Y_EARLY = 640
Y_RUNS_ON_SCALAR = ((0, 256), (256, 256), (512, 128), (640, 128), (896, 128))
Y_RUN_ON_VECTOR = (768, 128)
H2_SLOTS = 4
W1_PART = 256
CODE_STORES = (((0, 256),), ((256, 256),), ((512, 128), (640, 256)), ((896, 128),))
KIB = 1024
ROW_ALIGN = 256
LEAD = T // 4
SCALAR_WALK = 2
VECTOR_WALK = 4


def tile_list_satellite_radiance_calibration_kernel(
    tc, tab_words, tab_scales, tab2_words, tab2_scales, offs, offs2, lo, hi, gain, w1, w4_words, w4_scales,
    out_0, out_1, out_2,
):
    nc = tc.nc
    with ExitStack() as ctx:
        lists = ctx.enter_context(tc.tile_pool(name="lists", bufs=1))
        held = ctx.enter_context(tc.tile_pool(name="held", bufs=1))
        work = ctx.enter_context(tc.tile_pool(name="work", bufs=4))
        page = ctx.enter_context(tc.tile_pool(name="page", bufs=1))
        psum = ctx.enter_context(tc.psum_pool(name="psum", bufs=8))

        def kept(shape, dtype, name):
            return held.tile(shape, dtype, name=name, align_bytes=ROW_ALIGN)

        def placed(shape, dtype, name, kib):
            return page.tile(shape, dtype, name=name, align_bytes=ROW_ALIGN, offset=int(kib * KIB))

        fields = [(half, g) for half in range(HALVES) for g in range(PASSES)]
        w1_parts = [(g, n0) for g in range(PASSES) for n0 in range(0, N, W1_PART)]

        list1 = lists.tile([P, S // 16], U16, name="list1")
        list2 = lists.tile([P, S2 // 16], U16, name="list2")
        tab_w = [placed([P, T], U32, f"tab_w{a}", (0, 8)[a]) for a in range(PASSES)]
        tab2_w = [placed([P, T2], U32, f"tab2_w{a}", (16, 32)[a]) for a in range(PASSES)]
        tab_s = kept([P, T], U8, "tab_s")
        tab2_s = placed([P, T2], U8, "tab2_s", 46)
        v_w = [placed([P, S], U32, f"v_w{a}", (49, 53)[a]) for a in range(PASSES)]
        v2_w = [kept([P, S2], U32, f"v2_w{a}") for a in range(PASSES)]
        picked = kept([P, S + S2], U8, "picked")
        rows = placed([P, PASSES * (S + S2)], U8, "rows", 57)
        rows_of_pass = [rows[:, a * (S + S2) : (a + 1) * (S + S2)] for a in range(PASSES)]
        w4_w = [placed([P, 2 * N], U8, "w4_w0", 48), placed([P, 2 * N], U8, "w4_w1", 32)]
        w4_s = kept([P, PASSES, N], U8, "w4_s")
        w4_wd = [kept([P, 2 * N], U8, f"w4_wd{g}") for g in range(PASSES)]
        w4_sd = placed([P, PASSES * N], U8, "w4_sd", 12)
        lo_t = placed([P, PASSES, PACK], F32, "lo_t", 25)
        hi_t = placed([P, PASSES, PACK], F32, "hi_t", 25.25)
        gain_t = placed([P, PASSES, PACK], F32, "gain_t", 25.5)
        w1_raw = [
            placed([P, PACK, W1_PART], F32, f"w1_raw{part}", (17, 21, 8, 13)[part]) for part in range(len(w1_parts))
        ]
        c32 = {field: placed([P, PACK, BANK], F32, f"c32_{f}", 61 + 8 * f) for f, field in enumerate(fields)}
        h32 = {field: placed([P, PACK, BANK], F32, f"h32_{f}", 93 + 8 * f) for f, field in enumerate(fields)}

        nc.vector.memset(tab_s[:].bitcast(I32), 0)
        nc.vector.memset(tab2_s[:].bitcast(I32), 0)
        nc.vector.memset(w4_s[:].rearrange("p a n -> p (a n)").bitcast(I32), 0)
        nc.vector.memset(rows[:].bitcast(I32), 0)

        def load_words(dst, words, a, cols=slice(None)):
            nc.sync.dma_start(dst[:, cols].bitcast(I32), words[a].rearrange("p t i -> p (t i)").bitcast(I32)[:, cols])

        def load_w4_words(g):
            nc.sync.dma_start(w4_w[g][:].bitcast(I32), w4_words[g].bitcast(I32))

        def load_scale_rows(dst, scales):
            nc.sync.dma_start(dst[0:P:4, :].bitcast(I32), scales.rearrange("a r t -> (a r) t").bitcast(I32))

        def load_by_mode(dst, src):
            nc.sync.dma_start(dst[:], src.rearrange("(g p t) -> p g t", g=PASSES, t=PACK))

        def carry_scale_rows(a):
            for q in range(QUADRANTS):
                row = 4 * (16 * a + 4 * q)
                dst = rows_of_pass[a][32 * q : 32 * q + 4, :]
                nc.sync.dma_start(dst.bitcast(I32), picked[row : row + 16 : 4, :].bitcast(I32))

        def dealt(ap):
            return ap.rearrange("p (g t m) -> p g m t", g=PASSES, t=PACK)

        def gather_v2_words(a, half):
            nc.vector.tensor_copy(
                v2_w[a][:, half * BANK : (half + 1) * BANK],
                tab2_w[a][:].indirect(list2[:, half * BANK // 16 : (half + 1) * BANK // 16]),
            )

        load_words(tab_w[0], tab_words, 0, slice(0, LEAD))
        nc.sync.dma_start(list1[:], offs)
        nc.sync.dma_start(list2[:], offs2)
        load_scale_rows(tab_s, tab_scales)
        load_words(tab_w[0], tab_words, 0, slice(LEAD, T))
        load_scale_rows(tab2_s, tab2_scales)
        nc.sync.dma_start(w4_s[4:P:8, :, :].bitcast(I32), w4_scales.rearrange("a r n -> r a n").bitcast(I32))
        load_words(tab2_w[0], tab2_words, 0)
        load_words(tab_w[1], tab_words, 1)

        nc.vector.tensor_copy(dealt(picked[:, :S]), tab_s[:].indirect(list1[:]))
        nc.vector.tensor_copy(picked[:, S:], tab2_s[:].indirect(list2[:]))
        carry_scale_rows(0)
        load_words(tab2_w[1], tab2_words, 1)
        load_w4_words(0)
        carry_scale_rows(1)
        nc.vector.tensor_copy(dealt(v_w[0][:]), tab_w[0][:].indirect(list1[:]))
        for half in range(HALVES):
            gather_v2_words(0, half)
        nc.vector.tensor_copy(dealt(v_w[1][:]), tab_w[1][:].indirect(list1[:]))
        for part, (g, n0) in enumerate(w1_parts):
            part_rows = w1[g * PASS : (g + 1) * PASS, n0 : n0 + W1_PART]
            nc.sync.dma_start(w1_raw[part][:], part_rows.rearrange("(p j) n -> p j n", j=PACK))
            if part == 0:
                load_by_mode(lo_t, lo)
                load_by_mode(hi_t, hi)
                load_by_mode(gain_t, gain)
        for half in range(HALVES):
            gather_v2_words(1, half)
        load_w4_words(1)

        def deal_w4_words(g):
            nc.scalar.copy(
                w4_wd[g][:].bitcast(U16).rearrange("p (t b i) -> p b t i", t=PACK, i=8),
                w4_w[g][:].bitcast(U16).rearrange("p (b i t) -> p b t i", t=PACK, i=8),
            )

        deal_w4_words(0)
        nc.gpsimd.tensor_copy(
            w4_sd[:].rearrange("p (g t m) -> p g t m", g=PASSES, t=PACK),
            w4_s[:].rearrange("p g (m t) -> p g t m", t=PACK),
        )
        for q in range(QUADRANTS):
            nc.sync.dma_start(
                w4_sd[32 * q : 32 * q + 4, :].bitcast(I32), w4_sd[32 * q + 4 : 32 * q + 32 : 8, :].bitcast(I32)
            )

        w1_b = kept([P, PASSES, N * PACK], BF16, "w1_b")

        def round_w1(part):
            g, n0 = w1_parts[part]
            dst = w1_b[:, g, :].rearrange("p (u e m j) -> p u m j e", u=2, e=2, j=PACK)
            src = w1_raw[part][:].rearrange("p j (m u e) -> p u m j e", u=2, e=2)
            nc.scalar.copy(dst[:, :, n0 // PACK : (n0 + W1_PART) // PACK], src)

        for part in range(len(w1_parts) - 1):
            round_w1(part)

        def woven(ap, walk):
            return ap.rearrange("p (b i t) -> p b t i", i=walk, t=PACK)

        def by_rows(ap, walk):
            return ap.rearrange("p t (b i) -> p b t i", i=walk)

        sums = {}

        def first_pass(g, t, half, a):
            if a == 0:
                sums[g, t, half] = psum.tile([P, BANK], F32, name="acc")
            cols = slice(g * PASS + t * P, g * PASS + (t + 1) * P)
            js = slice(half * BANK, (half + 1) * BANK)
            nc.tensor.matmul_mx(
                sums[g, t, half][:],
                lhsT=v_w[a][:, cols].bitcast(FP8X4),
                lhsT_scale=rows_of_pass[a][:, cols],
                rhs=v2_w[a][:, js].bitcast(FP8X4),
                rhs_scale=rows_of_pass[a][:, S + js.start : S + js.stop],
                start=(a == 0),
                stop=(a == PASSES - 1),
            )

        h_b = {field: kept([P, BANK * PACK], BF16, f"h_b{f}") for f, field in enumerate(fields)}

        for a in range(PASSES):
            for g in range(PASSES):
                for t in range(PACK):
                    first_pass(g, t, 0, a)
        for f, (half, g) in enumerate(fields):
            for t in range(PACK):
                if half > 0:
                    for a in range(PASSES):
                        first_pass(g, t, half, a)
                c_row = c32[half, g][:, t, :]
                h_row = h32[half, g][:, t, :]
                nc.vector.tensor_scalar(
                    c_row, sums[g, t, half][:], lo_t[:, g, t : t + 1], hi_t[:, g, t : t + 1], ALU.max, ALU.min
                )
                if t < GPSIMD_SLICES[f]:
                    nc.gpsimd.tensor_scalar(h_row, c_row, gain_t[:, g, t : t + 1], 0.0, ALU.mult, ALU.add)
                else:
                    nc.scalar.activation(h_row, c_row, ACT.Copy, scale=gain_t[:, g, t : t + 1])
            if f == 0:
                round_w1(len(w1_parts) - 1)
            if g == PASSES - 1:
                for field in fields[f - 1 : f + 1]:
                    nc.scalar.copy(woven(h_b[field][:], SCALAR_WALK), by_rows(h32[field][:], SCALAR_WALK))
                if half == 0:
                    deal_w4_words(1)

        h_q = {field: kept([P, BANK], U32, f"h_q{f}") for f, field in enumerate(fields)}
        h_s = {field: placed([P, BANK], U8, f"h_s{f}", 57 + 0.5 * f) for f, field in enumerate(fields)}
        w1_q = kept([P, PASSES * N], U32, "w1_q")
        w1_s = placed([P, PASSES * N], U8, "w1_s", 59)
        y_early = kept([P, Y_EARLY * PACK], BF16, "y_early")
        y_late = placed([P, (S2 - Y_EARLY) * PACK], BF16, "y_late", 128)
        y_q = [placed([P, BANK], U32, f"y_q{half}", (85, 117)[half]) for half in range(HALVES)]
        y_s = kept([P, S2], U8, "y_s")

        starts = [sum(CHUNKS[:c]) for c in range(len(CHUNKS))]
        rounded = {}
        banks = {}
        results = {}

        def quantise_h(field):
            nc.vector.quantize_mx(h_q[field][:].bitcast(FP8X4), h_s[field][:], h_b[field][:])

        def make_h2(c, g):
            half, j0 = divmod(starts[c], BANK)
            slot = (PASSES * c + g) % H2_SLOTS
            rounded[c, g] = placed([P, CHUNKS[c] * PACK], BF16, f"h2_b{c}_{g}", 49 + 2 * slot)
            nc.vector.tensor_tensor(
                woven(rounded[c, g][:], VECTOR_WALK),
                by_rows(h32[half, g][:, :, j0 : j0 + CHUNKS[c]], VECTOR_WALK),
                by_rows(c32[half, g][:, :, j0 : j0 + CHUNKS[c]], VECTOR_WALK),
                ALU.mult,
            )

        def bank_slices(c):
            if CHUNKS[c] * PACK > BANK:
                return [(0, 1), (2, 3)]
            return [(0, 1, 2, 3)]

        def linear_passes(c, g):
            half, j0 = divmod(starts[c], BANK)
            js = slice(j0, j0 + CHUNKS[c])
            for bank, slices in enumerate(bank_slices(c)):
                if g == 0:
                    banks[c, bank] = psum.tile([P, len(slices), CHUNKS[c]], F32, name="acc")
                for s, t in enumerate(slices):
                    n0 = g * N + t * P
                    nc.tensor.matmul_mx(
                        banks[c, bank][:, s, :],
                        lhsT=w1_q[:, n0 : n0 + P].bitcast(FP8X4),
                        lhsT_scale=w1_s[:, n0 : n0 + P],
                        rhs=h_q[half, g][:, js].bitcast(FP8X4),
                        rhs_scale=h_s[half, g][:, js],
                        start=(g == 0 and s == 0),
                        stop=False,
                    )

        def quadratic_passes(c, g):
            slot = (PASSES * c + g) % H2_SLOTS
            codes = placed([P, CHUNKS[c]], U32, f"h2_q{c}_{g}", 125 + slot)
            scales = work.tile([P, CHUNKS[c]], U8, name="h2_s", align_bytes=ROW_ALIGN)
            nc.vector.quantize_mx(codes[:].bitcast(FP8X4), scales[:], rounded[c, g][:])
            for bank, slices in enumerate(bank_slices(c)):
                for s, t in enumerate(slices):
                    n0 = g * N + t * P
                    nc.tensor.matmul_mx(
                        banks[c, bank][:, s, :],
                        lhsT=w4_wd[g][:, 2 * t * P : 2 * (t + 1) * P].bitcast(FP4X4),
                        lhsT_scale=w4_sd[:, n0 : n0 + P],
                        rhs=codes[:].bitcast(FP8X4),
                        rhs_scale=scales[:],
                        start=False,
                        stop=(g == PASSES - 1 and s == len(slices) - 1),
                    )

        out_rows = out_0.rearrange("(p t) j -> p t j", t=PACK)

        def hand_out(c):
            results[c] = kept([P, PACK, CHUNKS[c]], F32, f"y32_{c}")
            js = slice(starts[c], starts[c] + CHUNKS[c])
            for bank, slices in enumerate(bank_slices(c)):
                ts = slice(slices[0], slices[-1] + 1)
                nc.scalar.copy(results[c][:, ts, :], banks[c, bank][:])
                nc.sync.dma_start(out_rows[:, ts, js], results[c][:, ts, :])

        def rounded_y(first, width):
            if first < Y_EARLY:
                return y_early[:, first * PACK : (first + width) * PACK]
            return y_late[:, (first - Y_EARLY) * PACK : (first - Y_EARLY + width) * PACK]

        def weave_y(copy, walk, first, width):
            c = max(k for k in range(len(CHUNKS)) if starts[k] <= first)
            src = banks[c, 0] if c == len(CHUNKS) - 1 else results[c]
            j0 = first - starts[c]
            copy(woven(rounded_y(first, width), walk), by_rows(src[:, :, j0 : j0 + width], walk))

        quantise_h((0, 0))
        nc.vector.quantize_mx(w1_q[:].bitcast(FP8X4), w1_s[:], w1_b[:].rearrange("p g n -> p (g n)"))
        for c in range(len(CHUNKS)):
            half, j0 = divmod(starts[c], BANK)
            if j0 == 0 and half > 0:
                quantise_h((half, 0))
            for g in range(PASSES):
                make_h2(c, g)
            linear_passes(c, 0)
            quadratic_passes(c, 0)
            if j0 == 0:
                quantise_h((half, 1))
            linear_passes(c, 1)
            quadratic_passes(c, 1)
            hand_out(c)
        for run in Y_RUNS_ON_SCALAR:
            weave_y(nc.scalar.copy, SCALAR_WALK, *run)

        out_words = out_1[0].rearrange("p m t -> p (m t)").bitcast(I32)

        def codes_of(first, width):
            half, j0 = divmod(first, BANK)
            return y_q[half][:, j0 : j0 + width]

        for store in CODE_STORES:
            for first, width in store:
                nc.vector.quantize_mx(
                    codes_of(first, width).bitcast(FP8X4), y_s[:, first : first + width], rounded_y(first, width)
                )
            first, width = store[0][0], sum(run[1] for run in store)
            queue = nc.scalar if store == CODE_STORES[-1] else nc.sync
            queue.dma_start(out_words[:, first : first + width], codes_of(first, width).bitcast(I32))
            if store == CODE_STORES[1]:
                weave_y(nc.vector.tensor_copy, VECTOR_WALK, *Y_RUN_ON_VECTOR)

        for q in range(QUADRANTS):
            queue = nc.sync if q % 2 == 0 else nc.scalar
            queue.dma_start(out_2[0, 4 * q : 4 * q + 4, :].bitcast(I32), y_s[32 * q : 32 * q + 4, :].bitcast(I32))
